import numpy as np, ml_dtypes
CORES = [51,54,179,182]
N = 4
BF = ml_dtypes.bfloat16
def gentries(a):
    return np.ascontiguousarray(a.reshape(8, 16, -1).transpose(0, 2, 1)).reshape(8, -1)
def gtable(e):
    e = np.asarray(e); return np.ascontiguousarray(e.reshape(8, -1, 16).transpose(0, 2, 1)).reshape(128, -1).astype(np.int32)
V, B, P, T, RO = 384, 1360, 192, 64, 3
C, M, GH = V + P * RO, B + P * RO, (N - 1) * T
I, SEV = B - GH, 176
THETA, DELTA = (460, 560, 520), (9, 7, 10)
def wire(rng, bias, edge=False, crowd=None, hole=None, full=()):
    en = np.zeros((N, 8, 2, B), np.int64); bl = np.full((N, 8, 16, V), -1, np.int64); snd = np.zeros((N, 8, N - 1, T), np.int64)
    for q in range(N):
        for g in range(8):
            if crowd is not None and crowd[g] >= 0:
                s = (rng.permutation(V)[:, None] * 16 + np.arange(16)).reshape(-1)
                a, z, w = s[:I].copy(), np.roll(s[I:2 * I], crowd[g]), s[2 * I:2 * I + GH].copy()
            else:
                key = rng.random((V, 16)) + bias[q, g][:, None]
                if hole is not None: key = key + 99.0 * (np.arange(16)[None, :] == hole[q, g][:, None])
                s = np.argsort(key.reshape(-1))[:2 * I + GH]; s = s[rng.permutation(2 * I + GH)]
                a, z, w = s[:I].copy(), s[I:2 * I].copy(), s[2 * I:].copy()
                if g in full:
                    s = s[np.argsort(bias[q, g][s // 16] >= 0, kind="stable")]; w, a, z = s[:GH].copy(), s[GH:GH + I].copy(), s[GH + I:].copy()
                    m = rng.random(I) < 0.5; a, z = np.where(m, z, a), np.where(m, a, z)
                for i in np.flatnonzero(a // 16 == z // 16):
                    if a[i] // 16 == z[i] // 16:
                        j = np.flatnonzero((z // 16 != a[i] // 16) & (a // 16 != z[i] // 16)); j = int(j[rng.integers(0, len(j))])
                        zi, zj = int(z[i]), int(z[j]); z[i] = zj; z[j] = zi
            if edge: o = np.concatenate([GH // 2 + rng.permutation(I), rng.permutation(np.concatenate([np.arange(GH // 2), np.arange(GH // 2 + I, B)]))])
            else: o = rng.permutation(B)
            k, tw = o[:I], o[I:]
            en[q, g, 0, k] = a // 16; en[q, g, 1, k] = z // 16
            bl[q, g, a % 16, a // 16] = k; bl[q, g, z % 16, z // 16] = k; bl[q, g, w % 16, w // 16] = tw
            snd[q, g] = tw.reshape(N - 1, T); far = C + np.arange(GH); first = (q + 1 + np.arange(GH) // T) % N > q
            en[q, g, 0, tw] = np.where(first, w // 16, far); en[q, g, 1, tw] = np.where(first, far, w // 16)
    return en, bl, snd
def cells(rng, s, swing):
    lead, n = s.shape[:-1], s.shape[-1]; base = (s >> 4)[..., None, :]
    x = base + (np.argsort(rng.random(lead + (16, n)), axis=-2) < (s & 15)[..., None, :])
    room = np.clip(np.minimum(base, 62 - base), 0, swing)
    z = (rng.random(lead + (8, n)) * (room + 1)).astype(np.int64) * (1 - 2 * rng.integers(0, 2, lead + (8, n)))
    x[..., 0::2, :] += z; x[..., 1::2, :] -= z
    return x
def twin(y, snd):
    for q in range(N):
        for d in range(1, N):
            r = (q + d) % N
            if q < r:
                for g in range(8): y[r, g][:, snd[r, g, N - 1 - d]] = y[q, g][:, snd[q, g, d - 1]]
    return y
def xsums(rng): return np.clip(rng.integers(100, 901, (N, 8, V)) + rng.integers(-260, 65, (N, 8, 1)), 0, 1008)
def ysums(rng, share): return np.where(rng.random((N, 8, B)) < share, SEV + (rng.integers(0, 640, (N, 8, B)) * rng.random((N, 8, B))).astype(np.int64), rng.integers(0, SEV, (N, 8, B)))
def pack(x, y, en, bl, snd):
    return {"x0": np.ascontiguousarray(x.reshape(N, 128, V)).astype(np.float32).astype(BF), "y0": np.ascontiguousarray(y.reshape(N, 128, B)).astype(np.float32).astype(BF),
            "bl0": np.ascontiguousarray(bl.reshape(N, 128, V)).astype(np.int32), "en0": np.ascontiguousarray(en.reshape(N, 16, B)).astype(np.int32), "snd": np.stack([gtable(a.reshape(8, -1)) for a in snd])}
def setup_inputs(rng):
    en, bl, snd = wire(rng, 0.6 * rng.random((N, 8, V)))
    return pack(cells(rng, xsums(rng), 12), twin(cells(rng, ysums(rng, 0.92), 12), snd), en, bl, snd)
def setup_inputs_spread(rng):
    en, bl, snd = wire(rng, 2.0 * rng.random((N, 8, V)))
    ex = rng.choice(np.array([0.3, 0.7, 1.0, 2.0, 4.0]), (N, 8, 1, V)); ey = rng.choice(np.array([0.2, 1.0, 3.0, 6.0]), (N, 8, 1, B))
    x = np.minimum((64 * rng.random((N, 8, 16, V)) ** ex).astype(np.int64), 63); y = np.minimum((64 * rng.random((N, 8, 16, B)) ** ey).astype(np.int64), 63)
    return pack(x, twin(y, snd), en, bl, snd)
def setup_inputs_ends(rng):
    en, bl, snd = wire(rng, np.zeros((N, 8, 1)) - np.abs(2 * np.arange(V) - (V - 1)) * 9.0 / V, edge=True)
    pat = np.argsort(rng.random((8, 16)), axis=1) < 8; gi = np.arange(8)[None, :, None]
    kinds = np.stack([np.ones((8, 16), bool), pat, ~pat, np.zeros((8, 16), bool)]).astype(np.int64) * 63
    key = rng.random((N, 8, V)); key[..., 0] = -1.0; key[..., V - 1] = -2.0
    go = np.where(gi % 2 == 0, key < 0.75, np.argsort(np.argsort(key, axis=2), axis=2) < P)
    kx = rng.integers(0, 3, (N, 8, V)); kx[..., 0] = 0; kx[..., V - 1] = 0
    x = kinds[np.where(go, kx, 3), gi].transpose(0, 1, 3, 2)
    ky = rng.choice(5, (N, 8, B), p=[0.2, 0.35, 0.2, 0.1, 0.15]); ky[:, 7] = np.where(ky[:, 7] >= 3, 1, ky[:, 7])
    y = np.ascontiguousarray(kinds[np.minimum(ky, 3), gi].transpose(0, 1, 3, 2))
    y = np.where((ky == 4)[:, :, None, :], 63 * rng.integers(0, 2, y.shape), y)
    return pack(x, twin(y, snd), en, bl, snd)
def setup_inputs_corners(rng):
    bias = rng.choice(np.array([-9.0, 0.0, 9.0]), (N, 8, V), p=[0.25, 0.55, 0.2]); bias[..., 0] = -9.0; bias[..., V - 1] = -9.0
    hole = np.where(rng.random((N, 8, V)) < 0.6, 15, rng.integers(0, 16, (N, 8, V))); hole = np.where((bias < 0) & (rng.random((N, 8, V)) < 0.6), hole, -1); hole[..., 0] = -1; hole[..., V - 1] = -1
    en, bl, snd = wire(rng, bias, hole=hole)
    s = rng.choice(np.array([SEV, SEV - 1, SEV + 1, 1008, 0]), (N, 8, B), p=[0.3, 0.2, 0.2, 0.15, 0.15]); s = np.where(rng.random((N, 8, B)) < 0.5, s, ysums(rng, 0.9))
    y = cells(rng, s, 12); y[:, 3] = 22; y[:, 5] = 52; y = twin(y, snd)
    thr = THETA[0] + (np.add.reduce((np.add.reduce(y, axis=2) >= SEV).astype(np.int64), axis=2) & 31)[:, :, None]
    n = rng.choice(np.array([0, 1, P - 1, P, P + 1, V]), (N, 8)); n[:, 3] = P; n[:, 5] = P + 1; n[0] = (0, 1, P - 1, P, P + 1, P + 1, V, P)
    hot = np.argsort(rng.random((N, 8, V)), axis=2) < n[:, :, None]
    up = np.where(rng.random((N, 8, V)) < 0.5, thr, thr + (rng.random((N, 8, V)) * (1009 - thr)).astype(np.int64))
    down = np.where(rng.random((N, 8, V)) < 0.5, thr - 1, (rng.random((N, 8, V)) * thr).astype(np.int64))
    x = cells(rng, np.where(hot, up, down), 12); x[:, 3] = np.where(hot[:, 3], 63, 0)[:, None, :]; x[:, 5] = np.where(hot[:, 5], 32, 0)[:, None, :]
    return pack(x, y, en, bl, snd)
def setup_inputs_crowd(rng):
    go = np.argsort(rng.random((N, 8, V)), axis=2) < P; two = [2, 7]
    bias = np.zeros((N, 8, V)); bias[:, two] = np.where(go[:, two], -9.0, 0.0)
    en, bl, snd = wire(rng, bias, crowd=(0, 1, -1, 0, 1, 0, 1, -1), full=(2, 7))
    s = xsums(rng); s[:, :2] = rng.integers(510, 1009, (N, 2, V)); s[:, 3] = rng.integers(510, 1009, (N, V)); s[np.arange(N), 3, rng.integers(0, V, N)] = rng.integers(0, 400, N)
    s[:, 5:7] = THETA[0] + np.array([B & 31, (B - 1) & 31])[None, :, None] + rng.choice(np.array([-40, -1, 0, 1, 40]), (N, 2, V), p=[0.1, 0.4, 0.3, 0.1, 0.1])
    t = ysums(rng, 0.9); live = ysums(rng, 2.0)
    for g in (0, 1, 3, 4, 5, 6): t[:, g] = live[:, g]
    y = cells(rng, t, 12); y[:, two] = rng.integers(52, 64, (N, 2, 16, B)); y = twin(y, snd)
    for q in range(N):
        for g in (1, 4, 6): y[q, g][:, int(rng.choice(np.setdiff1d(np.arange(B), snd[q, g].reshape(-1))))] = 10
        go[q, 2, int(rng.choice(np.flatnonzero(go[q, 2])))] = False
    x = cells(rng, s, 12); x[:, two] = np.where(go[:, two][:, :, None, :], rng.integers(32, 41, (N, 2, 16, V)), rng.integers(0, 8, (N, 2, 16, V)))
    return pack(x, y, en, bl, snd)
def check_inputs(d):
    bad = []
    for k, lo, hi in (("x0", 0, 63), ("y0", 0, 63), ("bl0", -1, B - 1), ("en0", 0, C + GH - 1), ("snd", 0, B - 1)):
        a = np.asarray(d[k]).astype(np.float64)
        if not (np.min(a) >= lo and np.max(a) <= hi and np.all(a == np.floor(a))): bad.append("range of " + k)
    if bad: return bad
    en = d["en0"].astype(np.int64).reshape(N, 8, 2, B); bl = d["bl0"].astype(np.int64).reshape(N, 8, 16, V)
    sl = np.stack([gentries(a) for a in d["snd"]]).astype(np.int64); y = d["y0"].astype(np.float32).reshape(N, 8, 16, B)
    for q in range(N):
        for g in range(8):
            s, e = sl[q, g], en[q, g]; tw = np.zeros(B, bool); tw[s] = True
            if len(np.unique(s)) < GH: bad.append("twins of snd differ")
            if np.any(e[:, ~tw] >= V) or np.any(e[0, ~tw] == e[1, ~tw]): bad.append("ends of en0 on one rank")
            first = (q + 1 + np.arange(GH) // T) % N > q; own = np.where(first, e[0, s], e[1, s]); far = np.where(first, e[1, s], e[0, s])
            if np.any(own >= V) or np.any(far != C + np.arange(GH)): bad.append("ends of en0 of twins")
            r, c = np.nonzero(bl[q, g] >= 0); have = np.sort(bl[q, g][r, c] * V + c)
            want = np.sort((np.arange(B)[None, :] * V + e)[e < V])
            if len(have) != len(want) or np.any(have != want): bad.append("slots of bl0")
        for k in range(1, N):
            r = (q + k) % N
            for g in range(8):
                if np.any(y[q, g][:, sl[q, g].reshape(N - 1, T)[k - 1]] != y[r, g][:, sl[r, g].reshape(N - 1, T)[N - 1 - k]]): bad.append("y0 of twins alike")
    return sorted(set(bad))
def reference(x0, y0, bl0, en0, snd):
    x = np.zeros((N, 8, 16, C), np.int32); x[..., :V] = x0.astype(np.float32).astype(np.int32).reshape(N, 8, 16, V)
    y = np.zeros((N, 8, 16, M), np.int32); y[..., :B] = y0.astype(np.float32).astype(np.int32).reshape(N, 8, 16, B)
    bits = y[..., :1024] & 7
    exists = np.zeros((N, 8, C), bool); exists[..., :V] = True
    bl = np.full((N, 8, 16, C), -1, np.int64); bl[..., :V] = bl0.reshape(N, 8, 16, V)
    en = np.zeros((N, 8, 2, M), np.int64); en[..., :B] = en0.reshape(N, 8, 2, B)
    sl = np.stack([gentries(a) for a in snd]).astype(np.int64).reshape(N, 8, N - 1, T)
    take = np.take_along_axis
    for t in range(RO):
        live = np.add.reduce(y, axis=2) >= SEV
        count = np.add.reduce(live.astype(np.int64), axis=2)
        cand = np.add.reduce(x, axis=2) >= THETA[t] + (count & 31)[:, :, None]
        place = np.add.accumulate(cand.astype(np.int64), axis=2) - cand
        div = cand & (place < P)
        low = np.where(div[:, :, None], np.maximum(x - DELTA[t], 0), x); high = np.where(div[:, :, None], np.minimum(x + DELTA[t], 63), x)
        own = [[take(en[q, :, 0 if q < (q + d) % N else 1], sl[q, :, d - 1], 1) for d in range(1, N)] for q in range(N)]
        for q in range(N):
            wl, wh, wd = [low[q]], [high[q]], [div[q]]
            for d in range(1, N):
                r = (q + d) % N; c = own[r][N - 1 - d]
                wl.append(take(low[r], c[:, None, :], 2)); wh.append(take(high[r], c[:, None, :], 2)); wd.append(take(div[r], c, 1))
            wl, wh, wd = np.concatenate(wl, axis=2), np.concatenate(wh, axis=2), np.concatenate(wd, axis=1)
            e = en[q].copy(); a = [take(w, e[:, 0][:, None, :], 2) for w in (wl, wh)]; z = [take(w, e[:, 1][:, None, :], 2) for w in (wl, wh)]
            score = np.stack([np.add.reduce(np.abs(2 * y[q] - a[i] - z[j]), axis=1) for i in (0, 1) for j in (0, 1)])
            best = np.argmin(score, axis=0); pole = np.stack([best >> 1, best & 1], axis=1)
            touched = live[q] & (take(wd, e[:, 0], 1) | take(wd, e[:, 1], 1))
            gap = np.abs(np.where((pole[:, 0] == 1)[:, None], a[1], a[0]) - np.where((pole[:, 1] == 1)[:, None], z[1], z[0]))
            yn = np.where(touched[:, None], (y[q] + gap) >> 1, y[q]); stays_live = np.add.reduce(yn, axis=1) >= SEV
            move = touched[:, None] & (e < C) & (pole == 1); ne = np.where(move, V + P * t + take(place[q][:, None, :], np.minimum(e, C - 1), 2), e)
            for g in range(8):
                v = np.flatnonzero(div[q, g]); n = V + P * t + np.arange(len(v)); old = bl[q, g][:, v]; b = np.maximum(old, 0)
                keep = (old >= 0) & stays_live[g][b]; side = np.where(e[g, 0][b] == v[None, :], pole[g, 0][b], pole[g, 1][b])
                tv = np.where(keep & (side == 0), old, -1); tn = np.where(keep & (side == 1), old, -1)
                k = np.flatnonzero(np.any(tv < 0, axis=0) & np.any(tn < 0, axis=0)); nb = B + P * t + k
                rv, rn = np.argmax(tv < 0, axis=0)[k], np.argmax(tn < 0, axis=0)[k]
                tv[rv, k] = nb; tn[rn, k] = nb
                bl[q, g][:, v] = tv; bl[q, g][:, n] = tn
                yn[g][:, nb] = high[q, g][:, v[k]] - low[q, g][:, v[k]]; ne[g, 0, nb] = v[k]; ne[g, 1, nb] = n[k]
                x[q, g][:, v] = low[q, g][:, v]; x[q, g][:, n] = high[q, g][:, v]; exists[q, g, n] = True
            y[q] = yn; en[q] = ne
        if t + 1 < RO:
            x = np.where(exists[:, :, None], np.minimum(np.maximum(x + np.take(bits, (np.arange(C) + 331 * t) & 1023, axis=3) - 3, 0), 63), x)
    return {"yx": x.reshape(N, 128, C).astype(np.float32).astype(BF), "yy": y.reshape(N, 128, M).astype(np.float32).astype(BF),
            "yl": bl.reshape(N, 128, C).astype(np.float32), "ye": en.reshape(N, 16, M).astype(np.float32)}

@@ -1,0 +1,719 @@
+import numpy as np
+from concourse.bass import DstId, RemoteDMATransfer
+from concourse.mybir import AluOpType as OP, ActivationFunctionType as AF
+
+V0, B0, P, RO = 384, 1360, 192, 3
+THETA, DELTA = (460, 560, 520), (9, 7, 10)
+FAR, DUM, KON = 960, 1344, 1536
+YA, LOW, HIGH, YB = 112, 2048, 4096, 5632
+BF, F32, I32, U16 = "bfloat16", "float32", "int32", "uint16"
+
+
+def _scratch():
+    s = {}
+    for names, cols, d in (
+        ("tb", 7568, BF), ("y0r", 1360, BF), ("xx", 960, BF), ("rr", 1744, BF), ("ww", 1536, BF),
+        ("nc rem dd zero exm", 768, BF), ("fl t8", 1024, BF), ("iov dlb", 960, BF), ("iof", 960, F32),
+        ("nl nh zh dll dhl all ahl alh ahh i0 i1 m128", 1744, BF), ("m256", 1552, BF),
+        ("st", 1760, BF), ("sg", 3456, BF), ("bm one2", 2048, BF),
+        ("sb0 sb1 sb2 ld0 ld1 ld2 xo eo nm ff jk my", 384, BF), ("wf", 320, BF),
+        ("blk nblk idn nidn ihf i63 i32 i4k n4k tri ntri ms dead unt kc", 128, BF), ("idf sf", 128, F32),
+        ("z1 z16 z8k z512 z01", 144, BF), ("gm", 8, BF), ("k1 k2 code sgl", 112, BF),
+        ("bl", 1536, F32), ("bli", 384, I32), ("enb", 1360, I32), ("ent", 256, I32), ("entf et sm", 256, F32),
+        ("sndi", 12, I32), ("col", 32, F32), ("coli", 8, I32),
+        ("e0 e1 ow0 ow1 adj0 adj1 jw jw4 jwm cp wi1 b0 b1 t0 t1 t2 t4 t5", 128, F32),
+        ("c1 mm", 224, F32), ("best ab", 224, I32), ("gu ix", 256, U16),
+        ("old", 216, F32), ("hib", 216, BF), ("ox", 216, U16), ("tg", 48, U16), ("dlu", 12, U16), ("ou su", 24, U16),
+        ("hg nyc lc ex ri e1b e2b kb nba nbb", 192, BF), ("ncst vn tn", 192, F32), ("r1 tv", 384, F32),
+    ):
+        for n in names.split():
+            s[n] = ("sbuf", [128, cols], d)
+    s["ps"] = ("psum", [128, 4096], F32)
+    return s
+
+
+SHAPES = _scratch()
+PART = {n: 128 * i for i, n in enumerate(n for n, s in SHAPES.items() if s[1][1] == 128 and s[2] == F32)}
+SCRATCH = {n: s for n, s in SHAPES.items() if n not in PART}
+SCRATCH["fw"] = ("sbuf", [128, 128 * len(PART)], F32)
+SEMAPHORES = ["qv", "qa", "qp", "qg", "sent", "arr0", "arr1", "arr2", "dy", "dx", "denb", "dsnd", "dbl", "dent", "dout", "dz",
+              "dr0", "dr1", "ga0", "ga1", "gb0", "gb1", "dyy", "gyy", "gy0", "dd0", "dd1", "dd2"]
+QSEM = {"V": "qv", "A": "qa", "P": "qp", "G": "qg"}
+CYC, PEC, GAT, SCA = 1.04, 0.52, 1.56, 3.8
+ONV = ()
+
+
+def ap(n, a, b, s=1, p=(0, 128, 1)):
+    if n in PART:
+        n, a, b = "fw", a + PART[n], b + PART[n]
+    return {"n": n, "a": a, "b": b, "s": s, "p": p}
+
+
+def ind(win, off):
+    return {"win": win, "off": off}
+
+
+def ps(bank, a, b, p=(0, 128, 1)):
+    return ap("ps", 512 * bank + a, 512 * bank + b, 1, p)
+
+
+def width(x):
+    if "win" in x:
+        return 16 * (x["off"]["b"] - x["off"]["a"])
+    return (x["b"] - x["a"] + x["s"] - 1) // x["s"]
+
+
+def size(x):
+    x = x.get("win", x)
+    return 2 if SCRATCH[x["n"]][2] in (BF, U16) else 4
+
+
+def build(T, send, q=0):
+    ops = []
+
+    def real(x):
+        if not isinstance(x, dict):
+            return x
+        if "win" in x:
+            return real(x["win"]).indirect(real(x["off"]))
+        p = x["p"]
+        return T[x["n"]][p[0]:p[1]:p[2], x["a"]:x["b"]:x["s"]]
+
+    def add(eng, fn, outs, ins, cost, lat=0.0, sem=None, inc=1):
+        w, r = [], []
+        for x in ins:
+            if isinstance(x, dict):
+                r += [x["win"], x["off"]] if "win" in x else [x]
+        for o in outs:
+            if "win" in o:
+                w.append(o["win"]); r.append(o["off"])
+            else:
+                w.append(o)
+        ops.append({"e": eng, "fn": fn, "w": w, "r": r, "c": cost, "lat": lat, "sem": sem, "inc": inc})
+
+    def vcost(out, ins, two=False):
+        k = 0.5 if all(size(x) == 2 for x in [out] + ins) else 1.0
+        if "win" in out:
+            k = SCA
+        elif "win" in ins[0]:
+            k = GAT
+        elif two and all(x["n"] != "ps" for x in ins):
+            k *= 2
+        return (60 + width(ins[0]) * k) * CYC
+
+    def TS(out, x, s1, o1, s2=None, o2=None):
+        if o2 is None:
+            fn = lambda g: g.vector.tensor_scalar(real(out), real(x), real(s1), None, o1)
+        else:
+            fn = lambda g: g.vector.tensor_scalar(real(out), real(x), real(s1), real(s2), o1, o2)
+        add("V", fn, [out], [x, s1, s2], vcost(out, [x]))
+
+    def TT(out, x, y, o):
+        add("V", lambda g: g.vector.tensor_tensor(real(out), real(x), real(y), o), [out], [x, y], vcost(out, [x, y], True))
+
+    def CP(out, x):
+        add("V", lambda g: g.vector.tensor_copy(real(out), real(x)), [out], [x], vcost(out, [x]))
+
+    def MS(out, c):
+        add("V", lambda g: g.vector.memset(real(out), c), [out], [], vcost(out, [out]))
+
+    def ACT(out, x, f=AF.Identity, scale=1.0, bias=0.0, acc=None):
+        def fn(g):
+            if acc is None:
+                return g.scalar.activation(real(out), real(x), f, bias=real(bias), scale=scale)
+            return g.scalar.activation(real(out), real(x), f, bias=bias, scale=scale, accum_out=real(acc))
+        add("A", fn, [out] + ([acc] if acc else []), [x, bias], (80 + width(x) * (GAT if "win" in x else 1.0)) * CYC + (100 if acc else 0))
+
+    def MMS(groups, fresh=True, done=True):
+        def fn(g):
+            for out, terms in groups:
+                for i, (l, r) in enumerate(terms):
+                    last = g.tensor.matmul(real(out), real(l), real(r), fresh and i == 0, done and i == len(terms) - 1)
+            return last
+        add("P", fn, [o for o, _ in groups], [x for _, ts in groups for t in ts for x in t],
+            60 + sum(max(64, width(r)) * (size(r) - 1 + size(r) // 4) for _, ts in groups for _, r in ts) * PEC)
+
+    def MM(out, terms):
+        MMS([(out, terms)])
+
+    def TR(o, x, i):
+        add("P", lambda g: g.tensor.transpose(real(o), real(x), real(i)), [o], [x, i], 300)
+
+    def full(n):
+        return ap(n, 0, SHAPES[n][1][1])
+
+    def wrap(z, n, a, k):
+        return [(ap(z, 15 - r, 143 - r), ap(n, a + r, a + 16 * k, 16)) for r in range(16)]
+
+    def DMA(eng, sem, pairs, outs, ins, lat=2200.0):
+        def fn(g):
+            for o, i in pairs:
+                if eng == "G":
+                    g.dma_start(o(), i(), accum_op=OP.add).then_inc(T.sem[sem], 16)
+                else:
+                    g.sync.dma_start(o(), i()).then_inc(T.sem[sem], 16)
+            return None
+        add(eng, fn, outs, ins, (1000.0 if eng == "G" else 60.0) * len(pairs), lat, sem, 16 * len(pairs))
+
+    def IOTA(out, pat, base, cm):
+        if SCRATCH[out["n"]][2] != I32:
+            fn = lambda g: g.iota(real(out), pat, base, cm, allow_small_or_imprecise_dtypes=True)
+        else:
+            fn = lambda g: g.iota(real(out), pat, base, cm)
+        add("G", fn, [out], [], 130 + 2 * width(out) * CYC)
+
+    def SEL(out, x, pat, o, base, cm):
+        add("G", lambda g: g.affine_select(real(out), real(x), pat, o, 0.0, base, cm), [out], [x], 170 + 2 * width(out) * CYC)
+
+    col = lambda i: ap("col", i, i + 1)
+    sm = lambda a, n: ap("sm", a, a + n)
+    R16, C256, R2, THR, LB, LP, NB, ACC, SLC = [col(i) for i in range(9)]
+    blk, nblk, idn, nidn, idf, i4k, n4k = [full(n) for n in ("blk", "nblk", "idn", "nidn", "idf", "i4k", "n4k")]
+    Q = ap("coli", 2, 3)
+    ecol = lambda r: 128 * (r % 2) + 16 * (r // 2)
+
+    MS(full("enb"), 0)
+    DMA("S", "dy", [(lambda: T.y0r[:], lambda: T.y0[:])], [full("y0r")], [], 3500.0)
+    DMA("S", "dx", [(lambda: T.xx[:, 0:V0], lambda: T.x0[:])], [ap("xx", 0, V0)], [], 3000.0)
+    DMA("S", "dsnd", [(lambda: T.sndi[:], lambda: T.snd[:])], [full("sndi")], [])
+    DMA("S", "denb", [(lambda h=h: T.enb[h:128:16, :], lambda h=h: T.en0[h:16:2, :]) for h in (0, 1)], [full("enb")], [])
+    DMA("S", "dent", [(lambda r=r: T.ent[0:85, ecol(r):ecol(r) + 16], lambda r=r: T.en0[r, :]) for r in range(16)], [full("ent")], [])
+    DMA("S", "dbl", [(lambda: T.bli[:], lambda: T.bl0[:])], [full("bli")], [])
+
+    MS(ap("one2", 0, 512), 1.0)
+    SEL(full("gm"), ap("one2", 0, 8), [[-16, 8]], OP.is_ge, 0, 1)
+    SEL(full("gm"), full("gm"), [[16, 8]], OP.is_ge, 15, -1)
+    SEL(blk, ap("one2", 0, 128), [[-16, 8], [0, 16]], OP.is_ge, 0, 1)
+    SEL(blk, blk, [[16, 8], [0, 16]], OP.is_ge, 15, -1)
+    IOTA(ap("coli", 0, 1), [[0, 1]], 0, 1)
+    SEL(idn, ap("one2", 0, 128), [[-1, 128]], OP.is_equal, 0, 1)
+    TS(ap("coli", 1, 2), ap("coli", 0, 1), 15, OP.bitwise_and)
+    CP(R16, ap("coli", 1, 2))
+    TS(C256, R16, -256.0, OP.mult)
+    TS(R2, R16, 2.0, OP.is_lt)
+    TS(col(10), R16, 1.0, OP.is_equal)
+    TS(col(14), R16, -1.0, OP.mult, 1.0, OP.add)
+    for z, c in (("z512", 512.0), ("z01", R2), ("z16", 0.0625), ("z1", 1.0), ("z8k", 8192.0)):
+        MS(full(z), 0.0)
+        TS(ap(z, 15, 143, 16), full("gm"), c, OP.mult)
+    for n, c in (("nidn", -1.0), ("ihf", 0.5), ("i63", 63.75), ("i32", 32.0), ("i4k", 4096.0), ("n4k", -4096.0), ("idf", 1.0)):
+        ACT(full(n), idn, scale=c)
+    ACT(nblk, blk, scale=-1.0)
+    SEL(full("tri"), blk, [[1, 128]], OP.is_gt, 0, -1)
+    TT(full("tri"), full("tri"), full("i32"), OP.subtract)
+    ACT(full("ntri"), full("tri"), scale=-1.0)
+    IOTA(ap("iof", 0, 384), [[1, 384]], 0, 0)
+    IOTA(ap("iof", 768, 960), [[1, 192]], DUM, 0)
+    IOTA(ap("iof", 384, 768), [[1, 384]], 384, 0)
+    for a, b in ((0, 384), (768, 960), (384, 768)):
+        ACT(ap("iov", a, b), ap("iof", a, b), AF.Relu, bias=C256)
+        TS(ap("iov", a, b), ap("iov", a, b), 256.0, OP.min)
+    TS(full("jw"), ap("iof", 0, 128), 16.0, OP.mult, R16, OP.add)
+    ACT(full("jw4"), full("jw"), bias=float(YB - LOW))
+    ACT(full("jwm"), full("jw"), bias=-float(LOW - YA))
+    ACT(full("ri"), ap("iof", 0, 192), bias=2.0)
+    MS(full("zero"), 0.0)
+    fills = [(n, a + c, min(a + c + 768, b)) for n, a, b in (("tb", LOW + V0, LOW + KON), ("tb", HIGH + V0, YB), ("ww", V0, 1536), ("dlb", P, 960))
+             for c in range(0, b - a, 768)]
+    DMA("S", "dz", [(lambda n=n, a=a, b=b: T[n][:, a:b], lambda a=a, b=b: T.zero[:, 0:b - a]) for n, a, b in fills],
+        [ap(n, a, b) for n, a, b in fills], [full("zero")])
+    MS(ap("tb", LOW + KON, HIGH), 128.0)
+    MS(ap("exm", 0, V0), -3.0)
+    MS(full("k1"), -71168.0)
+    MS(full("k2"), 24.0)
+    MS(ap("code", 0, 1), -256.0)
+    for h in "01":
+        MS(ap("ow" + h, 85, 128), 4096.0)
+        MS(ap("adj" + h, 85, 128), 0.0)
+
+    def late_constants():
+        for n, a, b, c in (("tb", YA, LOW, 128), ("bl", V0, 1536, -1), ("one2", 512, 2048, 1), ("m256", 0, 1552, -256), ("m128", 0, 1744, -128)):
+            for x in range(a, b, 512):
+                IOTA(ap(n, x, min(b, x + 512)), [[0, min(b, x + 512) - x]], c, 0)
+                ops[-1]["r"].append(ap("sent", 0, 1))
+        DMA("G", "gy0", [(lambda: T.tb[:, YA:YA + B0], lambda: T.y0r[:])], [ap("tb", YA, YA + B0)], [full("y0r")], 4000.0)
+        for r in range(0, 16, 4):
+            SEL(ap("bm", 128 * r, 128 * r + 512), ap("one2", 128 * r, 128 * r + 512), [[-1, 4], [-16, 8], [0, 16]], OP.is_equal, -r, 1)
+
+    def threshold(t, k, with_new):
+        th = float(THETA[t])
+        MM(ps(7, 0, k), [(blk, ap("sgl", 0, k))])
+        ACT(ap("jk", 0, k), ps(7, 0, k), acc=ACC)
+        if with_new:
+            TS(LB, ACC, 0.5, OP.mult, SLC, OP.add)
+            TS(col(12), LB, -15.5, OP.add)
+            TS(col(13), LB, th, OP.add)
+            return
+        TS(Q, ACC, 16.0 * k - 31.0, OP.add, 1.0 / 64, OP.mult)
+        TS(LP, ACC, 0.5, OP.mult, 8.0 * k + th, OP.add)
+        TS(THR, Q, -32.0, OP.mult, LP, OP.add)
+
+    def lists(a, b):
+        MMS([(ps(7, 128 * h + a, 128 * h + b), [(idf, ap("e%d" % h, a, b)), (idn, ap("dead", a, b))]) for h in (0, 1)])
+        for h in (0, 1):
+            TS(ap("gu", 128 * h + a, 128 * h + b), ps(7, 128 * h + a, 128 * h + b), float(DUM), OP.min)
+
+    def own_x(c):
+        CP(full("ou"), sm(0, 24))
+        for j in range(6):
+            ACT(ap("xo", 64 * j, 64 * j + 64), ind(ap("xx", 0, c), ap("ou", 4 * j, 4 * j + 4)), scale=-1.0 if j % 2 else 1.0)
+
+    MM(ps(4, 0, 85), wrap("z512", "y0r", 0, 85))
+    ACT(ap("sgl", 0, 85), ps(4, 0, 85), AF.Sign, bias=-512 * 175.5)
+    MM(ps(5, 0, V0), [(blk, ap("xx", 0, V0))])
+    threshold(0, 85, False)
+    ACT(ap("dead", 0, 85), ps(4, 0, 85), AF.Relu, scale=-8.0, bias=8 * 512 * 175.5)
+    for d in range(3):
+        for j in (0, 1):
+            CP(ap("old", 192 + 8 * d + 4 * j, 196 + 8 * d + 4 * j), ap("sndi", 4 * d, 4 * d + 4))
+    CP(full("su"), ap("old", 192, 216))
+    TS(full("eo"), ind(full("enb"), full("su")), 384.0, OP.min, -192.0, OP.add)
+    MM(ps(6, 0, 24), wrap("z01", "eo", 0, 24))
+    ACT(sm(0, 24), ps(6, 0, 24))
+    own_x(V0)
+    p85 = (0, 85, 1)
+    CP(ap("entf", 0, 256, 1, p85), ap("ent", 0, 256, 1, p85))
+    for h in (0, 1):
+        TR(ps(0, 128 * h, 128 * h + 85), ap("entf", 128 * h, 128 * h + 128, 1, p85), ap("idf", 0, 85, 1, p85))
+    for h in (0, 1):
+        e, raw, s1, s2 = ps(0, 128 * h, 128 * h + 85), ap("b%d" % h, 0, 85), ap("nm", 192 * h, 192 * h + 85), ap("nm", 192 * h + 96, 192 * h + 181)
+        ACT(raw, e)
+        ACT(s1, e, AF.Sign, bias=-(FAR + 63.5))
+        ACT(s2, e, AF.Sign, bias=-(FAR + 127.5))
+        ACT(ap("ow%d" % h, 0, 85), e, AF.Relu, scale=-4096.0, bias=4096 * (FAR - 0.5))
+        far = [(full("i32"), s1), (full("i32"), s2)]
+        MMS([(ps(1 + h, 0, 85), [(idf, raw)] + far), (ps(1 + h, 128, 213), far)])
+        ACT(ap("e%d" % h, 0, 85), ps(1 + h, 0, 85), bias=64.0)
+        ACT(ap("adj%d" % h, 0, 85), ps(1 + h, 128, 213), bias=64.0)
+    lists(0, 85)
+    for a in range(0, B0, 512):
+        TS(ap("rr", a, min(B0, a + 512)), ap("y0r", a, min(B0, a + 512)), 2.0, OP.mult)
+    CP(ap("bl", 0, V0), full("bli"))
+    for a in (0, 512):
+        TS(ap("fl", a, a + 512), ap("y0r", a, a + 512), 0.125, OP.mult, 128.5625, OP.add)
+        TS(ap("t8", a, a + 512), ap("fl", a, a + 512), -8.0, OP.mult, 1032.0, OP.add)
+
+    for t in range(RO):
+        M, C, dl, last = B0 + P * t, V0 + P * t, float(DELTA[t]), t == RO - 1
+        K, KC = M // 16, C // 16
+        S = K + 1
+        yc, yn = (YA, YB) if t % 2 == 0 else (YB, YA)
+        sb, ld = "sb%d" % t, "ld%d" % t
+        wl, wh, wwin = ap("tb", LOW, LOW + KON), ap("tb", HIGH, HIGH + KON), full("ww")
+        k = lambda n, a=0: ap(n, a, a + K)
+        w16 = lambda n, a, b, o=0: ap(n, o + 16 * a, o + 16 * b)
+        TS(ap("nc", 0, C), ps(5, 0, C), THR, OP.is_ge, -1.0, OP.mult)
+        o, x, z = ap("rem", 0, C), ap("nc", 0, C), ap("zero", 0, C)
+        add("V", lambda g, o=o, x=x, z=z: g.vector.tensor_tensor_scan(real(o), real(x), real(z), 193.0, OP.add, OP.max),
+            [o], [x, z], vcost(o, [x, z]))
+        TT(ap("ww", 0, C), ap("rem", 0, C), ap("nc", 0, C), OP.mult)
+        TS(ap("dd", 0, C), ap("ww", 0, C), 16.0, OP.mult, -dl, OP.max)
+        TT(full(sb), ind(ap("dd", 0, C), full("ou")), full("xo"), OP.add)
+        add("G", lambda g, t=t: send(g, t), [ap("sent", t, t + 1)], [full(sb)], 300.0, 0.0, "none")
+        add("X", None, [full(ld)], [ap("sent", t, t + 1)], 0.0, 4200.0 if t == 0 else 2700.0, "arr%d" % t, 0)
+        if t == 0:
+            late_constants()
+        for a in range(0, C, 512):
+            b = min(C, a + 512)
+            pl = ps(0, 0, b) if a == 0 else ps(6, 256, 256 + b - a)
+            MM(ps(5, a, b), [(idn, ap("xx", a, b)), (nidn, ap("dd", a, b))])
+            TS(ap("tb", HIGH + a, HIGH + b), ps(5, a, b), 63.0, OP.min)
+            MM(pl, [(idn, ap("xx", a, b)), (idn, ap("dd", a, b))])
+            ACT(ap("tb", LOW + a, LOW + b), pl, AF.Relu)
+        MM(ps(4, 0, KC), wrap("z16", "ww", 0, KC))
+        TS(sm(32, KC), ps(4, 0, KC), 0.0, OP.is_ge)
+        TT(sm(80, KC), sm(32, KC), ap("jw", 0, KC), OP.mult)
+        TT(sm(32, KC), ps(4, 0, KC), sm(80, KC), OP.add)
+        TS(ap("tg", 0, KC), sm(32, KC), 192.0, OP.add)
+        DMA("S", "dd%d" % t, [(lambda: T.dlb[:, 0:P], lambda: T.iov[:, 768:960])], [ap("dlb", 0, P)], [ap("iov", 768, 960)])
+        for a in range(0, KC, 12):
+            CP(ind(ap("dlb", 0, P + C), ap("tg", a, a + 12)), ap("iov", 16 * a, 16 * a + 192))
+        TS(ap("tb", HIGH + FAR, HIGH + FAR + 320), ap(ld, 64, 384), -1.0, OP.mult, 63.0, OP.min)
+        TS(ap("tb", LOW + FAR, LOW + FAR + 320), ap(ld, 0, 320), 0.0, OP.max)
+        MM(ps(6, 0, 320), [(idn, ap(ld, 0, 320)), (idn, ap(ld, 64, 384))])
+        ACT(full("wf"), ps(6, 0, 320))
+        cuts = [(c, min(K, c + 32)) for c in range(0, K, 32)]
+        halves = [(0, 32), (32, 64), (64, K)]
+        gu = lambda h, a, b: ap("gu", 128 * h + a, 128 * h + b)
+        for a, b in halves:
+            TT(w16("nh", a, b), ind(wh, gu(0, a, b)), w16("rr", a, b), OP.subtract)
+            ACT(w16("zh", a, b), ind(wh, gu(1, a, b)))
+        for a, b in halves:
+            TT(w16("nl", a, b), ind(wl, gu(0, a, b)), w16("rr", a, b), OP.subtract)
+        nb = 0
+        for n, o in (("nh", "ahh"), ("nl", "alh")):
+            for a, b in cuts:
+                d = ps((0, 1, 7)[nb % 3], 0, 16 * (b - a)); nb += 1
+                MM(d, [(idn, w16(n, a, b)), (idn, w16("zh", a, b))])
+                ACT(w16(o, a, b), d, AF.Abs)
+        for n, d, o in (("nh", "dhl", "ahl"), ("nl", "dll", "all")):
+            for a, b in halves:
+                TT(w16(d, a, b), ind(wl, gu(1, a, b)), w16(n, a, b), OP.add)
+                ACT(w16(o, a, b), w16(d, a, b), AF.Abs)
+        ones = ap("one2", 0, K)
+        IOTA(k("kc"), [[0, K]], C + 192, 0)
+        info = [ps(4, 128 + 128 * h, 128 + 128 * h + K) for h in (0, 1)]
+        for h in (0, 1):
+            for a, b in halves:
+                (CP if (h, a) in ONV else ACT)(w16("i%d" % h, a, b), ind(wwin, gu(h, a, b)))
+        for d in (1, 2, 3):
+            CP(ind(ap("i%d" % (1 if q + d < 4 else 0), 0, M), ap("su", 8 * d - 8, 8 * d - 4)), ap("wf", 128 * d - 128, 128 * d - 64))
+        for h in (0, 1):
+            MM(info[h], [(idn, k("kc")), (idn, k("dead"))] + wrap("z16", "i%d" % h, 0, K))
+        MM(ps(3, K, 2 * K), [(i4k, ones)] + wrap("z8k", "ahh", 0, K))
+        MM(ps(3, 0, K), wrap("z8k", "alh", 0, K))
+        MM(ps(2, K, 2 * K), [(i4k, ones)] + wrap("z8k", "ahl", 0, K))
+        for a, b in ((0, 64), (64, K)):
+            MM(ps(2, a, b), wrap("z8k", "all", 16 * a, b - a))
+        MM(ps(6, 480, 492), wrap("z1", "dlb", 0, 12))
+        CP(full("dlu"), ps(6, 480, 492))
+        if not last:
+            TS(sm(128, 12), ps(6, 480, 492), 0.0625, OP.mult)
+        ACT(ap("old", 0, P), ind(full("bl"), full("dlu")))
+        ACT(full("hib"), full("old"), scale=0.0625, bias=128.53125)
+        for n, c in (("sf", S), ("ms", -16 * S)):
+            IOTA(full(n), [[0, 128]], c, 0)
+            SEL(full(n), full(n), [[-1, 128]], OP.is_equal, 0, 1)
+        MM(ps(6, 256, 472), [(full("sf"), full("old")), (full("ms"), full("hib")), (idn, full("hib"))])
+        TS(full("ox"), ps(6, 256, 472), 1.0 + 129 * (16 * S - 1), OP.add)
+        IOTA(full("nba"), [[1, P]], (M + 1) % 64, 0)
+        IOTA(full("nbb"), [[0, P]], (M + 1) // 64 * 64 - 8192, 0)
+        ACT(full("hg"), ind(wh, full("dlu")))
+        TT(full("nyc"), ind(wl, full("dlu")), full("hg"), OP.subtract)
+        TS(full("ex"), full("nyc"), 0.0, OP.is_lt)
+        if last:
+            DMA("S", "dout", [(lambda: T.yx[:, 0:768], lambda: T.tb[:, LOW:LOW + 768]), (lambda: T.yx[:, 768:960], lambda: T.hg[:])],
+                [], [ap("tb", LOW, LOW + 768), full("hg")])
+            TS(full("ncst"), ap("iof", 0, P), float(C), OP.add, col(10), OP.mult)
+            MM(ps(6, 0, P), [(ap("z1", 15, 143), ap("dlb", 0, P))])
+            TT(full("vn"), ps(6, 0, P), full("ncst"), OP.add)
+        else:
+            MM(ps(6, 0, P), [(blk, full("nyc"))])
+            ACT(full("lc"), ps(6, 0, P), AF.Sign, scale=-1.0, bias=-175.5, acc=col(11))
+            TS(SLC, col(11), 0.5, OP.mult, 8.0 * K + 96, OP.add)
+            ACT(ap("exm", C, C + P), full("ex"), scale=64.0, bias=-67.0)
+            C2, sh = C + P, 331 * t
+            marks = sorted(set([0, 512, C, C2] + ([1024 - sh] if 1024 - sh < C2 else [])))
+            for a, b in zip(marks[:-1], marks[1:]):
+                src = ap("tb", LOW + a, LOW + b) if a < C else ap("hg", a - C, b - C)
+                y = (a + sh) & 1023
+                MM(ps(5, a, b), [(idn, src), (idn, ap("y0r", y, y + b - a)), (idn, ap("t8", y, y + b - a)), (idn, ap("exm", a, b))])
+            TS(ap("xx", 0, C2), ps(5, 0, C2), 0.0, OP.max, 63.0, OP.min)
+            for a in range(0, C2, 512):
+                b = min(C2, a + 512)
+                MM(ps(5, a, b), [(blk, ap("xx", a, b))])
+        ACT(k("wi1"), info[1])
+        TT(k("t0"), info[0], k("wi1"), OP.min)
+        TS(k("unt"), k("t0"), C + 192.0, OP.is_ge, 6144.0, OP.mult)
+        for h in (0, 1):
+            TT(info[h], info[h], k("ow%d" % h), OP.min)
+        pb = [ps(7, 128 * h, 128 * h + K) for h in (0, 1)]
+        MM(pb[0], [(idf, k("e0")), (idn, k("unt"))])
+        MM(pb[1], [(idf, k("e1")), (idn if t % 2 else nidn, k("unt"))])
+        TS(pb[0], pb[0], float(KON), OP.min)
+        if t % 2 == 0:
+            TT(pb[1], pb[1], k("jwm"), OP.max)
+            wz, off = ap("tb", YA, YB), float(LOW - YA)
+        else:
+            TT(pb[1], pb[1], k("jw4"), OP.min)
+            wz, off = ap("tb", LOW, YB + M), 0.0
+        ACT(ap("c1", 0, 2 * K), ps(3, 0, 2 * K), bias=2048.0)
+        TT(ap("mm", 0, 2 * K), ps(2, 0, 2 * K), ap("c1", 0, 2 * K), OP.min)
+        TT(k("best"), k("mm"), k("mm", K), OP.min)
+        TS(k("ab"), k("best"), 1, OP.logical_shift_right, 2048, OP.bitwise_and)
+        TT(k("t4"), pb[0], k("ab"), OP.add)
+        CP(k("ix"), k("t4"))
+        TS(k("ab", 112), k("best"), 2048, OP.bitwise_and)
+        TT(k("t5"), pb[1], k("ab", 112), OP.add)
+        TS(k("ix", 128), k("t5"), off, OP.add)
+        for i, (a, b) in enumerate([(0, 16), (16, 48), (48, 80), (80, K)]):
+            pre = ps((0, 1, 3, 2)[i], 0, 16 * (b - a))
+            MM(pre, [(full("ihf"), w16("tb", a, b, yc)), (full("i63"), ap("one2", 0, 16 * (b - a)))])
+            ACT(w16("zh", a, b), ind(ap("tb", LOW, YB), ap("ix", a, b)))
+            TT(w16("dll", a, b), ind(wz, ap("ix", 128 + a, 128 + b)), w16("zh", a, b), OP.subtract)
+            ACT(w16("dhl", a, b), w16("dll", a, b), AF.Abs, scale=0.5)
+            TT(w16("tb", a, b, yn), pre, w16("dhl", a, b), OP.add)
+        TT(k("t0"), info[0], k("ab"), OP.min)
+        TT(info[1], info[1], k("ab", 112), OP.min)
+        TT(k("t1"), info[1], k("t0"), OP.add)
+        ACT(k("t2"), k("t1"), AF.Relu, bias=1.0 - C)
+        TS(k("cp"), k("t2"), 200.0, OP.min, 1.0, OP.add)
+        TT(k("e0"), k("e0"), k("t0"), OP.max)
+        TT(k("e1"), info[1], k("e1"), OP.max)
+        if last:
+            pk = (0, K, 1)
+            for h in (0, 1):
+                TT(k("b%d" % h), k("e%d" % h), k("adj%d" % h), OP.subtract)
+                TR(ps(5, 128 * h, 128 * h + 128, pk), k("b%d" % h), idf)
+            ACT(ap("et", 0, 256, 1, pk), ps(5, 0, 256, pk))
+            DMA("S", "dout", [(lambda r=r: T.ye[r, 0:1744], lambda r=r: T.et[0:109, ecol(r):ecol(r) + 16]) for r in range(16)], [], [full("et")])
+        for a, b in ((0, 48), (48, K)):
+            MM(ps(4, a, b), [(blk, ap("k1", a, b)), (blk, ap("k2", a, b))] + wrap("z512", "tb", yn + 16 * a, b - a))
+        TT(k("code", 1), ps(4, 0, K), k("cp"), OP.min)
+        if last:
+            DMA("S", "dyy", [(lambda: T.yy[:, 0:1744], lambda: T.m128[:])], [ap("yy", 0, 1)], [full("m128")], 3000.0)
+            DMA("G", "gyy", [(lambda: T.yy[:, 0:1744], lambda yn=yn: T.tb[:, yn:yn + 1744])], [ap("yy", 0, 1)], [ap("tb", yn, yn + M)], 4000.0)
+        else:
+            ACT(k("dead"), ps(4, 0, K), AF.Relu, scale=-16.0)
+            DMA("S", "dr%d" % t, [(lambda M=M: T.rr[:, 0:M], lambda M=M: T.m256[:, 0:M])], [ap("rr", 0, M)], [ap("m256", 0, M)], 3000.0)
+            for n in ("ga", "gb"):
+                DMA("G", n + str(t), [(lambda M=M: T.rr[:, 0:M], lambda M=M, yn=yn: T.tb[:, yn:yn + M])], [ap("rr", 0, M)], [ap("tb", yn, yn + M)], 4000.0)
+            ACT(k("sgl"), k("code", 1), AF.Sign)
+            lists(0, K)
+            threshold(t + 1, K, True)
+        for j in range(4):
+            MMS([(ps(j, (r % 4) * S, (r % 4 + 1) * S), [(ap("bm", 128 * r, 128 * r + 128), ap("code", 0, S))]) for r in range(4 * j, 4 * j + 4)])
+            if j % 2:
+                TS(ap("st", 4 * S * j, 4 * S * (j + 1)), ps(j, 0, 4 * S), 0.0, OP.max)
+            else:
+                ACT(ap("st", 4 * S * j, 4 * S * (j + 1)), ps(j, 0, 4 * S), AF.Relu)
+        stw, W = ap("st", 0, 16 * S), (192 if last else 216)
+        H = W // 4
+        for j in (0, 2, 1, 3):
+            (CP if j >= 2 else ACT)(w16("sg", H * j, H * (j + 1)), ind(stw, ap("ox", H * j, H * (j + 1))))
+        for j in (0, 2, 1, 3):
+            MM(ps(4, H * j, H * (j + 1)), wrap("z16", "sg", 16 * H * j, H))
+        cd = ps(4, 0, P)
+        e1b, e2b, kb = full("e1b"), full("e2b"), full("kb")
+        TT(e1b, cd, full("ri"), OP.is_equal)
+        TS(e2b, cd, 200.0, OP.is_ge)
+        ACT(kb, cd, AF.Sign)
+        if not last:
+            MM(ps(0, P, 2 * P), [(blk, full("lc")), (blk, e1b), (blk, e2b)])
+            MM(ps(0, 0, P), [(blk, full("lc")), (nblk, e1b), (nblk, e2b), (blk, kb)])
+            ACT(full("jk"), ps(0, 0, 2 * P), AF.Relu, bias=-31.0, acc=NB)
+            TS(Q, NB, col(12), OP.subtract, -1.0 / 32, OP.mult)
+            TS(LP, NB, -1.0, OP.mult, col(13), OP.add)
+            TS(THR, Q, -32.0, OP.mult, LP, OP.add)
+            TS(sm(160, 24), ps(4, P, W), 2.0, OP.is_ge)
+            TS(sm(184, 24), ps(4, P, W), C - 2.0, OP.add)
+            TT(sm(208, 24), sm(160, 24), sm(184, 24), OP.mult)
+            TT(sm(0, 24), sm(0, 24), sm(208, 24), OP.max)
+            own_x(C + P)
+        for bank, pos, neg, first in ((1, blk, nblk, []), (2, full("tri"), full("ntri"), []), (3, i4k, n4k, [(idf, ap("old", 0, P))])):
+            MM(ps(bank, P, 2 * P), first + [(pos, e1b), (pos, e2b)])
+            MM(ps(bank, 0, P), first + [(neg, e1b), (neg, e2b), (pos, kb)])
+        ACT(full("nm"), ps(1, 0, 2 * P), AF.Relu, bias=-15.0)
+        ACT(full("ff"), ps(2, 0, 2 * P), AF.Relu, bias=col(14))
+        ACT(full("r1"), ps(3, 0, 2 * P), AF.Relu, bias=1.0 - 4096)
+        made = lambda pos, neg: [(pos, full("ex")), (neg, ap("nm", 0, P)), (neg, ap("nm", P, 2 * P))]
+        for h in (0, 1):
+            MM(ps(2, P * h, P * h + P), [(idn, full("nba")), (idn, full("nbb"))] + made(i4k, n4k) + [(i4k, ap("ff", P * h, P * h + P))])
+        TT(full("tv"), ps(2, 0, 2 * P), full("r1"), OP.max)
+        TS(ind(full("bl"), full("dlu")), ap("tv", 0, P), 1.0, OP.mult, -1.0, OP.add)
+        ACT(full("tn") if last else ap("bl", C, C + P), ap("tv", P, 2 * P), bias=-1.0)
+        MM(ps(1, 0, P), made(idn, nidn))
+        MM(ps(1, P, 2 * P), made(i4k, n4k) + [(nidn, full("nyc"))])
+        ym = ap("my", P, 2 * P)
+        ACT(ym, ps(1, P, 2 * P), AF.Relu, bias=-4096.0)
+        if last:
+            TT(full("vn"), ps(1, 0, P), full("vn"), OP.mult)
+            DMA("S", "dout", [(lambda: T.yy[:, 1744:1936], lambda: T.my[:, P:2 * P])], [], [ym])
+            DMA("S", "dout", [(lambda h=h: T.ye[h:16:2, 1744:1936], lambda h=h: T.vn[h:128:16, :]) for h in (0, 1)], [], [full("vn")])
+            DMA("S", "dout", [(lambda: T.yl[:, 0:768], lambda: T.bl[:, 0:768])], [], [ap("bl", 0, 768)], 3600.0)
+            DMA("S", "dout", [(lambda: T.yl[:, 768:960], lambda: T.tn[:])], [], [full("tn")], 2500.0)
+        else:
+            ACT(ap("my", 0, P), ps(1, 0, P))
+            ACT(ap("tb", yn + M, yn + M + P), ym, bias=128.0)
+            ACT(ap("rr", M, M + P), ym, scale=2.0)
+            MM(ps(3, 0, 24), wrap("z1", "my", 0, 24))
+            TT(ap("e0", K, K + 12), ps(3, 0, 12), sm(128, 12), OP.mult)
+            ACT(sm(232, 12), ap("jw", 0, 12), scale=0.0625, bias=C / 16.0)
+            TT(ap("e1", K, K + 12), ps(3, 0, 12), sm(232, 12), OP.mult)
+            ACT(ap("dead", K, K + 12), ps(3, 12, 24), AF.Relu, scale=-4096.0, bias=4096 * 175.5)
+            lists(K, K + 12)
+    return ops
+
+
+def span(x):
+    if x["n"] == "ps":
+        return x["a"] // 512 * 512, (x["b"] + 511) // 512 * 512
+    return x["a"], x["b"]
+
+
+def depend(ops):
+    log = {}
+    for i, o in enumerate(ops):
+        dep = {}
+        for kind, xs in (("r", o["r"]), ("w", o["w"])):
+            for x in xs:
+                a, b = span(x)
+                for (j, kj, aj, bj) in log.get(x["n"], []):
+                    if j == i or bj <= a or b <= aj:
+                        continue
+                    same = ops[j]["e"] == o["e"]
+                    if kind == "r" and kj == "r" and (x["n"] != "ps" or same):
+                        continue
+                    wait = not (x["n"] == "ps" and same and o["e"] == "P")
+                    dep[j] = dep.get(j, False) or wait
+        for kind, xs in (("r", o["r"]), ("w", o["w"])):
+            for x in xs:
+                a, b = span(x)
+                l = log.setdefault(x["n"], [])
+                if kind == "w":
+                    l[:] = [e for e in l if not (a <= e[2] and e[3] <= b)]
+                l.append((i, kind, a, b))
+        o["dep"] = dep
+
+
+def place(eng, cost, succ, left0, prio):
+    n = len(cost)
+    left, at, start = list(left0), [0.0] * n, [0.0] * n
+    ready = [(prio[i], i) for i in range(n) if left[i] == 0]
+    busy = {e: [] for e in "VAPGSX"}
+    while ready:
+        m = min(ready)
+        ready.remove(m)
+        i = m[1]
+        s, b, c = at[i], busy[eng[i]], cost[i]
+        x = len(b)
+        while x > 0 and b[x - 1][1] > s:
+            x -= 1
+        k = len(b)
+        while x < k and b[x][0] < s + c:
+            s = max(s, b[x][1])
+            x += 1
+        b.insert(x, (s, s + c))
+        start[i] = s
+        for j, d in succ[i]:
+            if s + c + d > at[j]:
+                at[j] = s + c + d
+            left[j] -= 1
+            if left[j] == 0:
+                ready.append((prio[j], j))
+    return start
+
+
+PRIO = {}
+
+
+def schedule(ops, wake=120.0, tries=16000, seed=1, heat=60.0):
+    n = len(ops)
+    eng, cost = [o["e"] for o in ops] + ["X"], [o["c"] + 1.0 for o in ops] + [1.0]
+    fwd, left = [[(n, o["lat"])] for o in ops] + [[]], [len(o["dep"]) for o in ops] + [n]
+    bwd = [[] for _ in ops] + [[(i, o["lat"]) for i, o in enumerate(ops)]]
+    for i, o in enumerate(ops):
+        for j, w in o["dep"].items():
+            d = ops[j]["lat"] + (wake if w else 0.0)
+            fwd[j].append((i, d)); bwd[i].append((j, d))
+    if n not in PRIO:
+        rank = [0.0] * (n + 1)
+        for i in range(n - 1, -1, -1):
+            rank[i] = cost[i] + max(rank[j] + d for j, d in fwd[i])
+        rng = np.random.RandomState(seed)
+        cur = best = place(eng, cost, fwd, left, [-r for r in rank])
+        name = [(o["e"], o["w"][0]["n"]) if o["w"] else o["e"] for o in ops]
+        kin = [[j for j in range(max(0, i - 14), min(n, i + 15)) if name[j] == name[i]] for i in range(n)]
+        arcs = None
+        for it in range(tries):
+            if it % 50 == 49:
+                back = place(eng, cost, bwd, [len(f) for f in fwd], [-(cur[i] + cost[i]) for i in range(n + 1)])
+                new = place(eng, cost, fwd, left, [-(back[i] + cost[i]) for i in range(n + 1)])
+                if new[n] <= cur[n]:
+                    cur, arcs = new, None
+                    if cur[n] < best[n]:
+                        best = cur
+                continue
+            if arcs is None:
+                ends = {(eng[i], round(cur[i] + cost[i], 3)): i for i in range(n)}
+                arcs, i = [], n
+                while i is not None:
+                    nxt = None
+                    for j, d in bwd[i]:
+                        if abs(cur[j] + cost[j] + d - cur[i]) < 1e-6:
+                            nxt = j
+                    if nxt is None:
+                        nxt = ends.get((eng[i], round(cur[i], 3)))
+                        if nxt is not None:
+                            arcs.append((nxt, i))
+                    i = nxt
+            u, v = arcs[rng.randint(len(arcs))]
+            prio = list(cur)
+            step = float(rng.exponential((400.0, 2000.0, 6000.0)[rng.randint(3)]))
+            fam = rng.uniform() < 0.5
+            if rng.randint(2):
+                for x in (kin[u] if fam else [u]):
+                    if cur[x] >= cur[u] - 3000:
+                        prio[x] = max(cur[x], cur[v] + step + 1e-3 * cur[x])
+            else:
+                to, todo = cur[u] - step * rng.randint(2) - 0.5, list(kin[v] if fam else [v])
+                while todo:
+                    x = todo.pop()
+                    if prio[x] > to:
+                        prio[x] = to - 1e-3 * (cur[n] - cur[x])
+                        todo += [j for j, _ in bwd[x]]
+            new = place(eng, cost, fwd, left, prio)
+            if new[n] <= cur[n] + heat * (1.0 - it / tries) * float(rng.exponential(1.0)):
+                cur, arcs = new, None
+                if cur[n] < best[n]:
+                    best = cur
+        PRIO[n] = best
+    st = place(eng, cost, fwd, left, PRIO[n])
+    for o, t in zip(ops, st):
+        o["t"] = t
+    return sorted(range(n), key=lambda i: (st[i], i))
+
+
+def emit(g, T, ops, order, arrivals, sent):
+    queue = {"V": g.vector, "A": g.scalar, "P": g.tensor, "G": g, "S": g.sync}
+    count, known = {}, {e: {} for e in queue}
+    for i in order:
+        o = ops[i]
+        e = o["e"]
+        if e == "X":
+            o["mark"], o["knows"] = (o["sem"], arrivals), {o["sem"]: arrivals}
+            count[o["sem"]] = arrivals
+            continue
+        kn = known[e]
+        need = sorted((j for j, w in o["dep"].items() if w and ops[j]["mark"]), key=lambda j: -ops[j]["mark"][1])
+        for j in need:
+            sem, val = ops[j]["mark"]
+            if kn.get(sem, 0) < val:
+                queue[e].wait_ge(T.sem[sem], val)
+                for s, v in ops[j]["knows"].items():
+                    kn[s] = max(kn.get(s, 0), v)
+        ins = o["fn"](g)
+        sem = o["sem"] or QSEM[e]
+        if sem == "none":
+            o["mark"] = None
+            continue
+        count[sem] = count.get(sem, 0) + o["inc"]
+        if o["sem"] is None:
+            ins.then_inc(T.sem[sem], 1)
+        o["mark"] = (sem, count[sem])
+        o["knows"] = dict(kn)
+        o["knows"][sem] = count[sem]
+    g.wait_ge(T.sem.sent, sent)
+    for sem, val in count.items():
+        g.sync.wait_ge(T.sem[sem], val)
+
+
+def masks(topo, src, dsts):
+    used, res = set(), {}
+    for d in sorted(dsts, key=lambda d: len(topo.engines(src, d))):
+        pick = [e for e in topo.engines(src, d) if e not in used][:4]
+        used.update(pick)
+        res[d] = sum(1 << e for e in pick)
+    return res
+
+
+def rank_program(g, core, T, topo):
+    q = T.rank_of(core)
+    if q is None:
+        return
+    n = len(T.cores)
+    peers = [T.cores[(q + d) % n] for d in range(1, n)]
+    mask = masks(topo, core, peers)
+
+    def send(g, t):
+        trs = []
+        for d in range(1, n):
+            rid, pid = topo.addr(peers[d - 1], core)
+            trs.append(RemoteDMATransfer(dst_ids=[DstId(rid=rid, pnc=pid)], dma_engine_mask=mask[peers[d - 1]],
+                                         remote_sem=T.sem["arr%d" % t], src=T["sb%d" % t][:, 128 * (d - 1):128 * d],
+                                         dst=T["ld%d" % t][:, 128 * (n - 1 - d):128 * (n - d)]))
+        return g.remote_dma_fused(trs, local_sem=T.sem.sent)
+
+    ops = build(T, send, q)
+    depend(ops)
+    emit(g, T, ops, schedule(ops), 4 * (n - 1), 4 * (n - 1) * RO)

@@ -4,27 +4,36 @@ from concourse.mybir import AluOpType as OP, ActivationFunctionType as AF
 
 V0, B0, P, RO = 384, 1360, 192, 3
 THETA, DELTA = (460, 560, 520), (9, 7, 10)
-FAR, DUM, KON = 960, 1344, 1536
-YA, LOW, HIGH, YB = 112, 2048, 4096, 5632
+FAR = 960
+U0 = 208
+HD, KON = 1024, 1008
+PB = 1200
+WB = [PB - 400 * (t + 1) for t in range(RO)]
+YO = [PB + 2016, PB + 2016 + 1376, PB + 2016 + 1376 + 1568]
+GW = (64, 48)
 BF, F32, I32, U16 = "bfloat16", "float32", "int32", "uint16"
+ZZ = {n: 144 * i for i, n in enumerate("z4k z01 zs z1 z8k zi zc zn8 z16k".split())}
 
 
 def _scratch():
     s = {}
     for names, cols, d in (
-        ("tb", 7568, BF), ("y0r", 1360, BF), ("xx", 960, BF), ("rr", 1744, BF), ("ww", 1536, BF),
-        ("nc rem dd zero exm", 768, BF), ("fl t8", 1024, BF), ("iov dlb", 960, BF), ("iof", 960, F32),
-        ("nl nh zh dll dhl all ahl alh ahh i0 i1 m128", 1744, BF), ("m256", 1552, BF),
-        ("st", 1760, BF), ("sg", 3456, BF), ("bm one2", 2048, BF),
-        ("sb0 sb1 sb2 ld0 ld1 ld2 xo eo nm ff jk my", 384, BF), ("wf", 320, BF),
-        ("blk nblk idn nidn ihf i63 i32 i4k n4k tri ntri ms dead unt kc", 128, BF), ("idf sf", 128, F32),
-        ("z1 z16 z8k z512 z01", 144, BF), ("gm", 8, BF), ("k1 k2 code sgl", 112, BF),
-        ("bl", 1536, F32), ("bli", 384, I32), ("enb", 1360, I32), ("ent", 256, I32), ("entf et sm", 256, F32),
-        ("sndi", 12, I32), ("col", 32, F32), ("coli", 8, I32),
-        ("e0 e1 ow0 ow1 adj0 adj1 jw jw4 jwm cp wi1 b0 b1 t0 t1 t2 t4 t5", 128, F32),
-        ("c1 mm", 224, F32), ("best ab", 224, I32), ("gu ix", 256, U16),
-        ("old", 216, F32), ("hib", 216, BF), ("ox", 216, U16), ("tg", 48, U16), ("dlu", 12, U16), ("ou su", 24, U16),
-        ("hg nyc lc ex ri e1b e2b kb nba nbb", 192, BF), ("ncst vn tn", 192, F32), ("r1 tv", 384, F32),
+        ("tb", YO[2] + 1744, BF), ("inf", 1360, BF), ("dzt", 976, BF),
+        ("y0r", 1360, BF), ("xx dlb", 960, BF), ("nex", 576, BF), ("rr az dz gz nw zt d0 d1 ab0 ab1 ab2 ab3 i0", 1744, BF),
+        ("m256", 256, BF), ("m128", 436, BF), ("c128", 272, BF), ("one2 half", 512, BF),
+        ("nc zero c192", 768, BF), ("cum", 784, BF), ("fl wd", 1024, BF), ("iov", 976, BF), ("iof", 976, F32),
+        ("st yf i1", 1760, BF), ("sg", 3264, BF), ("bm", 2048, BF),
+        ("sb0 sb1 sb2 nm", 384, BF), ("zz", 144 * len(ZZ), BF), ("gm", 8, BF),
+        ("blk idn nidn ihf i63 i4k n4k i2k i256 i1k ic n64 i2 n2112 i960 id0 ie0 id1 ie1 id2 ie2 tri t4 nt4 t2 ms b64 nb64 b32 nblk nd8 "
+         "e01 ne01 e0a e0b e1 idl nidl idl0 nidl0", 128, BF),
+        ("idf nidf blkh sf", 128, F32),
+        ("k12 cp sgl sw far unt mine th tj c208 c1k", 112, BF), ("k3", 16, BF),
+        ("bl", 1168, F32), ("bli", 384, I32), ("enb", 1360, I32), ("ent", 256, I32), ("entf et", 256, F32),
+        ("sndi", 12, I32), ("col", 32, F32), ("coli", 8, I32), ("oh", 16, F32), ("sm", 96, F32),
+        ("jw swf fa araw r0 r1", 112, F32), ("jt", 48, F32), ("own", 24, F32), ("pbc", 336, F32),
+        ("ee c1 mm t45 t01", 224, F32), ("iv kk", 224, BF), ("ab", 224, I32), ("best", 112, I32), ("gu", 448, U16), ("ix", 224, U16),
+        ("old", 204, F32), ("hib", 204, BF), ("ox", 204, U16), ("tg", 48, U16), ("dlu su", 12, U16), ("ou", 24, U16),
+        ("hg lg lc ri ne mv nx5 kbs nba nbb mone eo my", 192, BF), ("vn tv", 192, F32), ("rk", 384, F32),
     ):
         for n in names.split():
             s[n] = ("sbuf", [128, cols], d)
@@ -33,19 +42,23 @@ def _scratch():
 
 
 SHAPES = _scratch()
-PART = {n: 128 * i for i, n in enumerate(n for n, s in SHAPES.items() if s[1][1] == 128 and s[2] == F32)}
+PART = {n: (b, 128 * i) for b, d in (("fw", F32), ("mw", BF))
+        for i, n in enumerate(n for n, s in SHAPES.items() if s[1][1] == 128 and s[2] == d)}
 SCRATCH = {n: s for n, s in SHAPES.items() if n not in PART}
-SCRATCH["fw"] = ("sbuf", [128, 128 * len(PART)], F32)
-SEMAPHORES = ["qv", "qa", "qp", "qg", "sent", "arr0", "arr1", "arr2", "dy", "dx", "denb", "dsnd", "dbl", "dent", "dout", "dz",
-              "dr0", "dr1", "ga0", "ga1", "gb0", "gb1", "dyy", "gyy", "gy0", "dd0", "dd1", "dd2"]
+SCRATCH.update({b: ("sbuf", [128, 128 * sum(1 for x in PART.values() if x[0] == b)], d) for b, d in (("fw", F32), ("mw", BF))})
+SEMAPHORES = (["qv", "qa", "qp", "qg", "sent", "arr0", "arr1", "arr2", "dy", "dx", "denb", "dsnd", "dbl", "dent", "dout", "dz", "dz2",
+               "dyy", "gyy", "gy0", "dy0", "drr", "grr", "gwd", "dd0", "dd1", "dd2"]
+              + ["%s%d%d" % (n, t, g) for n in ("dr", "ga", "gb") for t in (0, 1) for g in (0, 1)])
 QSEM = {"V": "qv", "A": "qa", "P": "qp", "G": "qg"}
-CYC, PEC, GAT, SCA = 1.04, 0.52, 1.56, 3.8
-ONV = ()
+EST = ((0.92, 1.45, 3.8), (0.83, 1.1, 2.5), (1.12, 1.85, 4.5))
+HS = 64
+ONV = ((0, 0),)
+RELU = ()
 
 
 def ap(n, a, b, s=1, p=(0, 128, 1)):
     if n in PART:
-        n, a, b = "fw", a + PART[n], b + PART[n]
+        n, a, b = PART[n][0], a + PART[n][1], b + PART[n][1]
     return {"n": n, "a": a, "b": b, "s": s, "p": p}
 
 
@@ -68,8 +81,10 @@ def size(x):
     return 2 if SCRATCH[x["n"]][2] in (BF, U16) else 4
 
 
-def build(T, send, q=0):
+def build(T, send, est=EST[0]):
     ops = []
+    CYC, GAT, SCA = est
+    PEC = CYC / 2
 
     def real(x):
         if not isinstance(x, dict):
@@ -143,385 +158,484 @@ def build(T, send, q=0):
         return ap(n, 0, SHAPES[n][1][1])
 
     def wrap(z, n, a, k):
-        return [(ap(z, 15 - r, 143 - r), ap(n, a + r, a + 16 * k, 16)) for r in range(16)]
+        return [(ap("zz", ZZ[z] + 15 - r, ZZ[z] + 143 - r), ap(n, a + r, a + 16 * k, 16)) for r in range(16)]
 
-    def DMA(eng, sem, pairs, outs, ins, lat=2200.0):
+    def pairs(z, n, a):
+        return [(ap("zz", ZZ[z] + 15 - r, ZZ[z] + 143 - r), ap(n, a + r // 2, a + 192, 8)) for r in range(16)]
+
+    def DMA(eng, sem, copies, outs, ins, lat=1900.0):
         def fn(g):
-            for o, i in pairs:
+            for o, i in copies:
                 if eng == "G":
                     g.dma_start(o(), i(), accum_op=OP.add).then_inc(T.sem[sem], 16)
                 else:
-                    g.sync.dma_start(o(), i()).then_inc(T.sem[sem], 16)
+                    (g.scalar if eng == "A" else g.sync).dma_start(o(), i()).then_inc(T.sem[sem], 16)
             return None
-        add(eng, fn, outs, ins, (1000.0 if eng == "G" else 60.0) * len(pairs), lat, sem, 16 * len(pairs))
+        add(eng, fn, outs, ins, (1000.0 if eng == "G" else 60.0) * len(copies), lat, sem, 16 * len(copies))
 
-    def IOTA(out, pat, base, cm):
+    def IOTA(out, pat, base, cm, t=None):
         if SCRATCH[out["n"]][2] != I32:
             fn = lambda g: g.iota(real(out), pat, base, cm, allow_small_or_imprecise_dtypes=True)
         else:
             fn = lambda g: g.iota(real(out), pat, base, cm)
-        add("G", fn, [out], [], 130 + 2 * width(out) * CYC)
+        add("G", fn, [out], [] if t is None else [ap("sent", t, t + 1)], 130 + 2 * width(out) * CYC)
 
     def SEL(out, x, pat, o, base, cm):
         add("G", lambda g: g.affine_select(real(out), real(x), pat, o, 0.0, base, cm), [out], [x], 170 + 2 * width(out) * CYC)
 
+    EYE = [([[-1, 128]], OP.is_equal, 0, 1)]
+    BLK = [([[-16, 8], [0, 16]], OP.is_ge, 0, 1), ([[16, 8], [0, 16]], OP.is_ge, 15, -1)]
+
+    def scaled(n, rules, c, t=0):
+        IOTA(full(n), [[0, 128]], c, 0, t)
+        for pat, o, base, cm in rules:
+            SEL(full(n), full(n), pat, o, base, cm)
+
     col = lambda i: ap("col", i, i + 1)
     sm = lambda a, n: ap("sm", a, a + n)
-    R16, C256, R2, THR, LB, LP, NB, ACC, SLC = [col(i) for i in range(9)]
-    blk, nblk, idn, nidn, idf, i4k, n4k = [full(n) for n in ("blk", "nblk", "idn", "nidn", "idf", "i4k", "n4k")]
+    (R16, C256, R2, THR, LP, NB, SLC, C12, C13, BASE, WI, WC, K12, PAR, TMP, VNB, ALC, LT8, WS, DB, TM2, ACC) = [col(i) for i in range(22)]
+    OWB = [col(24 + t) for t in range(2)]
+    oh = lambda r: ap("oh", r, r + 1)
     Q = ap("coli", 2, 3)
+    blk, idn, nidn, idf, i4k, n4k, i2k = [full(n) for n in ("blk", "idn", "nidn", "idf", "i4k", "n4k", "i2k")]
+    ones = lambda n: ap("one2", 0, n)
     ecol = lambda r: 128 * (r % 2) + 16 * (r // 2)
+    ee = lambda h, a, b: ap("ee", 112 * h + a, 112 * h + b)
+    w16 = lambda n, a, b, o=0: ap(n, o + 16 * a, o + 16 * b)
 
-    MS(full("enb"), 0)
-    DMA("S", "dy", [(lambda: T.y0r[:], lambda: T.y0[:])], [full("y0r")], [], 3500.0)
-    DMA("S", "dx", [(lambda: T.xx[:, 0:V0], lambda: T.x0[:])], [ap("xx", 0, V0)], [], 3000.0)
-    DMA("S", "dsnd", [(lambda: T.sndi[:], lambda: T.snd[:])], [full("sndi")], [])
-    DMA("S", "denb", [(lambda h=h: T.enb[h:128:16, :], lambda h=h: T.en0[h:16:2, :]) for h in (0, 1)], [full("enb")], [])
+    DMA("S", "dy", [(lambda: T.y0r[:], lambda: T.y0[:])], [full("y0r")], [], 2800.0)
+    DMA("S", "dx", [(lambda: T.xx[:, 0:V0], lambda: T.x0[:])], [ap("xx", 0, V0)], [], 2400.0)
     DMA("S", "dent", [(lambda r=r: T.ent[0:85, ecol(r):ecol(r) + 16], lambda r=r: T.en0[r, :]) for r in range(16)], [full("ent")], [])
+    DMA("S", "dsnd", [(lambda: T.sndi[:], lambda: T.snd[:])], [full("sndi")], [])
+    DMA("A", "denb", [(lambda h=h: T.enb[h:128:16, :], lambda h=h: T.en0[h % 2:16:2, :]) for h in range(16)], [full("enb")], [], 4000.0)
+    DMA("S", "drr", [(lambda: T.rr[:, 0:B0], lambda: T.y0[:])], [ap("rr", 0, B0)], [], 4000.0)
+    DMA("G", "grr", [(lambda: T.rr[:, 0:B0], lambda: T.y0r[:])], [ap("rr", 0, B0)], [full("y0r")], 4000.0)
     DMA("S", "dbl", [(lambda: T.bli[:], lambda: T.bl0[:])], [full("bli")], [])
 
-    MS(ap("one2", 0, 512), 1.0)
-    SEL(full("gm"), ap("one2", 0, 8), [[-16, 8]], OP.is_ge, 0, 1)
-    SEL(full("gm"), full("gm"), [[16, 8]], OP.is_ge, 15, -1)
-    SEL(blk, ap("one2", 0, 128), [[-16, 8], [0, 16]], OP.is_ge, 0, 1)
-    SEL(blk, blk, [[16, 8], [0, 16]], OP.is_ge, 15, -1)
+    MS(ones(512), 1.0)
     IOTA(ap("coli", 0, 1), [[0, 1]], 0, 1)
-    SEL(idn, ap("one2", 0, 128), [[-1, 128]], OP.is_equal, 0, 1)
+    SEL(full("gm"), ones(8), [[-16, 8]], OP.is_ge, 0, 1)
+    SEL(full("gm"), full("gm"), [[16, 8]], OP.is_ge, 15, -1)
+    SEL(blk, ones(128), *BLK[0])
+    SEL(blk, blk, *BLK[1])
+    SEL(idn, ones(128), *EYE[0])
+    IOTA(ap("iof", 0, 208), [[1, 208]], 0, 0)
+    SEL(full("e01"), ones(128), [[-16, 8], [200, 16]], OP.is_equal, -200, 1)
+    IOTA(ap("iof", 208, 592), [[1, 384]], 208, 0)
     TS(ap("coli", 1, 2), ap("coli", 0, 1), 15, OP.bitwise_and)
     CP(R16, ap("coli", 1, 2))
+    TS(full("oh"), ap("iof", 0, 16), R16, OP.is_equal)
     TS(C256, R16, -256.0, OP.mult)
     TS(R2, R16, 2.0, OP.is_lt)
-    TS(col(10), R16, 1.0, OP.is_equal)
-    TS(col(14), R16, -1.0, OP.mult, 1.0, OP.add)
-    for z, c in (("z512", 512.0), ("z01", R2), ("z16", 0.0625), ("z1", 1.0), ("z8k", 8192.0)):
-        MS(full(z), 0.0)
-        TS(ap(z, 15, 143, 16), full("gm"), c, OP.mult)
-    for n, c in (("nidn", -1.0), ("ihf", 0.5), ("i63", 63.75), ("i32", 32.0), ("i4k", 4096.0), ("n4k", -4096.0), ("idf", 1.0)):
-        ACT(full(n), idn, scale=c)
-    ACT(nblk, blk, scale=-1.0)
-    SEL(full("tri"), blk, [[1, 128]], OP.is_gt, 0, -1)
-    TT(full("tri"), full("tri"), full("i32"), OP.subtract)
-    ACT(full("ntri"), full("tri"), scale=-1.0)
-    IOTA(ap("iof", 0, 384), [[1, 384]], 0, 0)
-    IOTA(ap("iof", 768, 960), [[1, 192]], DUM, 0)
-    IOTA(ap("iof", 384, 768), [[1, 384]], 384, 0)
-    for a, b in ((0, 384), (768, 960), (384, 768)):
+    TS(LT8, R16, 8.0, OP.is_lt)
+    ACT(TMP, oh(0), scale=-240.0)
+    ACT(BASE, oh(3), scale=255.0, bias=TMP)
+    ACT(WI, oh(1), scale=1.0 / 4096, bias=oh(0))
+    ACT(WC, oh(3), scale=4.0, bias=oh(0))
+    ACT(WS, LT8, scale=1.0 / 1024, bias=-1.0 / 2048)
+    TS(ap("coli", 3, 4), ap("coli", 0, 1), 1, OP.bitwise_and)
+    TS(PAR, ap("coli", 3, 4), float(HD), OP.mult)
+    MS(full("zz"), 0.0)
+    for z, c in (("z4k", 4096.0), ("z01", R2), ("zs", WS), ("z1", 1.0), ("z8k", 8192.0), ("zc", WC), ("zn8", -8192.0), ("z16k", 16384.0)):
+        TS(ap("zz", ZZ[z] + 15, ZZ[z] + 143, 16), full("gm"), c, OP.mult)
+    TS(ap("zz", ZZ["zi"] + 15, ZZ["zi"] + 143, 16), full("gm"), WI, OP.mult, 1.0 / HD, OP.mult)
+    MS(ap("e0a", 0, 256), 0.0)
+    for n, r, c in (("e0a", 0, 16.0), ("e0a", 3, -255.0 / 16), ("e0b", 0, -255.0 / 16), ("e0b", 3, 255.0 / 16)):
+        TS(ap(n, r, 128, 16), full("gm"), c, OP.mult)
+    for n, s, c in (("idf", idn, 1.0), ("blkh", blk, 0.5), ("nidf", idn, -1.0), ("ne01", full("e01"), -1.0), ("idl0", idn, DELTA[0]),
+                    ("nidl0", idn, -DELTA[0]), ("nidn", idn, -1.0), ("i4k", idn, 4096.0), ("n2112", idn, -2112.0), ("i960", idn, 960.0),
+                    ("id0", idn, 400.0), ("ie0", idn, 400.0 + HD)):
+        ACT(full(n), s, scale=float(c))
+
+    def digits(a, b):
         ACT(ap("iov", a, b), ap("iof", a, b), AF.Relu, bias=C256)
         TS(ap("iov", a, b), ap("iov", a, b), 256.0, OP.min)
-    TS(full("jw"), ap("iof", 0, 128), 16.0, OP.mult, R16, OP.add)
-    ACT(full("jw4"), full("jw"), bias=float(YB - LOW))
-    ACT(full("jwm"), full("jw"), bias=-float(LOW - YA))
-    ACT(full("ri"), ap("iof", 0, 192), bias=2.0)
+    digits(16, 592)
+    TS(full("jw"), ap("iof", 0, 112), 16.0, OP.mult, R16, OP.add)
+    ACT(full("jt"), ap("jw", 0, 48), bias=float(U0))
+    for a, b in ((0, 112), (224, 288)):
+        IOTA(ap("pbc", a, b), [[0, b - a]], KON, 0)
+    IOTA(full("best"), [[0, 112]], 0, 0)
     MS(full("zero"), 0.0)
-    fills = [(n, a + c, min(a + c + 768, b)) for n, a, b in (("tb", LOW + V0, LOW + KON), ("tb", HIGH + V0, YB), ("ww", V0, 1536), ("dlb", P, 960))
-             for c in range(0, b - a, 768)]
-    DMA("S", "dz", [(lambda n=n, a=a, b=b: T[n][:, a:b], lambda a=a, b=b: T.zero[:, 0:b - a]) for n, a, b in fills],
-        [ap(n, a, b) for n, a, b in fills], [full("zero")])
-    MS(ap("tb", LOW + KON, HIGH), 128.0)
-    MS(ap("exm", 0, V0), -3.0)
-    MS(full("k1"), -71168.0)
-    MS(full("k2"), 24.0)
-    MS(ap("code", 0, 1), -256.0)
-    for h in "01":
-        MS(ap("ow" + h, 85, 128), 4096.0)
-        MS(ap("adj" + h, 85, 128), 0.0)
+    ACT(full("c192"), full("zero"), bias=192.0)
+    MS(ap("cum", 0, 16), 0.0)
+    fills = [("tb", PB, PB + U0), ("tb", PB + U0 + V0, PB + 976), ("tb", PB + HD, PB + HD + U0), ("inf", 0, U0), ("inf", U0 + V0, 1360),
+             ("tb", WB[0], WB[0] + 16), ("dzt", 0, U0)]
+    later = [("tb", PB + HD + U0 + V0, YO[0]), ("yf", 0, 16), ("i1", B0, 1760)]
+    later += [("tb", a, a + 16) for t in (1, 2) for a in (WB[t], YO[t] - 16)]
+    for sem, fl in (("dz", fills), ("dz2", later)):
+        DMA("S", sem, [(lambda n=n, a=a, b=b: T[n][:, a:b], lambda a=a, b=b: T.zero[:, 0:b - a]) for n, a, b in fl],
+            [ap(n, a, b) for n, a, b in fl], [full("zero")])
+    MS(ap("tb", PB + 976, PB + HD), 128.0)
+    for n, a, c in (("sgl", 85, 1), ("sw", 85, 0), ("far", 85, 0), ("swf", 85, 0), ("fa", 85, 0), ("araw", 85, 0), ("r0", 85, 0), ("r1", 85, 0),
+                    ("c1k", 0, 1024), ("unt", 85, 0)):
+        IOTA(ap(n, a, 112), [[0, 112 - a]], c, 0)
+    MS(ap("cp", 0, 1), 0.0)
 
     def late_constants():
-        for n, a, b, c in (("tb", YA, LOW, 128), ("bl", V0, 1536, -1), ("one2", 512, 2048, 1), ("m256", 0, 1552, -256), ("m128", 0, 1744, -128)):
-            for x in range(a, b, 512):
-                IOTA(ap(n, x, min(b, x + 512)), [[0, min(b, x + 512) - x]], c, 0)
-                ops[-1]["r"].append(ap("sent", 0, 1))
-        DMA("G", "gy0", [(lambda: T.tb[:, YA:YA + B0], lambda: T.y0r[:])], [ap("tb", YA, YA + B0)], [full("y0r")], 4000.0)
+        for n, a, b, c in (("c128", 0, 272, 128), ("bl", 0, U0, -1), ("m256", 0, 256, -256),
+                           ("m128", 0, 436, -128), ("k3", 0, 16, -524288), ("c208", 0, 112, 208), ("mone", 0, 192, -1)):
+            IOTA(ap(n, a, b), [[0, b - a]], c, 0, 0)
+        DMA("S", "dy0", [(lambda a=a: T.tb[:, YO[0] + a:YO[0] + a + 272], lambda: T.c128[:]) for a in range(0, B0, 272)],
+            [ap("tb", YO[0], YO[0] + B0)], [full("c128")])
+        DMA("G", "gy0", [(lambda: T.tb[:, YO[0]:YO[0] + B0], lambda: T.y0r[:])], [ap("tb", YO[0], YO[0] + B0)], [full("y0r")], 4000.0)
+        DMA("G", "gwd", [(lambda: T.wd[:], lambda: T.y0r[:, 0:1024])], [full("wd")], [ap("y0r", 0, 1024), ap("sent", 0, 1)], 4000.0)
+        IOTA(ap("iof", 592, 976), [[1, 384]], 592, 0, 0)
+        IOTA(full("nba"), [[1, P]], B0 % 64, 0, 0)
+        ACT(full("ri"), ap("iof", 2, P + 2), scale=1.0 / 256)
+        IOTA(full("half"), [[0, 512]], 1, 0, 0)
+        SEL(full("half"), full("half"), [[0, 32], [-1, 16]], OP.is_ge, 7, 0)
         for r in range(0, 16, 4):
-            SEL(ap("bm", 128 * r, 128 * r + 512), ap("one2", 128 * r, 128 * r + 512), [[-1, 4], [-16, 8], [0, 16]], OP.is_equal, -r, 1)
+            SEL(ap("bm", 128 * r, 128 * r + 512), full("half"), [[-1, 4], [-16, 8], [0, 16]], OP.is_equal, -r, 1)
+        for n, c in (("i256", 256), ("i1k", 1024), ("i2", 2), ("n4k", -4096), ("n64", -64), ("i2k", 2048), ("id1", 800), ("ie1", 800 + HD),
+                     ("id2", 1200), ("ie2", 1200 + HD)):
+            scaled(n, EYE, c)
+        for n, c in (("b64", 64.0), ("nb64", -64.0), ("b32", 32.0), ("nblk", -1.0)):
+            ACT(full(n), blk, scale=c)
+        scaled("nd8", BLK + [([[0, 8], [1, 16]], OP.is_ge, -8, 0)], -4096)
+        SEL(full("tri"), blk, [[1, 128]], OP.is_gt, 0, -1)
+        TT(full("tri"), full("tri"), idn, OP.subtract)
+        for n, c in (("t4", 4096.0), ("nt4", -4096.0), ("t2", 2048.0)):
+            ACT(full(n), full("tri"), scale=c)
+        for n, c in (("ihf", 0.5), ("i63", 63.75), ("e1", oh(1))):
+            TS(full(n), idn, c, OP.mult)
+        for t in (0, 1):
+            ACT(OWB[t], PAR, bias=U0 + V0 + P * t - 2.0)
+        ACT(K12, LT8, scale=-1138944.0)
+        ACT(full("k12"), ones(112), scale=256.0, bias=K12)
+        ACT(DB, LT8, scale=-4096 * 2223.5, bias=4096 * 2223.5)
+        ACT(TMP, oh(0), scale=-float(U0))
+        ACT(VNB, oh(1), scale=float(V0 + 2 * P - B0 % 64), bias=TMP)
+        digits(592, 976)
 
-    def threshold(t, k, with_new):
-        th = float(THETA[t])
-        MM(ps(7, 0, k), [(blk, ap("sgl", 0, k))])
-        ACT(ap("jk", 0, k), ps(7, 0, k), acc=ACC)
-        if with_new:
-            TS(LB, ACC, 0.5, OP.mult, SLC, OP.add)
-            TS(col(12), LB, -15.5, OP.add)
-            TS(col(13), LB, th, OP.add)
-            return
-        TS(Q, ACC, 16.0 * k - 31.0, OP.add, 1.0 / 64, OP.mult)
-        TS(LP, ACC, 0.5, OP.mult, 8.0 * k + th, OP.add)
-        TS(THR, Q, -32.0, OP.mult, LP, OP.add)
+    def lists(t, g, bank):
+        w, o = GW[g], 256 * g
+        a, b = 64 * g, 64 * g + w
+        sg = (i4k, ap("sgl", a, b))
+        MMS([(ps(bank, o, o + w), [(idf, ee(0, a, b)), (full("id%d" % t), ap("mine", a, b)), sg]),
+             (ps(bank, o + w, o + 2 * w), [(idf, ee(0, a, b)), (full("ie%d" % t), ap("mine", a, b)), (idn, ap("far", a, b)), sg]),
+             (ps(bank, o + 2 * w, o + 3 * w), [(idf, ee(0, a, b)), (i4k, ones(w)), (full("i960"), ap("far", a, b))]),
+             (ps(bank, o + 3 * w, o + 4 * w), [(idf, ee(1, a, b)), sg])])
+        TS(ap("gu", o, o + 4 * w), ps(bank, o, o + 4 * w), -4096.0, OP.add)
 
-    def lists(a, b):
-        MMS([(ps(7, 128 * h + a, 128 * h + b), [(idf, ap("e%d" % h, a, b)), (idn, ap("dead", a, b))]) for h in (0, 1)])
-        for h in (0, 1):
-            TS(ap("gu", 128 * h + a, 128 * h + b), ps(7, 128 * h + a, 128 * h + b), float(DUM), OP.min)
-
-    def own_x(c):
-        CP(full("ou"), sm(0, 24))
-        for j in range(6):
-            ACT(ap("xo", 64 * j, 64 * j + 64), ind(ap("xx", 0, c), ap("ou", 4 * j, 4 * j + 4)), scale=-1.0 if j % 2 else 1.0)
-
-    MM(ps(4, 0, 85), wrap("z512", "y0r", 0, 85))
-    ACT(ap("sgl", 0, 85), ps(4, 0, 85), AF.Sign, bias=-512 * 175.5)
-    MM(ps(5, 0, V0), [(blk, ap("xx", 0, V0))])
-    threshold(0, 85, False)
-    ACT(ap("dead", 0, 85), ps(4, 0, 85), AF.Relu, scale=-8.0, bias=8 * 512 * 175.5)
-    for d in range(3):
-        for j in (0, 1):
-            CP(ap("old", 192 + 8 * d + 4 * j, 196 + 8 * d + 4 * j), ap("sndi", 4 * d, 4 * d + 4))
-    CP(full("su"), ap("old", 192, 216))
+    MM(ps(6, 0, V0), [(blk, ap("xx", 0, V0))])
+    MM(ps(7, 0, 85), wrap("z4k", "y0r", 0, 85))
+    ACT(ap("sgl", 0, 85), ps(7, 0, 85), AF.Sign, bias=-4096 * 175.5, acc=ACC)
+    MM(ps(7, 96, 97), [(full("blkh"), ACC)])
+    TS(Q, ps(7, 96, 97), 8.0 * 85 - 15.5, OP.add, 1.0 / 32, OP.mult)
+    TS(LP, ps(7, 96, 97), 8.0 * 85 + THETA[0], OP.add)
+    TS(THR, Q, -32.0, OP.mult, LP, OP.add)
+    CP(ap("old", P, P + 12), full("sndi"))
+    CP(full("su"), full("sndi"))
     TS(full("eo"), ind(full("enb"), full("su")), 384.0, OP.min, -192.0, OP.add)
-    MM(ps(6, 0, 24), wrap("z01", "eo", 0, 24))
-    ACT(sm(0, 24), ps(6, 0, 24))
-    own_x(V0)
+    MM(ps(3, 0, 24), pairs("z01", "eo", 0))
+    TS(full("ou"), ps(3, 0, 24), PAR, OP.add, float(U0), OP.add)
+    TS(full("own"), ps(3, 0, 24), PAR, OP.add, float(U0), OP.add)
     p85 = (0, 85, 1)
     CP(ap("entf", 0, 256, 1, p85), ap("ent", 0, 256, 1, p85))
     for h in (0, 1):
-        TR(ps(0, 128 * h, 128 * h + 85), ap("entf", 128 * h, 128 * h + 128, 1, p85), ap("idf", 0, 85, 1, p85))
+        TR(ps(h, 0, 85), ap("entf", 128 * h, 128 * h + 128, 1, p85), ap("idf", 0, 85, 1, p85))
+    k0 = lambda n: ap(n, 0, 85)
+    TS(k0("sw"), ps(1, 0, 85), float(FAR), OP.is_ge)
+    TT(k0("swf"), ps(1, 0, 85), k0("sw"), OP.mult)
+    TT(k0("araw"), ps(0, 0, 85), k0("swf"), OP.max)
     for h in (0, 1):
-        e, raw, s1, s2 = ps(0, 128 * h, 128 * h + 85), ap("b%d" % h, 0, 85), ap("nm", 192 * h, 192 * h + 85), ap("nm", 192 * h + 96, 192 * h + 181)
-        ACT(raw, e)
-        ACT(s1, e, AF.Sign, bias=-(FAR + 63.5))
-        ACT(s2, e, AF.Sign, bias=-(FAR + 127.5))
-        ACT(ap("ow%d" % h, 0, 85), e, AF.Relu, scale=-4096.0, bias=4096 * (FAR - 0.5))
-        far = [(full("i32"), s1), (full("i32"), s2)]
-        MMS([(ps(1 + h, 0, 85), [(idf, raw)] + far), (ps(1 + h, 128, 213), far)])
-        ACT(ap("e%d" % h, 0, 85), ps(1 + h, 0, 85), bias=64.0)
-        ACT(ap("adj%d" % h, 0, 85), ps(1 + h, 128, 213), bias=64.0)
-    lists(0, 85)
-    for a in range(0, B0, 512):
-        TS(ap("rr", a, min(B0, a + 512)), ap("y0r", a, min(B0, a + 512)), 2.0, OP.mult)
-    CP(ap("bl", 0, V0), full("bli"))
-    for a in (0, 512):
-        TS(ap("fl", a, a + 512), ap("y0r", a, a + 512), 0.125, OP.mult, 128.5625, OP.add)
-        TS(ap("t8", a, a + 512), ap("fl", a, a + 512), -8.0, OP.mult, 1032.0, OP.add)
+        ACT(k0("r%d" % h), ps(h, 0, 85))
+    TS(k0("far"), k0("araw"), float(FAR), OP.is_ge)
+    TT(k0("fa"), k0("araw"), k0("far"), OP.mult)
+    ACT(full("mine"), full("far"), scale=-1.0, bias=1.0)
+    MS(ap("kk", 0, 112), 1.0 / HD)
+    TS(ap("kk", 112, 224), full("mine"), 1.0 / HD, OP.mult)
+    MMS([(ps(0, 0, 112), [(idf, full("araw")), (idf, full("fa")), (full("n2112"), full("far"))]),
+         (ps(0, 112, 224), [(idf, full("r0")), (idf, full("r1")), (full("nidf"), full("araw"))])])
+    ACT(full("ee"), ps(0, 0, 224), bias=float(U0))
+    for g in (0, 1):
+        lists(0, g, (1, 5)[g])
+    TT(k0("fa"), k0("fa"), k0("swf"), OP.subtract)
+    TT(full("tj"), full("far"), full("sw"), OP.subtract)
+    TT(full("th"), full("tj"), full("sw"), OP.subtract)
+    ACT(full("tj"), full("th"), scale=2048.0, bias=3072.0)
+    ACT(full("th"), full("th"), scale=2048.0, bias=2048.0)
+    CP(ap("bl", U0, U0 + V0), full("bli"))
+    TS(full("fl"), ap("y0r", 0, 1024), 0.125, OP.mult, 128.5625, OP.add)
+    TS(full("wd"), full("fl"), -8.0, OP.mult, 1029.0, OP.add)
 
     for t in range(RO):
-        M, C, dl, last = B0 + P * t, V0 + P * t, float(DELTA[t]), t == RO - 1
-        K, KC = M // 16, C // 16
+        M, C, last = B0 + P * t, V0 + P * t, t == RO - 1
+        K, KC, UC = M // 16, C // 16, U0 + C
         S = K + 1
-        yc, yn = (YA, YB) if t % 2 == 0 else (YB, YA)
-        sb, ld = "sb%d" % t, "ld%d" % t
-        wl, wh, wwin = ap("tb", LOW, LOW + KON), ap("tb", HIGH, HIGH + KON), full("ww")
+        sb, F = "sb%d" % t, WB[t] + 16
+        yn, yo = ("yf", 16) if last else ("tb", YO[t + 1])
+        pt = lambda a, b: ap("tb", PB + a, PB + b)
+        idl, nidl = (full("idl0"), full("nidl0")) if t == 0 else (full("idl"), full("nidl"))
+        GK = [(0, 64), (64, K)]
+        wl, wh, wn, wi = pt(0, UC), pt(HD, HD + UC), ap("tb", WB[t], PB + HD + UC), ap("inf", 0, UC)
+        gu = lambda j, g, a, b: ap("gu", 256 * g + GW[g] * j + a - 64 * g, 256 * g + GW[g] * j + b - 64 * g)
+        cut = lambda a, b: [(c, min(b, c + 32)) for c in range(a, b, 32)]
+        cells = [(a, min(C, a + 512)) for a in range(0, C, 512)]
         k = lambda n, a=0: ap(n, a, a + K)
-        w16 = lambda n, a, b, o=0: ap(n, o + 16 * a, o + 16 * b)
-        TS(ap("nc", 0, C), ps(5, 0, C), THR, OP.is_ge, -1.0, OP.mult)
-        o, x, z = ap("rem", 0, C), ap("nc", 0, C), ap("zero", 0, C)
-        add("V", lambda g, o=o, x=x, z=z: g.vector.tensor_tensor_scan(real(o), real(x), real(z), 193.0, OP.add, OP.max),
+        for bank in (2, 4):
+            MMS([(ps(bank, a, b), [(idn, ap("xx", a, b))]) for a, b in cells], done=False)
+        if t == 0:
+            TS(ap("nc", 0, C), ps(6, 0, C), THR, OP.is_ge)
+        else:
+            TS(ap("nc", 0, C), ps(6, 0, C), NB, OP.add, THR, OP.is_ge)
+        o, x, z = ap("cum", 16, 16 + C), ap("nc", 0, C), ap("c192", 0, C)
+        add("V", lambda g, o=o, x=x, z=z: g.vector.tensor_tensor_scan(real(o), real(x), real(z), 0.0, OP.add, OP.min),
             [o], [x, z], vcost(o, [x, z]))
-        TT(ap("ww", 0, C), ap("rem", 0, C), ap("nc", 0, C), OP.mult)
-        TS(ap("dd", 0, C), ap("ww", 0, C), 16.0, OP.mult, -dl, OP.max)
-        TT(full(sb), ind(ap("dd", 0, C), full("ou")), full("xo"), OP.add)
+        now, was = (lambda a, b: ap("cum", 16 + a, 16 + b)), (lambda a, b: ap("cum", 15 + a, 15 + b))
+        MMS([(ps(2, a, b), [(idl, now(a, b)), (nidl, was(a, b))]) for a, b in cells], fresh=False)
+        MMS([(ps(4, a, b), [(nidl, now(a, b)), (idl, was(a, b))]) for a, b in cells], fresh=False)
+        ACT(pt(U0, UC), ps(4, 0, C), AF.Relu)
+        TS(pt(HD + U0, HD + UC), ps(2, 0, C), 63.0, OP.min)
+        ACT(full(sb), ind(pt(0, HD + UC), full("ou")))
         add("G", lambda g, t=t: send(g, t), [ap("sent", t, t + 1)], [full(sb)], 300.0, 0.0, "none")
-        add("X", None, [full(ld)], [ap("sent", t, t + 1)], 0.0, 4200.0 if t == 0 else 2700.0, "arr%d" % t, 0)
+        add("X", None, [ap("tb", F, F + 384)], [ap("sent", t, t + 1)], 0.0, 4200.0 if t == 0 else 3000.0, "arr%d" % t, 0)
         if t == 0:
             late_constants()
-        for a in range(0, C, 512):
-            b = min(C, a + 512)
-            pl = ps(0, 0, b) if a == 0 else ps(6, 256, 256 + b - a)
-            MM(ps(5, a, b), [(idn, ap("xx", a, b)), (nidn, ap("dd", a, b))])
-            TS(ap("tb", HIGH + a, HIGH + b), ps(5, a, b), 63.0, OP.min)
-            MM(pl, [(idn, ap("xx", a, b)), (idn, ap("dd", a, b))])
-            ACT(ap("tb", LOW + a, LOW + b), pl, AF.Relu)
-        MM(ps(4, 0, KC), wrap("z16", "ww", 0, KC))
-        TS(sm(32, KC), ps(4, 0, KC), 0.0, OP.is_ge)
-        TT(sm(80, KC), sm(32, KC), ap("jw", 0, KC), OP.mult)
-        TT(sm(32, KC), ps(4, 0, KC), sm(80, KC), OP.add)
-        TS(ap("tg", 0, KC), sm(32, KC), 192.0, OP.add)
-        DMA("S", "dd%d" % t, [(lambda: T.dlb[:, 0:P], lambda: T.iov[:, 768:960])], [ap("dlb", 0, P)], [ap("iov", 768, 960)])
+        for g, (a, b) in enumerate(GK):
+            TT(w16("nw", a, b), ind(wl, gu(3, g, a, b)), w16("rr", a, b), OP.subtract)
+        TT(ap("dzt", U0, UC), pt(HD + U0, HD + UC), pt(U0, UC), OP.subtract)
+        for g, (a, b) in enumerate(GK):
+            (CP if (2, g) in ONV else ACT)(w16("zt", a, b), ind(ap("dzt", 0, UC), gu(3, g, a, b)))
+        MMS([(ps(6, a, b), [(full("e0a"), now(a, b)), (full("e0b"), was(a, b))]) for a, b in cells])
+        ACT(ap("inf", U0, UC), ps(6, 0, C), AF.Relu, bias=BASE)
+        MM(ps(4, 256, 448), [(full("ne01"), ap("tb", F, F + 384, 2)), (full("e01"), ap("tb", F + 1, F + 384, 2))])
+        ACT(ap("inf", 976, 1360, 2), ps(4, 256, 448))
+        MM(ps(7, 256, 256 + KC), wrap("zc", "inf", U0, KC))
+        TT(sm(0, KC), ps(7, 256, 256 + KC), ap("jt", 0, KC), OP.min)
+        TS(ap("tg", 0, KC), sm(0, KC), -16.0, OP.add)
+        DMA("S", "dd%d" % t, [(lambda: T.dlb[:, 0:P], lambda: T.iov[:, 16:16 + P])] +
+            ([(lambda: T.dlb[:, P:960], lambda: T.zero[:, 0:768])] if t == 0 else []), [full("dlb")], [ap("iov", 16, 16 + P), full("zero")])
         for a in range(0, KC, 12):
-            CP(ind(ap("dlb", 0, P + C), ap("tg", a, a + 12)), ap("iov", 16 * a, 16 * a + 192))
-        TS(ap("tb", HIGH + FAR, HIGH + FAR + 320), ap(ld, 64, 384), -1.0, OP.mult, 63.0, OP.min)
-        TS(ap("tb", LOW + FAR, LOW + FAR + 320), ap(ld, 0, 320), 0.0, OP.max)
-        MM(ps(6, 0, 320), [(idn, ap(ld, 0, 320)), (idn, ap(ld, 64, 384))])
-        ACT(full("wf"), ps(6, 0, 320))
-        cuts = [(c, min(K, c + 32)) for c in range(0, K, 32)]
-        halves = [(0, 32), (32, 64), (64, K)]
-        gu = lambda h, a, b: ap("gu", 128 * h + a, 128 * h + b)
-        for a, b in halves:
-            TT(w16("nh", a, b), ind(wh, gu(0, a, b)), w16("rr", a, b), OP.subtract)
-            ACT(w16("zh", a, b), ind(wh, gu(1, a, b)))
-        for a, b in halves:
-            TT(w16("nl", a, b), ind(wl, gu(0, a, b)), w16("rr", a, b), OP.subtract)
-        nb = 0
-        for n, o in (("nh", "ahh"), ("nl", "alh")):
-            for a, b in cuts:
-                d = ps((0, 1, 7)[nb % 3], 0, 16 * (b - a)); nb += 1
-                MM(d, [(idn, w16(n, a, b)), (idn, w16("zh", a, b))])
-                ACT(w16(o, a, b), d, AF.Abs)
-        for n, d, o in (("nh", "dhl", "ahl"), ("nl", "dll", "all")):
-            for a, b in halves:
-                TT(w16(d, a, b), ind(wl, gu(1, a, b)), w16(n, a, b), OP.add)
-                ACT(w16(o, a, b), w16(d, a, b), AF.Abs)
-        ones = ap("one2", 0, K)
-        IOTA(k("kc"), [[0, K]], C + 192, 0)
-        info = [ps(4, 128 + 128 * h, 128 + 128 * h + K) for h in (0, 1)]
-        for h in (0, 1):
-            for a, b in halves:
-                (CP if (h, a) in ONV else ACT)(w16("i%d" % h, a, b), ind(wwin, gu(h, a, b)))
-        for d in (1, 2, 3):
-            CP(ind(ap("i%d" % (1 if q + d < 4 else 0), 0, M), ap("su", 8 * d - 8, 8 * d - 4)), ap("wf", 128 * d - 128, 128 * d - 64))
-        for h in (0, 1):
-            MM(info[h], [(idn, k("kc")), (idn, k("dead"))] + wrap("z16", "i%d" % h, 0, K))
-        MM(ps(3, K, 2 * K), [(i4k, ones)] + wrap("z8k", "ahh", 0, K))
-        MM(ps(3, 0, K), wrap("z8k", "alh", 0, K))
-        MM(ps(2, K, 2 * K), [(i4k, ones)] + wrap("z8k", "ahl", 0, K))
-        for a, b in ((0, 64), (64, K)):
-            MM(ps(2, a, b), wrap("z8k", "all", 16 * a, b - a))
-        MM(ps(6, 480, 492), wrap("z1", "dlb", 0, 12))
-        CP(full("dlu"), ps(6, 480, 492))
+            CP(ind(ap("dlb", 0, P + C), ap("tg", a, a + 12)), ap("iov", U0 + 16 * a, U0 + 16 * a + 192))
+        MM(ps(7, 320, 332), wrap("z1", "dlb", 0, 12))
+        CP(full("dlu"), ps(7, 320, 332))
         if not last:
-            TS(sm(128, 12), ps(6, 480, 492), 0.0625, OP.mult)
-        ACT(ap("old", 0, P), ind(full("bl"), full("dlu")))
-        ACT(full("hib"), full("old"), scale=0.0625, bias=128.53125)
-        for n, c in (("sf", S), ("ms", -16 * S)):
-            IOTA(full(n), [[0, 128]], c, 0)
-            SEL(full(n), full(n), [[-1, 128]], OP.is_equal, 0, 1)
-        MM(ps(6, 256, 472), [(full("sf"), full("old")), (full("ms"), full("hib")), (idn, full("hib"))])
-        TS(full("ox"), ps(6, 256, 472), 1.0 + 129 * (16 * S - 1), OP.add)
-        IOTA(full("nba"), [[1, P]], (M + 1) % 64, 0)
-        IOTA(full("nbb"), [[0, P]], (M + 1) // 64 * 64 - 8192, 0)
+            ACT(sm(64, 12), ps(7, 320, 332))
+            ACT(sm(80, 12), ap("jw", 0, 12), bias=float(UC))
+        ACT(ap("old", 0, P), ind(ap("bl", 0, UC), full("dlu")))
+        W = P if last else P + 12
+        ACT(ap("hib", 0, W), ap("old", 0, W), scale=0.0625, bias=128.53125)
+        scaled("sf", EYE, S, t)
+        scaled("ms", EYE, -16 * S, t)
+        MM(ps(6, 256, 256 + W), [(full("sf"), ap("old", 0, W)), (full("ms"), ap("hib", 0, W)), (idn, ap("hib", 0, W))])
+        TS(ap("ox", 0, W), ps(6, 256, 256 + W), 1.0 + 129 * (16 * S - 1), OP.add)
+        IOTA(full("nbb"), [[0, P]], M // 64 * 64 - 4096, 0, t)
         ACT(full("hg"), ind(wh, full("dlu")))
-        TT(full("nyc"), ind(wl, full("dlu")), full("hg"), OP.subtract)
-        TS(full("ex"), full("nyc"), 0.0, OP.is_lt)
+        ACT(full("lg"), ind(wl, full("dlu")))
+        nex, gap = ap("nex", P * t, P * t + P), [(idn, full("hg")), (nidn, full("lg"))]
+        MMS([(ps(7, 0, P), gap)] + ([] if last else [(ps(7, P, 2 * P), [(blk, full("hg")), (full("nblk"), full("lg"))])]))
+        ACT(nex, ps(7, 0, P), AF.Relu, scale=-1.0, bias=1.0)
+        TS(full("nx5"), nex, 1024.0, OP.mult, 512.0, OP.add)
         if last:
-            DMA("S", "dout", [(lambda: T.yx[:, 0:768], lambda: T.tb[:, LOW:LOW + 768]), (lambda: T.yx[:, 768:960], lambda: T.hg[:])],
-                [], [ap("tb", LOW, LOW + 768), full("hg")])
-            TS(full("ncst"), ap("iof", 0, P), float(C), OP.add, col(10), OP.mult)
-            MM(ps(6, 0, P), [(ap("z1", 15, 143), ap("dlb", 0, P))])
-            TT(full("vn"), ps(6, 0, P), full("ncst"), OP.add)
+            DMA("S", "dout", [(lambda: T.yx[:, 0:768], lambda: T.tb[:, PB + U0:PB + U0 + 768]), (lambda: T.yx[:, 768:960], lambda: T.hg[:])],
+                [], [pt(U0, U0 + 768), full("hg")])
         else:
-            MM(ps(6, 0, P), [(blk, full("nyc"))])
-            ACT(full("lc"), ps(6, 0, P), AF.Sign, scale=-1.0, bias=-175.5, acc=col(11))
-            TS(SLC, col(11), 0.5, OP.mult, 8.0 * K + 96, OP.add)
-            ACT(ap("exm", C, C + P), full("ex"), scale=64.0, bias=-67.0)
+            scaled("idl", EYE, DELTA[t + 1], t)
+            scaled("nidl", EYE, -DELTA[t + 1], t)
+            ACT(full("lc"), ps(7, P, 2 * P), AF.Sign, bias=-175.5, acc=ALC)
+            ACT(SLC, ALC, scale=0.5, bias=8.0 * K + 96 - 15.5)
             C2, sh = C + P, 331 * t
-            marks = sorted(set([0, 512, C, C2] + ([1024 - sh] if 1024 - sh < C2 else [])))
+            marks = sorted(set([0, V0, 512, C, C2] + ([1024 - sh] if 1024 - sh < C2 else [])))
             for a, b in zip(marks[:-1], marks[1:]):
-                src = ap("tb", LOW + a, LOW + b) if a < C else ap("hg", a - C, b - C)
+                src = pt(U0 + a, U0 + b) if a < C else ap("hg", a - C, b - C)
                 y = (a + sh) & 1023
-                MM(ps(5, a, b), [(idn, src), (idn, ap("y0r", y, y + b - a)), (idn, ap("t8", y, y + b - a)), (idn, ap("exm", a, b))])
-            TS(ap("xx", 0, C2), ps(5, 0, C2), 0.0, OP.max, 63.0, OP.min)
-            for a in range(0, C2, 512):
-                b = min(C2, a + 512)
-                MM(ps(5, a, b), [(blk, ap("xx", a, b))])
-        ACT(k("wi1"), info[1])
-        TT(k("t0"), info[0], k("wi1"), OP.min)
-        TS(k("unt"), k("t0"), C + 192.0, OP.is_ge, 6144.0, OP.mult)
+                MM(ps(6, a, b), [(idn, src), (idn, ap("wd", y, y + b - a))] + ([(full("n64"), ap("nex", a - V0, b - V0))] if a >= V0 else []))
+            TS(ap("xx", 0, C2), ps(6, 0, C2), 0.0, OP.max, 63.0, OP.min)
+            MMS([(ps(6, a, min(C2, a + 512)), [(blk, ap("xx", a, min(C2, a + 512)))]) for a in (0, 512)])
+        nb = [0]
+        for h in (1, 0):
+            for g, (a, b) in enumerate(GK):
+                (CP if (h, g) in ONV else ACT)(w16("i%d" % h, a, b), ind(wi if h else full("inf"), gu(2 + h, g, a, b)))
+
+        def sums(g):
+            a, b = GK[g]
+            for h in (0, 1):
+                TT(w16("d%d" % h, a, b), ind(wn, gu(h, g, a, b)), w16("nw", a, b), OP.add)
+                if (h, g) in RELU:
+                    TS(w16("ab%d" % h, a, b), w16("d%d" % h, a, b), 0.0, OP.max)
+                else:
+                    ACT(w16("ab%d" % h, a, b), w16("d%d" % h, a, b), AF.Abs)
+            for h in (0, 1):
+                for c, d in cut(a, b):
+                    pp = ps(nb[0] % 2, 0, 16 * (d - c)); nb[0] += 1
+                    MM(pp, [(idn, w16("zt", c, d)), (idn, w16("d%d" % h, c, d))])
+                    ACT(w16("ab%d" % (2 + h), c, d), pp, AF.Abs)
+
+        def before(parts):
+            MM(ps(4, 0, S), wrap("zi", "i1", 0, S))
+            MM(ps(4, S, S + K), wrap("zi", "i0", 0, K))
+            ACT(ap("iv", 0, S + K), ps(4, 0, S + K))
+            scaled("ic", EYE, C + P, t)
+            MMS([(ps(4, 0, S), [(idn, ap("iv", 0, S)), (full("ic"), ap("kk", 0, S))]), (ps(4, S, S + K), [(idn, k("iv", S)), (full("ic"), k("kk", 112))])])
+            MM(ps(5, 256, 256 + K), [(full("i1k"), k("iv")), (full("i1k"), k("iv", S)), (full("i256"), k("sgl"))])
+            ACT(k("unt"), ps(5, 256, 256 + K), AF.Relu, scale=-2.0 ** 23, bias=8192.0 + 2.0 ** 23 * 256)
+            for a, b, o in parts:
+                w, z = b - a, (288 if a else 112)
+                we = w + w % 2
+                ACT(ap("pbc", z, z + w), ap("jw", a, b), bias=float(YO[t] - WB[t]))
+                MMS([(ps(5, o, o + we), [(idf, ee(1, a, a + we)), (idn, ap("unt", a, a + we))]),
+                     (ps(5, o + we, o + we + w), [(idf, ee(0, a, b)), (full("id%d" % t), ap("mine", a, b)), (idn, ap("unt", a, b))])])
+                pb = ps(5, o, o + we + w)
+                TT(pb, pb, ap("pbc", z - we, z + w), OP.min)
+
+        def choice(g, o):
+            a, b = GK[g]
+            w = b - a
+            we = w + w % 2
+            two_far = (full("i2"), ap("far", a, b))
+            some = lambda h: ((wrap("zn8", "d%d" % h, 16 * a, w) + wrap("z16k", "ab%d" % h, 16 * a, w)) if (h, g) in RELU
+                              else wrap("z8k", "ab%d" % h, 16 * a, w))
+            MM(ps(2, 0, w), some(0))
+            MM(ps(3, 0, w), [(idn, ap("th", a, b)), two_far] + some(1))
+            MM(ps(2, w, 2 * w), [(idn, ap("c1k", a, b))] + wrap("z8k", "ab2", 16 * a, w))
+            MM(ps(3, w, 2 * w), [(idn, ap("tj", a, b)), two_far] + wrap("z8k", "ab3", 16 * a, w))
+            two = lambda n: ap(n, o, o + we + w)
+            ACT(ap("c1", 0, 2 * w), ps(2, 0, 2 * w))
+            TT(ap("mm", 0, 2 * w), ps(3, 0, 2 * w), ap("c1", 0, 2 * w), OP.min)
+            TT(ap("best", a, b), ap("mm", 0, w), ap("mm", w, 2 * w), OP.min)
+            TS(ap("ab", o, o + we), ap("best", a, a + we), HD, OP.bitwise_and)
+            TS(ap("ab", o + we, o + we + w), ap("best", a, b), 1, OP.logical_shift_right, HD + 1, OP.bitwise_and)
+            TT(two("t45"), ps(5, o, o + we + w), two("ab"), OP.add)
+            CP(two("ix"), two("t45"))
+            TT(ap("t01", a, b), ps(4, a, b), ap("ab", o, o + w), OP.mult)
+            TT(ap("t01", S + a, S + b), ps(4, S + a, S + b), ap("ab", o + we, o + we + w), OP.mult)
+
+        def new_y(parts, g, o):
+            a, b = GK[g]
+            we = b - a + (b - a) % 2
+            for c, d in parts:
+                pre = ps(nb[0] % 2, 0, 16 * (d - c)); nb[0] += 1
+                MM(pre, [(full("ihf"), w16("tb", c, d, YO[t])), (full("i63"), ones(16 * (d - c)))])
+                ACT(w16("az", c, d), ind(ap("tb", WB[t], YO[t] + M), ap("ix", o + we + c - a, o + we + d - a)))
+                TT(w16("dz", c, d), ind(pt(0, HD + UC), ap("ix", o + c - a, o + d - a)), w16("az", c, d), OP.subtract)
+                ACT(w16("gz", c, d), w16("dz", c, d), AF.Abs, scale=0.5)
+                TT(w16(yn, c, d, yo), pre, w16("gz", c, d), OP.add)
+
+        def doubled(g):
+            x, y = 16 * GK[g][0], 16 * GK[g][1]
+            DMA("S", "dr%d%d" % (t, g), [(lambda u=u: T.rr[:, u:min(y, u + 256)], lambda u=u: T.m256[:, 0:min(y, u + 256) - u]) for u in range(x, y, 256)],
+                [ap("rr", x, y)], [full("m256")], 3000.0)
+            for n in ("ga", "gb"):
+                DMA("G", "%s%d%d" % (n, t, g), [(lambda: T.rr[:, x:y], lambda yo=yo: T.tb[:, yo + x:yo + y])], [ap("rr", x, y)],
+                    [ap(yn, yo + x, yo + y)], 3500.0)
+
+        sums(0); before([(0, 64, 0), (64, K, 128)]); sums(1); choice(0, 0); choice(1, 128)
+        new_y([(0, 32), (32, 64)], 0, 0); new_y([(64, 88), (88, K)] if K > 96 else [(64, K)], 1, 128)
+        MM(ps(5, 256, 256 + K), [(idf, k("t01")), (idf, k("t01", S))])
+        TS(k("cp", 1), ps(5, 256, 256 + K), 2.0 - UC, OP.add, 1.0, OP.max)
         for h in (0, 1):
-            TT(info[h], info[h], k("ow%d" % h), OP.min)
-        pb = [ps(7, 128 * h, 128 * h + K) for h in (0, 1)]
-        MM(pb[0], [(idf, k("e0")), (idn, k("unt"))])
-        MM(pb[1], [(idf, k("e1")), (idn if t % 2 else nidn, k("unt"))])
-        TS(pb[0], pb[0], float(KON), OP.min)
-        if t % 2 == 0:
-            TT(pb[1], pb[1], k("jwm"), OP.max)
-            wz, off = ap("tb", YA, YB), float(LOW - YA)
-        else:
-            TT(pb[1], pb[1], k("jw4"), OP.min)
-            wz, off = ap("tb", LOW, YB + M), 0.0
-        ACT(ap("c1", 0, 2 * K), ps(3, 0, 2 * K), bias=2048.0)
-        TT(ap("mm", 0, 2 * K), ps(2, 0, 2 * K), ap("c1", 0, 2 * K), OP.min)
-        TT(k("best"), k("mm"), k("mm", K), OP.min)
-        TS(k("ab"), k("best"), 1, OP.logical_shift_right, 2048, OP.bitwise_and)
-        TT(k("t4"), pb[0], k("ab"), OP.add)
-        CP(k("ix"), k("t4"))
-        TS(k("ab", 112), k("best"), 2048, OP.bitwise_and)
-        TT(k("t5"), pb[1], k("ab", 112), OP.add)
-        TS(k("ix", 128), k("t5"), off, OP.add)
-        for i, (a, b) in enumerate([(0, 16), (16, 48), (48, 80), (80, K)]):
-            pre = ps((0, 1, 3, 2)[i], 0, 16 * (b - a))
-            MM(pre, [(full("ihf"), w16("tb", a, b, yc)), (full("i63"), ap("one2", 0, 16 * (b - a)))])
-            ACT(w16("zh", a, b), ind(ap("tb", LOW, YB), ap("ix", a, b)))
-            TT(w16("dll", a, b), ind(wz, ap("ix", 128 + a, 128 + b)), w16("zh", a, b), OP.subtract)
-            ACT(w16("dhl", a, b), w16("dll", a, b), AF.Abs, scale=0.5)
-            TT(w16("tb", a, b, yn), pre, w16("dhl", a, b), OP.add)
-        TT(k("t0"), info[0], k("ab"), OP.min)
-        TT(info[1], info[1], k("ab", 112), OP.min)
-        TT(k("t1"), info[1], k("t0"), OP.add)
-        ACT(k("t2"), k("t1"), AF.Relu, bias=1.0 - C)
-        TS(k("cp"), k("t2"), 200.0, OP.min, 1.0, OP.add)
-        TT(k("e0"), k("e0"), k("t0"), OP.max)
-        TT(k("e1"), info[1], k("e1"), OP.max)
+            TT(ee(h, 0, K), ee(h, 0, K), k("t01", S * (1 - h)), OP.max)
         if last:
             pk = (0, K, 1)
+            MMS([(ps(6, 0, K), [(idf, ee(1, 0, K)), (i4k, k("sw")), (n4k, ones(K)), (nidn, k("c208"))]),
+                 (ps(6, 128, 128 + K), [(idf, ee(0, 0, K)), (n4k, k("far")), (nidn, k("c208"))]),
+                 (ps(6, 256, 256 + K), [(idf, ee(1, 0, K)), (nidn, k("c208"))])])
+            TT(k("araw"), ps(6, 0, K), k("fa"), OP.max)
+            TT(k("r0"), ps(6, 128, 128 + K), k("araw"), OP.max)
+            TT(k("r1"), ps(6, 256, 256 + K), k("swf"), OP.max)
             for h in (0, 1):
-                TT(k("b%d" % h), k("e%d" % h), k("adj%d" % h), OP.subtract)
-                TR(ps(5, 128 * h, 128 * h + 128, pk), k("b%d" % h), idf)
-            ACT(ap("et", 0, 256, 1, pk), ps(5, 0, 256, pk))
+                TR(ps(7, 128 * h, 128 * h + 128, pk), k("r%d" % h), idf)
+            ACT(ap("et", 0, 256, 1, pk), ps(7, 0, 256, pk))
             DMA("S", "dout", [(lambda r=r: T.ye[r, 0:1744], lambda r=r: T.et[0:109, ecol(r):ecol(r) + 16]) for r in range(16)], [], [full("et")])
-        for a, b in ((0, 48), (48, K)):
-            MM(ps(4, a, b), [(blk, ap("k1", a, b)), (blk, ap("k2", a, b))] + wrap("z512", "tb", yn + 16 * a, b - a))
-        TT(k("code", 1), ps(4, 0, K), k("cp"), OP.min)
-        if last:
-            DMA("S", "dyy", [(lambda: T.yy[:, 0:1744], lambda: T.m128[:])], [ap("yy", 0, 1)], [full("m128")], 3000.0)
-            DMA("G", "gyy", [(lambda: T.yy[:, 0:1744], lambda yn=yn: T.tb[:, yn:yn + 1744])], [ap("yy", 0, 1)], [ap("tb", yn, yn + M)], 4000.0)
-        else:
-            ACT(k("dead"), ps(4, 0, K), AF.Relu, scale=-16.0)
-            DMA("S", "dr%d" % t, [(lambda M=M: T.rr[:, 0:M], lambda M=M: T.m256[:, 0:M])], [ap("rr", 0, M)], [ap("m256", 0, M)], 3000.0)
-            for n in ("ga", "gb"):
-                DMA("G", n + str(t), [(lambda M=M: T.rr[:, 0:M], lambda M=M, yn=yn: T.tb[:, yn:yn + M])], [ap("rr", 0, M)], [ap("tb", yn, yn + M)], 4000.0)
-            ACT(k("sgl"), k("code", 1), AF.Sign)
-            lists(0, K)
-            threshold(t + 1, K, True)
+            DMA("S", "dyy", [(lambda a=a: T.yy[:, a:a + 436], lambda: T.m128[:]) for a in range(0, 1744, 436)], [ap("yy", 0, 1)], [full("m128")], 3000.0)
+            DMA("G", "gyy", [(lambda: T.yy[:, 0:1744], lambda: T.yf[:, 16:1760])], [ap("yy", 0, 1)], [full("yf")], 4000.0)
         for j in range(4):
-            MMS([(ps(j, (r % 4) * S, (r % 4 + 1) * S), [(ap("bm", 128 * r, 128 * r + 128), ap("code", 0, S))]) for r in range(4 * j, 4 * j + 4)])
+            MMS([(ps(j, (r % 4) * S, (r % 4 + 1) * S), [(ap("bm", 128 * r, 128 * r + 128), ap("cp", 0, S)),
+                                                         (full("nd8"), ap(yn, yo - 16 + r, yo + M, 16))]) for r in range(4 * j, 4 * j + 4)])
             if j % 2:
-                TS(ap("st", 4 * S * j, 4 * S * (j + 1)), ps(j, 0, 4 * S), 0.0, OP.max)
+                TS(ap("st", 4 * S * j, 4 * S * (j + 1)), ps(j, 0, 4 * S), DB, OP.add, 0.0, OP.max)
             else:
-                ACT(ap("st", 4 * S * j, 4 * S * (j + 1)), ps(j, 0, 4 * S), AF.Relu)
-        stw, W = ap("st", 0, 16 * S), (192 if last else 216)
-        H = W // 4
-        for j in (0, 2, 1, 3):
-            (CP if j >= 2 else ACT)(w16("sg", H * j, H * (j + 1)), ind(stw, ap("ox", H * j, H * (j + 1))))
-        for j in (0, 2, 1, 3):
-            MM(ps(4, H * j, H * (j + 1)), wrap("z16", "sg", 16 * H * j, H))
-        cd = ps(4, 0, P)
-        e1b, e2b, kb = full("e1b"), full("e2b"), full("kb")
-        TT(e1b, cd, full("ri"), OP.is_equal)
-        TS(e2b, cd, 200.0, OP.is_ge)
-        ACT(kb, cd, AF.Sign)
+                ACT(ap("st", 4 * S * j, 4 * S * (j + 1)), ps(j, 0, 4 * S), AF.Relu, bias=DB)
         if not last:
-            MM(ps(0, P, 2 * P), [(blk, full("lc")), (blk, e1b), (blk, e2b)])
-            MM(ps(0, 0, P), [(blk, full("lc")), (nblk, e1b), (nblk, e2b), (blk, kb)])
-            ACT(full("jk"), ps(0, 0, 2 * P), AF.Relu, bias=-31.0, acc=NB)
-            TS(Q, NB, col(12), OP.subtract, -1.0 / 32, OP.mult)
-            TS(LP, NB, -1.0, OP.mult, col(13), OP.add)
-            TS(THR, Q, -32.0, OP.mult, LP, OP.add)
-            TS(sm(160, 24), ps(4, P, W), 2.0, OP.is_ge)
-            TS(sm(184, 24), ps(4, P, W), C - 2.0, OP.add)
-            TT(sm(208, 24), sm(160, 24), sm(184, 24), OP.mult)
-            TT(sm(0, 24), sm(0, 24), sm(208, 24), OP.max)
-            own_x(C + P)
-        for bank, pos, neg, first in ((1, blk, nblk, []), (2, full("tri"), full("ntri"), []), (3, i4k, n4k, [(idf, ap("old", 0, P))])):
-            MM(ps(bank, P, 2 * P), first + [(pos, e1b), (pos, e2b)])
-            MM(ps(bank, 0, P), first + [(neg, e1b), (neg, e2b), (pos, kb)])
-        ACT(full("nm"), ps(1, 0, 2 * P), AF.Relu, bias=-15.0)
-        ACT(full("ff"), ps(2, 0, 2 * P), AF.Relu, bias=col(14))
-        ACT(full("r1"), ps(3, 0, 2 * P), AF.Relu, bias=1.0 - 4096)
-        made = lambda pos, neg: [(pos, full("ex")), (neg, ap("nm", 0, P)), (neg, ap("nm", P, 2 * P))]
-        for h in (0, 1):
-            MM(ps(2, P * h, P * h + P), [(idn, full("nba")), (idn, full("nbb"))] + made(i4k, n4k) + [(i4k, ap("ff", P * h, P * h + P))])
-        TT(full("tv"), ps(2, 0, 2 * P), full("r1"), OP.max)
-        TS(ind(full("bl"), full("dlu")), ap("tv", 0, P), 1.0, OP.mult, -1.0, OP.add)
-        ACT(full("tn") if last else ap("bl", C, C + P), ap("tv", P, 2 * P), bias=-1.0)
-        MM(ps(1, 0, P), made(idn, nidn))
-        MM(ps(1, P, 2 * P), made(i4k, n4k) + [(nidn, full("nyc"))])
-        ym = ap("my", P, 2 * P)
-        ACT(ym, ps(1, P, 2 * P), AF.Relu, bias=-4096.0)
+            doubled(0); doubled(1)
+            lv = ps(4, 384, 384 + K)
+            MM(lv, [(blk, k("k12"))] + wrap("z4k", yn, yo, K))
+            ACT(k("sgl"), lv, AF.Sign, acc=ACC)
+            lists(t + 1, 0, 5)
+            MM(ps(5, 500, 501), [(full("blkh"), ACC)])
+            ACT(TM2, ps(5, 500, 501), bias=SLC)
+        stw = ap("st", 0, 16 * S)
+        hs = [0, HS, 2 * HS, (2 * HS + W) // 4 * 2, W]
+        for j in range(4):
+            (CP if j % 2 else ACT)(w16("sg", hs[j], hs[j + 1]), ind(stw, ap("ox", hs[j], hs[j + 1])))
+        parts = [(0, 2 * HS), (2 * HS, P)]
+        for a, b in parts:
+            cd = ps(2 if a else 3, a, b)
+            MM(cd, wrap("zs", "sg", 16 * a, b - a))
+            TT(ap("ne", a, b), cd, ap("ri", a, b), OP.not_equal)
+            TT(ap("mv", a, b), cd, ap("ne", a, b), OP.is_ge)
+            ACT(ap("kbs", a, b), cd, AF.Sign)
+
+        def held(m, a=0, b=P):
+            return [(m[1], ap("mv", a, b)), (m[2], ap("kbs", a, b))], [(m[0], ap("mv", a, b))]
+        for a, b in parts:
+            lc = [] if last else [(full("ihf"), ap("lc", a, b))]
+            x = held([full(n) for n in ("b64", "nb64", "b32")], a, b)
+            nmb = 1 if a else 0
+            MMS([(ps(nmb, 2 * a, a + b), lc + [(idn, ap("nx5", a, b))] + x[0]), (ps(nmb, a + b, 2 * b), lc + x[1])])
+            if last:
+                ACT(ap("nm", 2 * a, 2 * b), ps(nmb, 2 * a, 2 * b), AF.Relu, bias=-1023.0)
+            else:
+                ACT(ap("nm", 2 * a, 2 * b), ps(nmb, 2 * a, 2 * b), AF.Relu, bias=-991.5, acc=NB if a else LP)
+                if not a:
+                    ACT(C12, LP, scale=-1.0, bias=TM2)
+                    ACT(C13, C12, bias=THETA[t + 1] + 15.5)
+        if not last:
+            TS(Q, NB, C12, OP.subtract, -1.0 / 32, OP.mult)
+            TS(THR, Q, -32.0, OP.mult, C13, OP.add)
+            MM(ps(1, 400, 424), pairs("zs", "sg", 16 * P))
+            ACT(sm(0, 24), ps(1, 400, 424), AF.Relu, scale=4096.0 * 256, bias=-6144.0)
+            ACT(sm(24, 24), ps(1, 400, 424), scale=256.0, bias=OWB[t])
+            TT(sm(0, 24), sm(0, 24), sm(24, 24), OP.min)
+            TT(full("own"), sm(0, 24), full("own"), OP.max)
+            CP(full("ou"), full("own"))
+        cols = lambda terms, a, b: [(l, ap(x["n"], x["a"] + a, x["a"] + b)) for l, x in terms]
+        made = lambda a, b: [(n4k, ap("nm", 2 * a, a + b)), (n4k, ap("nm", a + b, 2 * b))]
+        for a, b in (parts if last else [(0, P)]):
+            x = held([i4k, n4k, i2k], a, b)
+            MMS([(ps(1, a, b), [(idn, ap("mone", a, b)), (i2k, ones(b - a))] + x[0]), (ps(1, P + a, P + b), [(idn, ap("mone", a, b))] + x[1])])
+            for h in (0, 1):
+                TT(ap("rk", P * h + a, P * h + b), ps(1, P * h + a, P * h + b), ap("old", a, b), OP.min)
+        tvb = (4, 6) if last else (0, 1)
+        tvs = [[(idn, full("nba")), (idn, full("nbb")), (full("t4" if h else "t2"), full("mone"))] + x
+               for h, x in enumerate(held([full(n) for n in ("t4", "nt4", "t2")]))]
+
+        def slots():
+            if not last:
+                for h in (0, 1):
+                    MMS([(ps(tvb[h], a, b), cols(tvs[h], a, b) + made(a, b)) for a, b in parts])
+            for a, b in (parts if last else [(0, P)]):
+                if last:
+                    for h in (0, 1):
+                        MMS([(ps(tvb[h], a, b), cols(tvs[h], a, b))], done=False)
+                    for h in (0, 1):
+                        MMS([(ps(tvb[h], a, b), made(a, b))], fresh=False)
+                TT(ap("tv", a, b), ps(tvb[0], a, b), ap("rk", a, b), OP.max)
+                CP(ind(ap("bl", 0, UC), ap("dlu", a // 16, b // 16)), ap("tv", a, b))
+                TT(ap("bl", UC + a, UC + b), ps(tvb[1], a, b), ap("rk", P + a, P + b), OP.max)
+        MMS([(ps(5 if last else 0, a, b), cols(gap, a, b) + made(a, b)) for a, b in parts])
         if last:
-            TT(full("vn"), ps(1, 0, P), full("vn"), OP.mult)
-            DMA("S", "dout", [(lambda: T.yy[:, 1744:1936], lambda: T.my[:, P:2 * P])], [], [ym])
+            slots()
+            MMS([(ps(5, P + a, P + b), cols([(ap("zz", ZZ["z1"] + 15, ZZ["z1"] + 143), ap("dlb", 0, P)), (full("e1"), full("nba"))], a, b) + made(a, b))
+                 for a, b in parts])
+            ACT(full("my"), ps(5, 0, P), AF.Relu)
+            ACT(full("vn"), ps(5, P, 2 * P), AF.Relu, bias=VNB)
+            DMA("S", "dout", [(lambda: T.yy[:, 1744:1936], lambda: T.my[:])], [], [full("my")])
             DMA("S", "dout", [(lambda h=h: T.ye[h:16:2, 1744:1936], lambda h=h: T.vn[h:128:16, :]) for h in (0, 1)], [], [full("vn")])
-            DMA("S", "dout", [(lambda: T.yl[:, 0:768], lambda: T.bl[:, 0:768])], [], [ap("bl", 0, 768)], 3600.0)
-            DMA("S", "dout", [(lambda: T.yl[:, 768:960], lambda: T.tn[:])], [], [full("tn")], 2500.0)
+            DMA("S", "dout", [(lambda: T.yl[:, 768:960], lambda: T.bl[:, U0 + 768:U0 + 960])], [], [ap("bl", U0 + 768, U0 + 960)], 2500.0)
+            DMA("S", "dout", [(lambda: T.yl[:, 0:768], lambda: T.bl[:, U0:U0 + 768])], [], [ap("bl", U0, U0 + 768)], 3600.0)
         else:
-            ACT(ap("my", 0, P), ps(1, 0, P))
-            ACT(ap("tb", yn + M, yn + M + P), ym, bias=128.0)
-            ACT(ap("rr", M, M + P), ym, scale=2.0)
-            MM(ps(3, 0, 24), wrap("z1", "my", 0, 24))
-            TT(ap("e0", K, K + 12), ps(3, 0, 12), sm(128, 12), OP.mult)
-            ACT(sm(232, 12), ap("jw", 0, 12), scale=0.0625, bias=C / 16.0)
-            TT(ap("e1", K, K + 12), ps(3, 0, 12), sm(232, 12), OP.mult)
-            ACT(ap("dead", K, K + 12), ps(3, 12, 24), AF.Relu, scale=-4096.0, bias=4096 * 175.5)
-            lists(K, K + 12)
+            TS(ap(yn, yo + M, yo + M + P), ps(0, 0, P), 128.0, OP.add, 128.0, OP.max)
+            ACT(ap("rr", M, M + P), ps(0, 0, P), AF.Relu, scale=2.0)
+            ny = ps(0, 400, 412)
+            MM(ny, [(blk, ap("k3", 0, 12))] + wrap("z4k", yn, yo + M, 12))
+            for h in (0, 1):
+                TT(ee(h, K, K + 12), ny, sm(64 + 16 * h, 12), OP.min)
+            ACT(ap("sgl", K, K + 12), ny, AF.Sign, bias=-4096 * 175.5)
+            lists(t + 1, 1, 1)
+            slots()
     return ops
 
 
@@ -559,99 +673,132 @@ def depend(ops):
 def place(eng, cost, succ, left0, prio):
     n = len(cost)
     left, at, start = list(left0), [0.0] * n, [0.0] * n
-    ready = [(prio[i], i) for i in range(n) if left[i] == 0]
+    ready = sorted((prio[i], i) for i in range(n) if left[i] == 0)
     busy = {e: [] for e in "VAPGSX"}
     while ready:
-        m = min(ready)
-        ready.remove(m)
-        i = m[1]
+        i = ready.pop(0)[1]
         s, b, c = at[i], busy[eng[i]], cost[i]
-        x = len(b)
+        x = k = len(b)
         while x > 0 and b[x - 1][1] > s:
             x -= 1
-        k = len(b)
         while x < k and b[x][0] < s + c:
-            s = max(s, b[x][1])
+            if b[x][1] > s:
+                s = b[x][1]
             x += 1
         b.insert(x, (s, s + c))
         start[i] = s
+        s += c
         for j, d in succ[i]:
-            if s + c + d > at[j]:
-                at[j] = s + c + d
+            if s + d > at[j]:
+                at[j] = s + d
             left[j] -= 1
             if left[j] == 0:
-                ready.append((prio[j], j))
+                m = (prio[j], j)
+                lo, hi = 0, len(ready)
+                while lo < hi:
+                    y = (lo + hi) // 2
+                    if ready[y] > m:
+                        hi = y
+                    else:
+                        lo = y + 1
+                ready.insert(lo, m)
     return start
 
 
-PRIO = {}
+ORDER = {}
 
 
-def schedule(ops, wake=120.0, tries=16000, seed=1, heat=60.0):
+def schedule(ops, wake=150.0, tries=15000, seed=1, heat=60.0):
     n = len(ops)
+    if n in ORDER:
+        return ORDER[n][0]
     eng, cost = [o["e"] for o in ops] + ["X"], [o["c"] + 1.0 for o in ops] + [1.0]
-    fwd, left = [[(n, o["lat"])] for o in ops] + [[]], [len(o["dep"]) for o in ops] + [n]
-    bwd = [[] for _ in ops] + [[(i, o["lat"]) for i, o in enumerate(ops)]]
-    for i, o in enumerate(ops):
-        for j, w in o["dep"].items():
-            d = ops[j]["lat"] + (wake if w else 0.0)
-            fwd[j].append((i, d)); bwd[i].append((j, d))
-    if n not in PRIO:
-        rank = [0.0] * (n + 1)
-        for i in range(n - 1, -1, -1):
-            rank[i] = cost[i] + max(rank[j] + d for j, d in fwd[i])
-        rng = np.random.RandomState(seed)
-        cur = best = place(eng, cost, fwd, left, [-r for r in rank])
-        name = [(o["e"], o["w"][0]["n"]) if o["w"] else o["e"] for o in ops]
-        kin = [[j for j in range(max(0, i - 14), min(n, i + 15)) if name[j] == name[i]] for i in range(n)]
-        arcs = None
-        for it in range(tries):
-            if it % 50 == 49:
-                back = place(eng, cost, bwd, [len(f) for f in fwd], [-(cur[i] + cost[i]) for i in range(n + 1)])
-                new = place(eng, cost, fwd, left, [-(back[i] + cost[i]) for i in range(n + 1)])
-                if new[n] <= cur[n]:
-                    cur, arcs = new, None
-                    if cur[n] < best[n]:
-                        best = cur
-                continue
-            if arcs is None:
-                ends = {(eng[i], round(cur[i] + cost[i], 3)): i for i in range(n)}
-                arcs, i = [], n
-                while i is not None:
-                    nxt = None
-                    for j, d in bwd[i]:
-                        if abs(cur[j] + cost[j] + d - cur[i]) < 1e-6:
-                            nxt = j
-                    if nxt is None:
-                        nxt = ends.get((eng[i], round(cur[i], 3)))
-                        if nxt is not None:
-                            arcs.append((nxt, i))
-                    i = nxt
-            u, v = arcs[rng.randint(len(arcs))]
-            prio = list(cur)
-            step = float(rng.exponential((400.0, 2000.0, 6000.0)[rng.randint(3)]))
-            fam = rng.uniform() < 0.5
+    arcs = [[(j, ops[j]["lat"] + (wake if w else 0.0)) for j, w in o["dep"].items()] for o in ops]
+    via, bwd = [dict() for _ in ops], []
+    for i, a in enumerate(arcs):
+        bwd.append([(j, d) for j, d in a if not any(x != j and via[x].get(j, -1e9) + cost[x] + e >= d for x, e in a)])
+        for j, d in a:
+            via[i][j] = max(via[i].get(j, 0.0), d)
+            for y, e in arcs[j]:
+                via[i][y] = max(via[i].get(y, 0.0), e + cost[j] + d)
+    ends = set(range(n)) - {j for a in bwd for j, _ in a} | {i for i, o in enumerate(ops) if o["lat"]}
+    bwd.append([(i, ops[i]["lat"]) for i in sorted(ends)])
+    fwd = [[] for _ in range(n + 1)]
+    for i, a in enumerate(bwd):
+        for j, d in a:
+            fwd[j].append((i, d))
+    left, right = [len(a) for a in bwd], [len(f) for f in fwd]
+
+    def packed(a):
+        back = place(eng, cost, bwd, right, [-(a[i] + cost[i]) for i in range(n + 1)])
+        b = place(eng, cost, fwd, left, [-back[i] - cost[i] for i in range(n + 1)])
+        return b if b[n] <= a[n] else a
+
+    others = [[o["c"] + 1.0 for o in build(None, None, e)] + [1.0] for e in EST[1:]]
+
+    def worth(a):
+        order, total = sorted(range(n + 1), key=lambda i: a[i]), a[n]
+        for e, c in zip(EST[1:], others):
+            fin, free = [0.0] * (n + 1), dict.fromkeys("VAPGSX", 0.0)
+            for i in order:
+                s = free[eng[i]]
+                for j, d in bwd[i]:
+                    if fin[j] + d > s:
+                        s = fin[j] + d
+                fin[i] = free[eng[i]] = s + c[i]
+            total += fin[n] * EST[0][0] / e[0]
+        return total / len(EST)
+
+    rank = [0.0] * (n + 1)
+    for i in range(n - 1, -1, -1):
+        rank[i] = cost[i] + max(rank[j] + d for j, d in fwd[i])
+    rng = np.random.RandomState(seed)
+    cur = best = packed(place(eng, cost, fwd, left, [-r for r in rank]))
+    tight, now = None, worth(cur)
+    least = now
+    for it in range(tries):
+        if tight is None:
+            stop = {(eng[i], round(cur[i] + cost[i], 3)): i for i in range(n)}
+            tight, i = [], n
+            while i is not None:
+                nxt = None
+                for j, d in bwd[i]:
+                    if abs(cur[j] + cost[j] + d - cur[i]) < 1e-6:
+                        nxt = j
+                if nxt is None:
+                    nxt = stop.get((eng[i], round(cur[i], 3)))
+                    if nxt is not None:
+                        tight.append((nxt, i))
+                i = nxt
+        step = (300.0, 1500.0, 5000.0)[rng.randint(3)]
+        if rng.uniform() < 0.3:
+            c = np.array(cur)
+            pick = (np.abs(c - rng.uniform(0, cur[n])) < (2000.0, 6000.0)[rng.randint(2)]) & (rng.uniform(size=n + 1) < (0.1, 0.3)[rng.randint(2)])
+            prio = (c + pick * rng.normal(0.0, step, n + 1)).tolist()
+        else:
+            u, v = tight[rng.randint(len(tight))]
+            prio, step = list(cur), float(rng.exponential(step))
             if rng.randint(2):
-                for x in (kin[u] if fam else [u]):
-                    if cur[x] >= cur[u] - 3000:
-                        prio[x] = max(cur[x], cur[v] + step + 1e-3 * cur[x])
+                prio[u] = cur[v] + step + 1.0
             else:
-                to, todo = cur[u] - step * rng.randint(2) - 0.5, list(kin[v] if fam else [v])
+                to, todo = cur[u] - step * rng.randint(2) - 0.5, [v]
                 while todo:
                     x = todo.pop()
                     if prio[x] > to:
                         prio[x] = to - 1e-3 * (cur[n] - cur[x])
                         todo += [j for j, _ in bwd[x]]
-            new = place(eng, cost, fwd, left, prio)
-            if new[n] <= cur[n] + heat * (1.0 - it / tries) * float(rng.exponential(1.0)):
-                cur, arcs = new, None
-                if cur[n] < best[n]:
-                    best = cur
-        PRIO[n] = best
-    st = place(eng, cost, fwd, left, PRIO[n])
-    for o, t in zip(ops, st):
-        o["t"] = t
-    return sorted(range(n), key=lambda i: (st[i], i))
+        new = place(eng, cost, fwd, left, prio)
+        if rng.uniform() < 0.1:
+            new = packed(new)
+        room = heat * (1.0 - it / tries) * float(rng.exponential(1.0))
+        if new[n] <= cur[n] + room + 600.0:
+            w = worth(new)
+            if w <= now + room:
+                cur, now, tight = new, w, None
+                if now < least:
+                    best, least = cur, now
+    ORDER[n] = (sorted(range(n), key=lambda i: (best[i], i)), best)
+    return ORDER[n][0]
 
 
 def emit(g, T, ops, order, arrivals, sent):
@@ -697,10 +844,7 @@ def masks(topo, src, dsts):
     return res
 
 
-def rank_program(g, core, T, topo):
-    q = T.rank_of(core)
-    if q is None:
-        return
+def make_ops(T, core, q, topo):
     n = len(T.cores)
     peers = [T.cores[(q + d) % n] for d in range(1, n)]
     mask = masks(topo, core, peers)
@@ -711,9 +855,17 @@ def rank_program(g, core, T, topo):
             rid, pid = topo.addr(peers[d - 1], core)
             trs.append(RemoteDMATransfer(dst_ids=[DstId(rid=rid, pnc=pid)], dma_engine_mask=mask[peers[d - 1]],
                                          remote_sem=T.sem["arr%d" % t], src=T["sb%d" % t][:, 128 * (d - 1):128 * d],
-                                         dst=T["ld%d" % t][:, 128 * (n - 1 - d):128 * (n - d)]))
+                                         dst=T.tb[:, WB[t] + 16 + 128 * (n - 1 - d):WB[t] + 16 + 128 * (n - d)]))
         return g.remote_dma_fused(trs, local_sem=T.sem.sent)
 
-    ops = build(T, send, q)
+    return build(T, send)
+
+
+def rank_program(g, core, T, topo):
+    q = T.rank_of(core)
+    if q is None:
+        return
+    n = len(T.cores)
+    ops = make_ops(T, core, q, topo)
     depend(ops)
     emit(g, T, ops, schedule(ops), 4 * (n - 1), 4 * (n - 1) * RO)

@@ -18,22 +18,22 @@ ZZ = {n: 144 * i for i, n in enumerate("z4k z01 zs z1 z8k zi zc zn8 z16k".split(
 def _scratch():
     s = {}
     for names, cols, d in (
-        ("tb", YO[2] + 1744, BF), ("inf", 1360, BF), ("dzt", 976, BF),
+        ("tb", YO[2] + 1744, BF), ("inf", PB + 976, BF), ("dzt", 976, BF),
         ("y0r", 1360, BF), ("xx dlb", 960, BF), ("nex", 576, BF), ("rr az dz gz nw zt d0 d1 ab0 ab1 ab2 ab3 i0", 1744, BF),
-        ("m256", 256, BF), ("m128", 436, BF), ("c128", 272, BF), ("one2 half", 512, BF),
+        ("m128", 436, BF), ("c128", 272, BF), ("one2 half", 512, BF),
         ("nc zero c192", 768, BF), ("cum", 784, BF), ("fl wd", 1024, BF), ("iov", 976, BF), ("iof", 976, F32),
         ("st yf i1", 1760, BF), ("sg", 3264, BF), ("bm", 2048, BF),
         ("sb0 sb1 sb2 nm", 384, BF), ("zz", 144 * len(ZZ), BF), ("gm", 8, BF),
-        ("blk idn nidn ihf i63 i4k n4k i2k i256 i1k ic n64 i2 n2112 i960 id0 ie0 id1 ie1 id2 ie2 tri t4 nt4 t2 ms b64 nb64 b32 nblk nd8 "
+        ("blk idn nidn ihf i63 i4k n4k i1k ic n64 i2 id0 ie0 id1 ie1 id2 ie2 tri t4 nt4 ms b64 nb64 nblk nd8 "
          "e01 ne01 e0a e0b e1 idl nidl idl0 nidl0", 128, BF),
-        ("idf nidf blkh sf", 128, F32),
+        ("idf blkh sf", 128, F32),
         ("k12 cp sgl sw far unt mine th tj c208 c1k", 112, BF), ("k3", 16, BF),
         ("bl", 1168, F32), ("bli", 384, I32), ("enb", 1360, I32), ("ent", 256, I32), ("entf et", 256, F32),
         ("sndi", 12, I32), ("col", 32, F32), ("coli", 8, I32), ("oh", 16, F32), ("sm", 96, F32),
         ("jw swf fa araw r0 r1", 112, F32), ("jt", 48, F32), ("own", 24, F32), ("pbc", 336, F32),
         ("ee c1 mm t45 t01", 224, F32), ("iv kk", 224, BF), ("ab", 224, I32), ("best", 112, I32), ("gu", 448, U16), ("ix", 224, U16),
         ("old", 204, F32), ("hib", 204, BF), ("ox", 204, U16), ("tg", 48, U16), ("dlu su", 12, U16), ("ou", 24, U16),
-        ("hg lg lc ri ne mv nx5 kbs nba nbb mone eo my", 192, BF), ("vn tv", 192, F32), ("rk", 384, F32),
+        ("hg lg lc ri ne mv kbs nba nbb mone eo my", 192, BF), ("vn tv", 192, F32), ("rk", 384, F32),
     ):
         for n in names.split():
             s[n] = ("sbuf", [128, cols], d)
@@ -46,11 +46,12 @@ PART = {n: (b, 128 * i) for b, d in (("fw", F32), ("mw", BF))
         for i, n in enumerate(n for n, s in SHAPES.items() if s[1][1] == 128 and s[2] == d)}
 SCRATCH = {n: s for n, s in SHAPES.items() if n not in PART}
 SCRATCH.update({b: ("sbuf", [128, 128 * sum(1 for x in PART.values() if x[0] == b)], d) for b, d in (("fw", F32), ("mw", BF))})
-SEMAPHORES = (["qv", "qa", "qp", "qg", "sent", "arr0", "arr1", "arr2", "dy", "dx", "denb", "dsnd", "dbl", "dent", "dout", "dz", "dz2",
-               "dyy", "gyy", "gy0", "dy0", "drr", "grr", "gwd", "dd0", "dd1", "dd2"]
-              + ["%s%d%d" % (n, t, g) for n in ("dr", "ga", "gb") for t in (0, 1) for g in (0, 1)])
+SEMAPHORES = ["qv", "qa", "qp", "qg", "sent", "arr0", "arr1", "arr2", "dy", "dx", "denb", "dsnd", "dbl", "dent", "dout", "dz", "dz2",
+              "dyy", "gyy", "gy0", "dy0", "gwd", "dd0", "dd1", "dd2"]
 QSEM = {"V": "qv", "A": "qa", "P": "qp", "G": "qg"}
-EST = ((0.92, 1.45, 3.8), (0.83, 1.1, 2.5), (1.12, 1.85, 4.5))
+EST = ((0.92, 1.45, 3.8), (0.83, 1.2, 2.5), (1.12, 1.85, 4.5))
+LAG = ((0.9, 135.0), (0.65, 115.0), (1.1, 150.0))
+HALF = (1, 2)
 HS = 64
 ONV = ((0, 0),)
 RELU = ()
@@ -197,7 +198,7 @@ def build(T, send, est=EST[0]):
     OWB = [col(24 + t) for t in range(2)]
     oh = lambda r: ap("oh", r, r + 1)
     Q = ap("coli", 2, 3)
-    blk, idn, nidn, idf, i4k, n4k, i2k = [full(n) for n in ("blk", "idn", "nidn", "idf", "i4k", "n4k", "i2k")]
+    blk, idn, nidn, idf, i4k, n4k = [full(n) for n in ("blk", "idn", "nidn", "idf", "i4k", "n4k")]
     ones = lambda n: ap("one2", 0, n)
     ecol = lambda r: 128 * (r % 2) + 16 * (r // 2)
     ee = lambda h, a, b: ap("ee", 112 * h + a, 112 * h + b)
@@ -205,12 +206,10 @@ def build(T, send, est=EST[0]):
 
     DMA("S", "dy", [(lambda: T.y0r[:], lambda: T.y0[:])], [full("y0r")], [], 2800.0)
     DMA("S", "dx", [(lambda: T.xx[:, 0:V0], lambda: T.x0[:])], [ap("xx", 0, V0)], [], 2400.0)
-    DMA("S", "dent", [(lambda r=r: T.ent[0:85, ecol(r):ecol(r) + 16], lambda r=r: T.en0[r, :]) for r in range(16)], [full("ent")], [])
+    DMA("S", "dent", [(lambda r=r: T.ent[0:85, ecol(r):ecol(r) + 16], lambda r=r: T.en0[r, :]) for r in range(16)], [full("ent")], [], 3000.0)
     DMA("S", "dsnd", [(lambda: T.sndi[:], lambda: T.snd[:])], [full("sndi")], [])
-    DMA("A", "denb", [(lambda h=h: T.enb[h:128:16, :], lambda h=h: T.en0[h % 2:16:2, :]) for h in range(16)], [full("enb")], [], 4000.0)
-    DMA("S", "drr", [(lambda: T.rr[:, 0:B0], lambda: T.y0[:])], [ap("rr", 0, B0)], [], 4000.0)
-    DMA("G", "grr", [(lambda: T.rr[:, 0:B0], lambda: T.y0r[:])], [ap("rr", 0, B0)], [full("y0r")], 4000.0)
-    DMA("S", "dbl", [(lambda: T.bli[:], lambda: T.bl0[:])], [full("bli")], [])
+    MS(full("enb"), 0)
+    DMA("A", "denb", [(lambda h=h: T.enb[h:128:16, :], lambda h=h: T.en0[h:16:2, :]) for h in (0, 1)], [full("enb")], [], 2400.0)
 
     MS(ones(512), 1.0)
     IOTA(ap("coli", 0, 1), [[0, 1]], 0, 1)
@@ -242,8 +241,8 @@ def build(T, send, est=EST[0]):
     MS(ap("e0a", 0, 256), 0.0)
     for n, r, c in (("e0a", 0, 16.0), ("e0a", 3, -255.0 / 16), ("e0b", 0, -255.0 / 16), ("e0b", 3, 255.0 / 16)):
         TS(ap(n, r, 128, 16), full("gm"), c, OP.mult)
-    for n, s, c in (("idf", idn, 1.0), ("blkh", blk, 0.5), ("nidf", idn, -1.0), ("ne01", full("e01"), -1.0), ("idl0", idn, DELTA[0]),
-                    ("nidl0", idn, -DELTA[0]), ("nidn", idn, -1.0), ("i4k", idn, 4096.0), ("n2112", idn, -2112.0), ("i960", idn, 960.0),
+    for n, s, c in (("idf", idn, 1.0), ("blkh", blk, 0.5), ("ne01", full("e01"), -1.0), ("idl0", idn, DELTA[0]),
+                    ("nidl0", idn, -DELTA[0]), ("nidn", idn, -1.0), ("i4k", idn, 4096.0),
                     ("id0", idn, 400.0), ("ie0", idn, 400.0 + HD)):
         ACT(full(n), s, scale=float(c))
 
@@ -259,27 +258,36 @@ def build(T, send, est=EST[0]):
     MS(full("zero"), 0.0)
     ACT(full("c192"), full("zero"), bias=192.0)
     MS(ap("cum", 0, 16), 0.0)
-    fills = [("tb", PB, PB + U0), ("tb", PB + U0 + V0, PB + 976), ("tb", PB + HD, PB + HD + U0), ("inf", 0, U0), ("inf", U0 + V0, 1360),
-             ("tb", WB[0], WB[0] + 16), ("dzt", 0, U0)]
-    later = [("tb", PB + HD + U0 + V0, YO[0]), ("yf", 0, 16), ("i1", B0, 1760)]
+    fills = [("tb", PB, PB + U0), ("tb", PB + U0 + V0, PB + 976), ("tb", PB + HD, PB + HD + U0), ("inf", WB[0], PB + U0),
+             ("dzt", 0, U0)]
+    MS(ap("tb", WB[0], WB[0] + 16), 0.0)
+    for t in range(RO):
+        MS(ap("i1", B0 + P * t, B0 + P * t + 16), 0.0)
+    later = [("inf", 0, WB[1]), ("inf", WB[1], WB[0]), ("tb", PB + HD + U0 + V0, YO[0]), ("yf", 0, 16)]
     later += [("tb", a, a + 16) for t in (1, 2) for a in (WB[t], YO[t] - 16)]
-    for sem, fl in (("dz", fills), ("dz2", later)):
+
+    def zeros(sem, fl, more=()):
         DMA("S", sem, [(lambda n=n, a=a, b=b: T[n][:, a:b], lambda a=a, b=b: T.zero[:, 0:b - a]) for n, a, b in fl],
-            [ap(n, a, b) for n, a, b in fl], [full("zero")])
+            [ap(n, a, b) for n, a, b in fl], [full("zero")] + list(more), 2600.0)
+    zeros("dz", fills)
     MS(ap("tb", PB + 976, PB + HD), 128.0)
-    for n, a, c in (("sgl", 85, 1), ("sw", 85, 0), ("far", 85, 0), ("swf", 85, 0), ("fa", 85, 0), ("araw", 85, 0), ("r0", 85, 0), ("r1", 85, 0),
-                    ("c1k", 0, 1024), ("unt", 85, 0)):
+    for n, a, c in (("sgl", 85, 1), ("sw", 85, 0), ("far", 85, 0), ("swf", 85, 0), ("fa", 85, 0), ("c1k", 0, 1024), ("unt", 85, 0)):
         IOTA(ap(n, a, 112), [[0, 112 - a]], c, 0)
+    for h in (0, 1):
+        IOTA(ee(h, 85, 112), [[0, 27]], 0, 0)
     MS(ap("cp", 0, 1), 0.0)
 
     def late_constants():
-        for n, a, b, c in (("c128", 0, 272, 128), ("bl", 0, U0, -1), ("m256", 0, 256, -256),
-                           ("m128", 0, 436, -128), ("k3", 0, 16, -524288), ("c208", 0, 112, 208), ("mone", 0, 192, -1)):
+        landed = ap("tb", WB[0] + 16, WB[0] + 400)
+        zeros("dz2", later, [landed])
+        DMA("S", "dbl", [(lambda: T.bli[:], lambda: T.bl0[:])], [full("bli")], [landed])
+        CP(ap("bl", U0, U0 + V0), full("bli"))
+        for n, a, b, c in (("c128", 0, 272, 128), ("bl", 0, U0, -1), ("k3", 0, 16, -524288), ("mone", 0, 192, -1)):
             IOTA(ap(n, a, b), [[0, b - a]], c, 0, 0)
         DMA("S", "dy0", [(lambda a=a: T.tb[:, YO[0] + a:YO[0] + a + 272], lambda: T.c128[:]) for a in range(0, B0, 272)],
-            [ap("tb", YO[0], YO[0] + B0)], [full("c128")])
+            [ap("tb", YO[0], YO[0] + B0)], [full("c128"), landed])
         DMA("G", "gy0", [(lambda: T.tb[:, YO[0]:YO[0] + B0], lambda: T.y0r[:])], [ap("tb", YO[0], YO[0] + B0)], [full("y0r")], 4000.0)
-        DMA("G", "gwd", [(lambda: T.wd[:], lambda: T.y0r[:, 0:1024])], [full("wd")], [ap("y0r", 0, 1024), ap("sent", 0, 1)], 4000.0)
+        DMA("G", "gwd", [(lambda: T.wd[:], lambda: T.y0r[:, 0:1024])], [full("wd")], [ap("y0r", 0, 1024), landed], 4000.0)
         IOTA(ap("iof", 592, 976), [[1, 384]], 592, 0, 0)
         IOTA(full("nba"), [[1, P]], B0 % 64, 0, 0)
         ACT(full("ri"), ap("iof", 2, P + 2), scale=1.0 / 256)
@@ -287,17 +295,16 @@ def build(T, send, est=EST[0]):
         SEL(full("half"), full("half"), [[0, 32], [-1, 16]], OP.is_ge, 7, 0)
         for r in range(0, 16, 4):
             SEL(ap("bm", 128 * r, 128 * r + 512), full("half"), [[-1, 4], [-16, 8], [0, 16]], OP.is_equal, -r, 1)
-        for n, c in (("i256", 256), ("i1k", 1024), ("i2", 2), ("n4k", -4096), ("n64", -64), ("i2k", 2048), ("id1", 800), ("ie1", 800 + HD),
-                     ("id2", 1200), ("ie2", 1200 + HD)):
+        for n, c in (("n4k", -4096), ("n64", -64), ("id1", 800), ("ie1", 800 + HD)):
             scaled(n, EYE, c)
-        for n, c in (("b64", 64.0), ("nb64", -64.0), ("b32", 32.0), ("nblk", -1.0)):
+        for n, c in (("b64", 64.0), ("nb64", -64.0), ("nblk", -1.0)):
             ACT(full(n), blk, scale=c)
         scaled("nd8", BLK + [([[0, 8], [1, 16]], OP.is_ge, -8, 0)], -4096)
         SEL(full("tri"), blk, [[1, 128]], OP.is_gt, 0, -1)
         TT(full("tri"), full("tri"), idn, OP.subtract)
-        for n, c in (("t4", 4096.0), ("nt4", -4096.0), ("t2", 2048.0)):
+        for n, c in (("t4", 4096.0), ("nt4", -4096.0)):
             ACT(full(n), full("tri"), scale=c)
-        for n, c in (("ihf", 0.5), ("i63", 63.75), ("e1", oh(1))):
+        for n, c in (("i1k", 1024.0), ("i2", 2.0), ("ihf", 0.5), ("i63", 63.75), ("e1", oh(1))):
             TS(full(n), idn, c, OP.mult)
         for t in (0, 1):
             ACT(OWB[t], PAR, bias=U0 + V0 + P * t - 2.0)
@@ -314,9 +321,8 @@ def build(T, send, est=EST[0]):
         sg = (i4k, ap("sgl", a, b))
         MMS([(ps(bank, o, o + w), [(idf, ee(0, a, b)), (full("id%d" % t), ap("mine", a, b)), sg]),
              (ps(bank, o + w, o + 2 * w), [(idf, ee(0, a, b)), (full("ie%d" % t), ap("mine", a, b)), (idn, ap("far", a, b)), sg]),
-             (ps(bank, o + 2 * w, o + 3 * w), [(idf, ee(0, a, b)), (i4k, ones(w)), (full("i960"), ap("far", a, b))]),
-             (ps(bank, o + 3 * w, o + 4 * w), [(idf, ee(1, a, b)), sg])])
-        TS(ap("gu", o, o + 4 * w), ps(bank, o, o + 4 * w), -4096.0, OP.add)
+             (ps(bank, o + 2 * w, o + 3 * w), [(idf, ee(1, a, b)), sg])])
+        TS(ap("gu", o, o + 3 * w), ps(bank, o, o + 3 * w), -4096.0, OP.add)
 
     MM(ps(6, 0, V0), [(blk, ap("xx", 0, V0))])
     MM(ps(7, 0, 85), wrap("z4k", "y0r", 0, 85))
@@ -333,33 +339,36 @@ def build(T, send, est=EST[0]):
     TS(full("own"), ps(3, 0, 24), PAR, OP.add, float(U0), OP.add)
     p85 = (0, 85, 1)
     CP(ap("entf", 0, 256, 1, p85), ap("ent", 0, 256, 1, p85))
-    for h in (0, 1):
-        TR(ps(h, 0, 85), ap("entf", 128 * h, 128 * h + 128, 1, p85), ap("idf", 0, 85, 1, p85))
+    turn = lambda h: (ap("entf", 128 * h, 128 * h + 128, 1, p85), ap("idf", 0, 85, 1, p85))
+    more = (idn, ap("c208", 0, 85))
+    MS(ap("c208", 0, 85), float(U0))
+    for bank, terms in ((1, [turn(1), more]), (0, [turn(0), more]), (5, [turn(0), turn(1), more, more])):
+        MM(ps(bank, 0, 85), terms)
     k0 = lambda n: ap(n, 0, 85)
-    TS(k0("sw"), ps(1, 0, 85), float(FAR), OP.is_ge)
+    TS(k0("sw"), ps(1, 0, 85), float(FAR + U0), OP.is_ge)
     TT(k0("swf"), ps(1, 0, 85), k0("sw"), OP.mult)
     TT(k0("araw"), ps(0, 0, 85), k0("swf"), OP.max)
-    for h in (0, 1):
-        ACT(k0("r%d" % h), ps(h, 0, 85))
-    TS(k0("far"), k0("araw"), float(FAR), OP.is_ge)
+    ACT(k0("r0"), k0("araw"), AF.Abs, scale=2.0, bias=16.0 - 2 * (FAR + U0))
+    TT(ee(1, 0, 85), ps(5, 0, 85), k0("araw"), OP.subtract)
+    TS(k0("far"), k0("araw"), float(FAR + U0), OP.is_ge)
+    TT(ee(0, 0, 85), k0("araw"), k0("r0"), OP.min)
     TT(k0("fa"), k0("araw"), k0("far"), OP.mult)
     ACT(full("mine"), full("far"), scale=-1.0, bias=1.0)
     MS(ap("kk", 0, 112), 1.0 / HD)
     TS(ap("kk", 112, 224), full("mine"), 1.0 / HD, OP.mult)
-    MMS([(ps(0, 0, 112), [(idf, full("araw")), (idf, full("fa")), (full("n2112"), full("far"))]),
-         (ps(0, 112, 224), [(idf, full("r0")), (idf, full("r1")), (full("nidf"), full("araw"))])])
-    ACT(full("ee"), ps(0, 0, 224), bias=float(U0))
     for g in (0, 1):
-        lists(0, g, (1, 5)[g])
+        lists(0, g, (1, 7)[g])
     TT(k0("fa"), k0("fa"), k0("swf"), OP.subtract)
     TT(full("tj"), full("far"), full("sw"), OP.subtract)
     TT(full("th"), full("tj"), full("sw"), OP.subtract)
     ACT(full("tj"), full("th"), scale=2048.0, bias=3072.0)
     ACT(full("th"), full("th"), scale=2048.0, bias=2048.0)
-    CP(ap("bl", U0, U0 + V0), full("bli"))
-    TS(full("fl"), ap("y0r", 0, 1024), 0.125, OP.mult, 128.5625, OP.add)
+    for a, b in ((0, 1024), (1024, B0)):
+        ACT(ap("rr", a, b), ap("y0r", a, b), scale=2.0)
+    ACT(full("fl"), ap("y0r", 0, 1024), scale=0.125, bias=128.5625)
     TS(full("wd"), full("fl"), -8.0, OP.mult, 1029.0, OP.add)
 
+    deferred = []
     for t in range(RO):
         M, C, last = B0 + P * t, V0 + P * t, t == RO - 1
         K, KC, UC = M // 16, C // 16, U0 + C
@@ -369,44 +378,56 @@ def build(T, send, est=EST[0]):
         pt = lambda a, b: ap("tb", PB + a, PB + b)
         idl, nidl = (full("idl0"), full("nidl0")) if t == 0 else (full("idl"), full("nidl"))
         GK = [(0, 64), (64, K)]
-        wl, wh, wn, wi = pt(0, UC), pt(HD, HD + UC), ap("tb", WB[t], PB + HD + UC), ap("inf", 0, UC)
+        wl, wh, wn, wi = pt(0, UC), pt(HD, HD + UC), ap("tb", WB[t], PB + HD + UC), [ap("inf", WB[t], PB + UC), ap("inf", PB, PB + UC)]
         gu = lambda j, g, a, b: ap("gu", 256 * g + GW[g] * j + a - 64 * g, 256 * g + GW[g] * j + b - 64 * g)
         cut = lambda a, b: [(c, min(b, c + 32)) for c in range(a, b, 32)]
-        cells = [(a, min(C, a + 512)) for a in range(0, C, 512)]
+        cells = [(0, C // 2), (C // 2, C)] if t in HALF else [(0, C)]
+        cps = lambda bank, a, b: ps(bank + (a > 0), 0, b - a)
         k = lambda n, a=0: ap(n, a, a + K)
         for bank in (2, 4):
-            MMS([(ps(bank, a, b), [(idn, ap("xx", a, b))]) for a, b in cells], done=False)
-        if t == 0:
-            TS(ap("nc", 0, C), ps(6, 0, C), THR, OP.is_ge)
-        else:
-            TS(ap("nc", 0, C), ps(6, 0, C), NB, OP.add, THR, OP.is_ge)
-        o, x, z = ap("cum", 16, 16 + C), ap("nc", 0, C), ap("c192", 0, C)
-        add("V", lambda g, o=o, x=x, z=z: g.vector.tensor_tensor_scan(real(o), real(x), real(z), 0.0, OP.add, OP.min),
-            [o], [x, z], vcost(o, [x, z]))
+            MMS([(cps(bank, a, b), [(idn, ap("xx", a, b))]) for a, b in cells], done=False)
+        for a, b in cells:
+            if t == 0:
+                TS(ap("nc", a, b), ps(6, a, b), THR, OP.is_ge)
+            else:
+                TS(ap("nc", a, b), ps(6, a, b), NB, OP.add, THR, OP.is_ge)
+        for a, b in cells:
+            o, x, z, i = ap("cum", 16 + a, 16 + b), ap("nc", a, b), ap("c192", a, b), ap("cum", 15 + a, 16 + a)
+            add("V", lambda g, o=o, x=x, z=z, i=i: g.vector.tensor_tensor_scan(real(o), real(x), real(z), real(i), OP.add, OP.min),
+                [o], [x, z, i], vcost(o, [x, z]))
         now, was = (lambda a, b: ap("cum", 16 + a, 16 + b)), (lambda a, b: ap("cum", 15 + a, 15 + b))
-        MMS([(ps(2, a, b), [(idl, now(a, b)), (nidl, was(a, b))]) for a, b in cells], fresh=False)
-        MMS([(ps(4, a, b), [(nidl, now(a, b)), (idl, was(a, b))]) for a, b in cells], fresh=False)
-        ACT(pt(U0, UC), ps(4, 0, C), AF.Relu)
-        TS(pt(HD + U0, HD + UC), ps(2, 0, C), 63.0, OP.min)
+        for a, b in cells:
+            MMS([(cps(2, a, b), [(idl, now(a, b)), (nidl, was(a, b))])], fresh=False)
+            MMS([(cps(4, a, b), [(nidl, now(a, b)), (idl, was(a, b))])], fresh=False)
+        for a, b in cells:
+            ACT(pt(U0 + a, U0 + b), cps(4, a, b), AF.Relu)
+            TS(pt(HD + U0 + a, HD + U0 + b), cps(2, a, b), 63.0, OP.min)
         ACT(full(sb), ind(pt(0, HD + UC), full("ou")))
         add("G", lambda g, t=t: send(g, t), [ap("sent", t, t + 1)], [full(sb)], 300.0, 0.0, "none")
         add("X", None, [ap("tb", F, F + 384)], [ap("sent", t, t + 1)], 0.0, 4200.0 if t == 0 else 3000.0, "arr%d" % t, 0)
         if t == 0:
             late_constants()
+        else:
+            deferred.pop()()
+        if t == 1:
+            IOTA(full("m128"), [[0, 436]], -128, 0, 1)
+            for n, c in (("id2", 1200), ("ie2", 1200 + HD)):
+                scaled(n, EYE, c, 1)
         for g, (a, b) in enumerate(GK):
-            TT(w16("nw", a, b), ind(wl, gu(3, g, a, b)), w16("rr", a, b), OP.subtract)
+            TT(w16("nw", a, b), ind(wl, gu(2, g, a, b)), w16("rr", a, b), OP.subtract)
         TT(ap("dzt", U0, UC), pt(HD + U0, HD + UC), pt(U0, UC), OP.subtract)
         for g, (a, b) in enumerate(GK):
-            (CP if (2, g) in ONV else ACT)(w16("zt", a, b), ind(ap("dzt", 0, UC), gu(3, g, a, b)))
-        MMS([(ps(6, a, b), [(full("e0a"), now(a, b)), (full("e0b"), was(a, b))]) for a, b in cells])
-        ACT(ap("inf", U0, UC), ps(6, 0, C), AF.Relu, bias=BASE)
-        MM(ps(4, 256, 448), [(full("ne01"), ap("tb", F, F + 384, 2)), (full("e01"), ap("tb", F + 1, F + 384, 2))])
-        ACT(ap("inf", 976, 1360, 2), ps(4, 256, 448))
-        MM(ps(7, 256, 256 + KC), wrap("zc", "inf", U0, KC))
+            (CP if (2, g) in ONV else ACT)(w16("zt", a, b), ind(ap("dzt", 0, UC), gu(2, g, a, b)))
+        MMS([(ps(6, a, min(C, a + 512)), [(full("e0a"), now(a, min(C, a + 512))), (full("e0b"), was(a, min(C, a + 512)))]) for a in range(0, C, 512)])
+        ACT(ap("inf", PB + U0, PB + UC), ps(6, 0, C), AF.Relu, bias=BASE)
+        MM(ps(5, 256, 448), [(full("ne01"), ap("tb", F, F + 384, 2)), (full("e01"), ap("tb", F + 1, F + 384, 2))])
+        ACT(ap("inf", F, F + 384, 2), ps(5, 256, 448))
+        MM(ps(7, 256, 256 + KC), wrap("zc", "inf", PB + U0, KC))
         TT(sm(0, KC), ps(7, 256, 256 + KC), ap("jt", 0, KC), OP.min)
         TS(ap("tg", 0, KC), sm(0, KC), -16.0, OP.add)
         DMA("S", "dd%d" % t, [(lambda: T.dlb[:, 0:P], lambda: T.iov[:, 16:16 + P])] +
-            ([(lambda: T.dlb[:, P:960], lambda: T.zero[:, 0:768])] if t == 0 else []), [full("dlb")], [ap("iov", 16, 16 + P), full("zero")])
+            ([(lambda: T.dlb[:, P:960], lambda: T.zero[:, 0:768])] if t == 0 else []), [full("dlb")],
+            [ap("iov", 16, 16 + P), full("zero")] + ([ap("tb", F, F + 384)] if t == 0 else []))
         for a in range(0, KC, 12):
             CP(ind(ap("dlb", 0, P + C), ap("tg", a, a + 12)), ap("iov", U0 + 16 * a, U0 + 16 * a + 192))
         MM(ps(7, 320, 332), wrap("z1", "dlb", 0, 12))
@@ -427,7 +448,6 @@ def build(T, send, est=EST[0]):
         nex, gap = ap("nex", P * t, P * t + P), [(idn, full("hg")), (nidn, full("lg"))]
         MMS([(ps(7, 0, P), gap)] + ([] if last else [(ps(7, P, 2 * P), [(blk, full("hg")), (full("nblk"), full("lg"))])]))
         ACT(nex, ps(7, 0, P), AF.Relu, scale=-1.0, bias=1.0)
-        TS(full("nx5"), nex, 1024.0, OP.mult, 512.0, OP.add)
         if last:
             DMA("S", "dout", [(lambda: T.yx[:, 0:768], lambda: T.tb[:, PB + U0:PB + U0 + 768]), (lambda: T.yx[:, 768:960], lambda: T.hg[:])],
                 [], [pt(U0, U0 + 768), full("hg")])
@@ -447,7 +467,7 @@ def build(T, send, est=EST[0]):
         nb = [0]
         for h in (1, 0):
             for g, (a, b) in enumerate(GK):
-                (CP if (h, g) in ONV else ACT)(w16("i%d" % h, a, b), ind(wi if h else full("inf"), gu(2 + h, g, a, b)))
+                (CP if (h, g) in ONV else ACT)(w16("i%d" % h, a, b), ind(wi[h], gu(2 * h, g, a, b)))
 
         def sums(g):
             a, b = GK[g]
@@ -469,8 +489,8 @@ def build(T, send, est=EST[0]):
             ACT(ap("iv", 0, S + K), ps(4, 0, S + K))
             scaled("ic", EYE, C + P, t)
             MMS([(ps(4, 0, S), [(idn, ap("iv", 0, S)), (full("ic"), ap("kk", 0, S))]), (ps(4, S, S + K), [(idn, k("iv", S)), (full("ic"), k("kk", 112))])])
-            MM(ps(5, 256, 256 + K), [(full("i1k"), k("iv")), (full("i1k"), k("iv", S)), (full("i256"), k("sgl"))])
-            ACT(k("unt"), ps(5, 256, 256 + K), AF.Relu, scale=-2.0 ** 23, bias=8192.0 + 2.0 ** 23 * 256)
+            MM(ps(5, 256, 256 + K), [(full("i1k"), k("iv")), (full("i1k"), k("iv", S))])
+            ACT(k("unt"), ps(5, 256, 256 + K), AF.Relu, scale=-2.0 ** 23, bias=8192.0)
             for a, b, o in parts:
                 w, z = b - a, (288 if a else 112)
                 we = w + w % 2
@@ -513,14 +533,6 @@ def build(T, send, est=EST[0]):
                 ACT(w16("gz", c, d), w16("dz", c, d), AF.Abs, scale=0.5)
                 TT(w16(yn, c, d, yo), pre, w16("gz", c, d), OP.add)
 
-        def doubled(g):
-            x, y = 16 * GK[g][0], 16 * GK[g][1]
-            DMA("S", "dr%d%d" % (t, g), [(lambda u=u: T.rr[:, u:min(y, u + 256)], lambda u=u: T.m256[:, 0:min(y, u + 256) - u]) for u in range(x, y, 256)],
-                [ap("rr", x, y)], [full("m256")], 3000.0)
-            for n in ("ga", "gb"):
-                DMA("G", "%s%d%d" % (n, t, g), [(lambda: T.rr[:, x:y], lambda yo=yo: T.tb[:, yo + x:yo + y])], [ap("rr", x, y)],
-                    [ap(yn, yo + x, yo + y)], 3500.0)
-
         sums(0); before([(0, 64, 0), (64, K, 128)]); sums(1); choice(0, 0); choice(1, 128)
         new_y([(0, 32), (32, 64)], 0, 0); new_y([(64, 88), (88, K)] if K > 96 else [(64, K)], 1, 128)
         MM(ps(5, 256, 256 + K), [(idf, k("t01")), (idf, k("t01", S))])
@@ -529,16 +541,15 @@ def build(T, send, est=EST[0]):
             TT(ee(h, 0, K), ee(h, 0, K), k("t01", S * (1 - h)), OP.max)
         if last:
             pk = (0, K, 1)
-            MMS([(ps(6, 0, K), [(idf, ee(1, 0, K)), (i4k, k("sw")), (n4k, ones(K)), (nidn, k("c208"))]),
-                 (ps(6, 128, 128 + K), [(idf, ee(0, 0, K)), (n4k, k("far")), (nidn, k("c208"))]),
-                 (ps(6, 256, 256 + K), [(idf, ee(1, 0, K)), (nidn, k("c208"))])])
+            MMS([(ps(6, 0, K), [(idf, ee(1, 0, K)), (i4k, k("sw")), (n4k, ones(K))]),
+                 (ps(6, 128, 128 + K), [(idf, ee(0, 0, K)), (n4k, k("far"))])])
             TT(k("araw"), ps(6, 0, K), k("fa"), OP.max)
             TT(k("r0"), ps(6, 128, 128 + K), k("araw"), OP.max)
-            TT(k("r1"), ps(6, 256, 256 + K), k("swf"), OP.max)
+            TT(k("r1"), ee(1, 0, K), k("swf"), OP.max)
             for h in (0, 1):
                 TR(ps(7, 128 * h, 128 * h + 128, pk), k("r%d" % h), idf)
-            ACT(ap("et", 0, 256, 1, pk), ps(7, 0, 256, pk))
-            DMA("S", "dout", [(lambda r=r: T.ye[r, 0:1744], lambda r=r: T.et[0:109, ecol(r):ecol(r) + 16]) for r in range(16)], [], [full("et")])
+            ACT(ap("et", 0, 256, 1, pk), ps(7, 0, 256, pk), AF.Relu, bias=-float(U0))
+            DMA("S", "dout", [(lambda r=r: T.ye[r, 0:1744], lambda r=r: T.et[0:109, ecol(r):ecol(r) + 16]) for r in range(16)], [], [full("et")], 6000.0)
             DMA("S", "dyy", [(lambda a=a: T.yy[:, a:a + 436], lambda: T.m128[:]) for a in range(0, 1744, 436)], [ap("yy", 0, 1)], [full("m128")], 3000.0)
             DMA("G", "gyy", [(lambda: T.yy[:, 0:1744], lambda: T.yf[:, 16:1760])], [ap("yy", 0, 1)], [full("yf")], 4000.0)
         for j in range(4):
@@ -549,13 +560,13 @@ def build(T, send, est=EST[0]):
             else:
                 ACT(ap("st", 4 * S * j, 4 * S * (j + 1)), ps(j, 0, 4 * S), AF.Relu, bias=DB)
         if not last:
-            doubled(0); doubled(1)
+            for a, b in GK:
+                ACT(w16("rr", a, b), w16(yn, a, b, yo), scale=2.0, bias=-256.0)
             lv = ps(4, 384, 384 + K)
             MM(lv, [(blk, k("k12"))] + wrap("z4k", yn, yo, K))
             ACT(k("sgl"), lv, AF.Sign, acc=ACC)
-            lists(t + 1, 0, 5)
-            MM(ps(5, 500, 501), [(full("blkh"), ACC)])
-            ACT(TM2, ps(5, 500, 501), bias=SLC)
+            MM(ps(4, 500, 501), [(full("blkh"), ACC)])
+            ACT(TM2, ps(4, 500, 501), bias=SLC)
         stw = ap("st", 0, 16 * S)
         hs = [0, HS, 2 * HS, (2 * HS + W) // 4 * 2, W]
         for j in range(4):
@@ -565,16 +576,16 @@ def build(T, send, est=EST[0]):
             cd = ps(2 if a else 3, a, b)
             MM(cd, wrap("zs", "sg", 16 * a, b - a))
             TT(ap("ne", a, b), cd, ap("ri", a, b), OP.not_equal)
+            TS(ap("kbs", a, b), cd, 0.0, OP.is_gt)
             TT(ap("mv", a, b), cd, ap("ne", a, b), OP.is_ge)
-            ACT(ap("kbs", a, b), cd, AF.Sign)
 
         def held(m, a=0, b=P):
-            return [(m[1], ap("mv", a, b)), (m[2], ap("kbs", a, b))], [(m[0], ap("mv", a, b))]
+            return [(m[1], ap("mv", a, b)), (m[0], ap("kbs", a, b))], [(m[0], ap("mv", a, b))]
         for a, b in parts:
             lc = [] if last else [(full("ihf"), ap("lc", a, b))]
-            x = held([full(n) for n in ("b64", "nb64", "b32")], a, b)
+            x = held([full(n) for n in ("b64", "nb64")], a, b)
             nmb = 1 if a else 0
-            MMS([(ps(nmb, 2 * a, a + b), lc + [(idn, ap("nx5", a, b))] + x[0]), (ps(nmb, a + b, 2 * b), lc + x[1])])
+            MMS([(ps(nmb, 2 * a, a + b), lc + [(full("i1k"), ap("nex", P * t + a, P * t + b))] + x[0]), (ps(nmb, a + b, 2 * b), lc + x[1])])
             if last:
                 ACT(ap("nm", 2 * a, 2 * b), ps(nmb, 2 * a, 2 * b), AF.Relu, bias=-1023.0)
             else:
@@ -585,6 +596,7 @@ def build(T, send, est=EST[0]):
         if not last:
             TS(Q, NB, C12, OP.subtract, -1.0 / 32, OP.mult)
             TS(THR, Q, -32.0, OP.mult, C13, OP.add)
+            lists(t + 1, 0, 0)
             MM(ps(1, 400, 424), pairs("zs", "sg", 16 * P))
             ACT(sm(0, 24), ps(1, 400, 424), AF.Relu, scale=4096.0 * 256, bias=-6144.0)
             ACT(sm(24, 24), ps(1, 400, 424), scale=256.0, bias=OWB[t])
@@ -593,16 +605,15 @@ def build(T, send, est=EST[0]):
             CP(full("ou"), full("own"))
         cols = lambda terms, a, b: [(l, ap(x["n"], x["a"] + a, x["a"] + b)) for l, x in terms]
         made = lambda a, b: [(n4k, ap("nm", 2 * a, a + b)), (n4k, ap("nm", a + b, 2 * b))]
-        for a, b in (parts if last else [(0, P)]):
-            x = held([i4k, n4k, i2k], a, b)
-            MMS([(ps(1, a, b), [(idn, ap("mone", a, b)), (i2k, ones(b - a))] + x[0]), (ps(1, P + a, P + b), [(idn, ap("mone", a, b))] + x[1])])
-            for h in (0, 1):
-                TT(ap("rk", P * h + a, P * h + b), ps(1, P * h + a, P * h + b), ap("old", a, b), OP.min)
-        tvb = (4, 6) if last else (0, 1)
-        tvs = [[(idn, full("nba")), (idn, full("nbb")), (full("t4" if h else "t2"), full("mone"))] + x
-               for h, x in enumerate(held([full(n) for n in ("t4", "nt4", "t2")]))]
+        tvb, rkb = ((4, 6), 7) if last else ((2, 3), 3)
+        tvs = [[(idn, full("nba")), (idn, full("nbb")), (full("t4"), full("mone"))] + x for x in held([full("t4"), full("nt4")])]
 
-        def slots():
+        def slots(last=last, UC=UC, tvb=tvb, rkb=rkb, tvs=tvs):
+            for a, b in (parts if last else [(0, P)]):
+                x = held([i4k, n4k], a, b)
+                MMS([(ps(rkb, a, b), [(idn, ap("mone", a, b))] + x[0]), (ps(rkb, P + a, P + b), [(idn, ap("mone", a, b))] + x[1])])
+                for h in (0, 1):
+                    TT(ap("rk", P * h + a, P * h + b), ps(rkb, P * h + a, P * h + b), ap("old", a, b), OP.min)
             if not last:
                 for h in (0, 1):
                     MMS([(ps(tvb[h], a, b), cols(tvs[h], a, b) + made(a, b)) for a, b in parts])
@@ -635,7 +646,7 @@ def build(T, send, est=EST[0]):
                 TT(ee(h, K, K + 12), ny, sm(64 + 16 * h, 12), OP.min)
             ACT(ap("sgl", K, K + 12), ny, AF.Sign, bias=-4096 * 175.5)
             lists(t + 1, 1, 1)
-            slots()
+            deferred.append(slots)
     return ops
 
 
@@ -708,12 +719,12 @@ def place(eng, cost, succ, left0, prio):
 ORDER = {}
 
 
-def schedule(ops, wake=150.0, tries=15000, seed=1, heat=60.0):
+def schedule(ops, tries=1200, seed=1, starts=6, heat=60.0, windows=2400, moves=200, slack=40.0):
     n = len(ops)
     if n in ORDER:
         return ORDER[n][0]
     eng, cost = [o["e"] for o in ops] + ["X"], [o["c"] + 1.0 for o in ops] + [1.0]
-    arcs = [[(j, ops[j]["lat"] + (wake if w else 0.0)) for j, w in o["dep"].items()] for o in ops]
+    arcs = [[(j, ops[j]["lat"] * LAG[0][0] + (LAG[0][1] if w else 0.0)) for j, w in o["dep"].items()] for o in ops]
     via, bwd = [dict() for _ in ops], []
     for i, a in enumerate(arcs):
         bwd.append([(j, d) for j, d in a if not any(x != j and via[x].get(j, -1e9) + cost[x] + e >= d for x, e in a)])
@@ -722,11 +733,14 @@ def schedule(ops, wake=150.0, tries=15000, seed=1, heat=60.0):
             for y, e in arcs[j]:
                 via[i][y] = max(via[i].get(y, 0.0), e + cost[j] + d)
     ends = set(range(n)) - {j for a in bwd for j, _ in a} | {i for i, o in enumerate(ops) if o["lat"]}
-    bwd.append([(i, ops[i]["lat"]) for i in sorted(ends)])
-    fwd = [[] for _ in range(n + 1)]
-    for i, a in enumerate(bwd):
-        for j, d in a:
-            fwd[j].append((i, d))
+    bwd.append([(i, ops[i]["lat"] * LAG[0][0]) for i in sorted(ends)])
+    bwds = [[[(j, ops[j]["lat"] * f + (w if i < n and ops[i]["dep"][j] else 0.0)) for j, _ in a] for i, a in enumerate(bwd)] for f, w in LAG]
+    fwds = [[[] for _ in range(n + 1)] for _ in LAG]
+    for bw, fw in zip(bwds, fwds):
+        for i, a in enumerate(bw):
+            for j, d in a:
+                fw[j].append((i, d))
+    fwd = fwds[0]
     left, right = [len(a) for a in bwd], [len(f) for f in fwd]
 
     def packed(a):
@@ -738,11 +752,11 @@ def schedule(ops, wake=150.0, tries=15000, seed=1, heat=60.0):
 
     def worth(a):
         order, total = sorted(range(n + 1), key=lambda i: a[i]), a[n]
-        for e, c in zip(EST[1:], others):
+        for e, c, bw in zip(EST[1:], others, bwds[1:]):
             fin, free = [0.0] * (n + 1), dict.fromkeys("VAPGSX", 0.0)
             for i in order:
                 s = free[eng[i]]
-                for j, d in bwd[i]:
+                for j, d in bw[i]:
                     if fin[j] + d > s:
                         s = fin[j] + d
                 fin[i] = free[eng[i]] = s + c[i]
@@ -753,10 +767,13 @@ def schedule(ops, wake=150.0, tries=15000, seed=1, heat=60.0):
     for i in range(n - 1, -1, -1):
         rank[i] = cost[i] + max(rank[j] + d for j, d in fwd[i])
     rng = np.random.RandomState(seed)
-    cur = best = packed(place(eng, cost, fwd, left, [-r for r in rank]))
-    tight, now = None, worth(cur)
-    least = now
-    for it in range(tries):
+    first = packed(place(eng, cost, fwd, left, [-r for r in rank]))
+    found = []
+    for it in list(range(tries)) * starts:
+        if it == 0:
+            cur = best = first
+            tight, now = None, worth(cur)
+            least = now
         if tight is None:
             stop = {(eng[i], round(cur[i] + cost[i], 3)): i for i in range(n)}
             tight, i = [], n
@@ -797,7 +814,94 @@ def schedule(ops, wake=150.0, tries=15000, seed=1, heat=60.0):
                 cur, now, tight = new, w, None
                 if now < least:
                     best, least = cur, now
-    ORDER[n] = (sorted(range(n), key=lambda i: (best[i], i)), best)
+        if it == tries - 1:
+            found.append(best)
+    costs, share = [cost] + others, [EST[0][0] / e[0] for e in EST]
+
+    def run(c, seq, fin, free, bw=bwd):
+        for i in seq:
+            s = free[eng[i]]
+            for j, d in bw[i]:
+                if fin[j] + d > s:
+                    s = fin[j] + d
+            fin[i] = free[eng[i]] = s + c[i]
+
+    def polish(order, windows):
+        for it in range(windows):
+            anew(order, slack * (1.0 - it / windows))
+        fin = [0.0] * (n + 1)
+        run(cost, order, fin, dict.fromkeys("VAPGSX", 0.0))
+        return [fin[i] - cost[i] for i in range(n + 1)]
+
+    def anew(order, heat):
+        many = (40, 70, 110)[rng.randint(3)]
+        lo = rng.randint(-many // 2, n - many // 2)
+        lo, hi = max(0, lo), min(n, lo + many)
+        win, state = order[lo:hi], []
+        inside = {x: k for k, x in enumerate(win)}
+        for c, bw, fw in zip(costs, bwds, fwds):
+            fin, free = [0.0] * (n + 1), dict.fromkeys("VAPGSX", 0.0)
+            run(c, order[:lo], fin, free, bw)
+            tail, nxt = [0.0] * (n + 1), dict.fromkeys("VAPGSX", 0.0)
+            for i in order[:hi - 1:-1]:
+                s = nxt[eng[i]]
+                for j, d in fw[i]:
+                    if tail[j] + d > s:
+                        s = tail[j] + d
+                tail[i] = nxt[eng[i]] = s + c[i]
+            base = max([fin[j] + d + tail[i] for i in order[hi:] for j, d in bw[i] if j not in inside] + [0.0])
+            out = {x: max([d + tail[j] for j, d in fw[x] if j not in inside] + [0.0]) for x in win}
+            state.append((c, fin, free, nxt, base, out, bw))
+
+        def value(seq, m):
+            total, head, rest = 0.0, seq[:m], seq[m:]
+            for w, (c, fin, free, nxt, base, out, bw) in zip(share, state):
+                f = dict(free)
+                for x in head:
+                    f[eng[x]] = fin[x]
+                run(c, rest, fin, f, bw)
+                total += w * max(base, max([fin[x] + out[x] for x in seq]), max([f[e] + nxt[e] for e in f]))
+            return total
+        pred = {x: [j for j, _ in bwd[x] if j in inside] for x in win}
+        succ = {x: [j for j, _ in fwd[x] if j in inside] for x in win}
+        seq, pos, clean = win, inside, len(win)
+        now = value(seq, 0)
+        draw = rng.uniform(size=(moves, 2)).tolist()
+        room = (rng.exponential(size=moves) * heat).tolist()
+        for (u, v), z in zip(draw, room):
+            p = int(u * len(seq))
+            k = seq[p]
+            a, b = max([pos[j] + 1 for j in pred[k]] + [0]), min([pos[j] - 1 for j in succ[k]] + [len(seq) - 1])
+            same = [q for q in range(a, b + 1) if q != p and eng[seq[q]] == eng[k]]
+            if not same:
+                continue
+            q = same[int(v * len(same))]
+            new = seq[:p] + seq[p + 1:]
+            new.insert(q, k)
+            w = value(new, min(p, q, clean))
+            if w <= now + z:
+                seq, now, clean = new, w, len(win)
+                pos = {x: y for y, x in enumerate(seq)}
+            else:
+                clean = min(p, q)
+        order[lo:hi] = seq
+        fin = [0.0] * (n + 1)
+        run(cost, order, fin, dict.fromkeys("VAPGSX", 0.0))
+        order.sort(key=lambda i: fin[i] - cost[i])
+
+    by_start = lambda a: sorted(range(n + 1), key=lambda i: (a[i], i))
+    found = [polish(by_start(a), windows // 8) for a in found]
+    marks = [0] + [i for i, o in enumerate(ops) if o["e"] == "X"] + [n]
+    prio, base = [0.0] * (n + 1), 0.0
+    for a, b in zip(marks, marks[1:]):
+        x = min(found, key=lambda s: s[b] - (s[a] if a else 0.0))
+        for i in range(a, b + 1):
+            prio[i] = x[i] - (x[a] if a else 0.0) + base
+        base = prio[b]
+    found.append(polish(by_start(place(eng, cost, fwd, left, prio)), windows // 8))
+    order = by_start(min(found, key=worth))
+    best = polish(order, windows)
+    ORDER[n] = (order[:n], best)
     return ORDER[n][0]
 
 

import numpy as np
from concourse.bass import DstId, RemoteDMATransfer
from concourse.mybir import AluOpType as OP, ActivationFunctionType as AF

V0, B0, P, RO = 384, 1360, 192, 3
THETA, DELTA = (460, 560, 520), (9, 7, 10)
FAR = 960
U0 = 208
HD, KON = 1024, 1008
PB = 1200
WB = [PB - 400 * (t + 1) for t in range(RO)]
YO = [PB + 2016, PB + 2016 + 1376, PB + 2016 + 1376 + 1568]
GW = (64, 48)
BF, F32, I32, U16 = "bfloat16", "float32", "int32", "uint16"
ZZ = {n: 144 * i for i, n in enumerate("z4k z01 zs z1 z8k zi zc zn8 z16k".split())}


def _scratch():
    s = {}
    for names, cols, d in (
        ("tb", YO[2] + 1744, BF), ("inf", PB + 976, BF), ("dzt", 976, BF),
        ("y0r", 1360, BF), ("xx dlb", 960, BF), ("nex", 576, BF), ("rr az dz gz nw zt d0 d1 ab0 ab1 ab2 ab3 i0", 1744, BF),
        ("m128", 436, BF), ("c128", 272, BF), ("one2 half", 512, BF),
        ("nc zero c192", 768, BF), ("cum", 784, BF), ("fl wd", 1024, BF), ("iov", 976, BF), ("iof", 976, F32),
        ("st yf i1", 1760, BF), ("sg", 3264, BF), ("bm", 2048, BF),
        ("sb0 sb1 sb2 nm", 384, BF), ("zz", 144 * len(ZZ), BF), ("gm", 8, BF),
        ("blk idn nidn ihf i63 i4k n4k i1k ic n64 i2 id0 ie0 id1 ie1 id2 ie2 tri t4 nt4 ms b64 nb64 nblk nd8 "
         "e01 ne01 e0a e0b e1 idl nidl idl0 nidl0", 128, BF),
        ("idf blkh sf", 128, F32),
        ("k12 cp sgl sw far unt mine th tj c208 c1k", 112, BF), ("k3", 16, BF),
        ("bl", 1168, F32), ("bli", 384, I32), ("enb", 1360, I32), ("ent", 256, I32), ("entf et", 256, F32),
        ("sndi", 12, I32), ("col", 32, F32), ("coli", 8, I32), ("oh", 16, F32), ("sm", 96, F32),
        ("jw swf fa araw r0 r1", 112, F32), ("jt", 48, F32), ("own", 24, F32), ("pbc", 336, F32),
        ("ee c1 mm t45 t01", 224, F32), ("iv kk", 224, BF), ("ab", 224, I32), ("best", 112, I32), ("gu", 448, U16), ("ix", 224, U16),
        ("old", 204, F32), ("hib", 204, BF), ("ox", 204, U16), ("tg", 48, U16), ("dlu su", 12, U16), ("ou", 24, U16),
        ("hg lg lc ri ne mv kbs nba nbb mone eo my", 192, BF), ("vn tv", 192, F32), ("rk", 384, F32),
    ):
        for n in names.split():
            s[n] = ("sbuf", [128, cols], d)
    s["ps"] = ("psum", [128, 4096], F32)
    return s


SHAPES = _scratch()
PART = {n: (b, 128 * i) for b, d in (("fw", F32), ("mw", BF))
        for i, n in enumerate(n for n, s in SHAPES.items() if s[1][1] == 128 and s[2] == d)}
SCRATCH = {n: s for n, s in SHAPES.items() if n not in PART}
SCRATCH.update({b: ("sbuf", [128, 128 * sum(1 for x in PART.values() if x[0] == b)], d) for b, d in (("fw", F32), ("mw", BF))})
SEMAPHORES = ["qv", "qa", "qp", "qg", "sent", "arr0", "arr1", "arr2", "dy", "dx", "denb", "dsnd", "dbl", "dent", "dout", "dz", "dz2",
              "dyy", "gyy", "gy0", "dy0", "gwd", "dd0", "dd1", "dd2"]
QSEM = {"V": "qv", "A": "qa", "P": "qp", "G": "qg"}
EST = ((0.92, 1.45, 3.8), (0.83, 1.2, 2.5), (1.12, 1.85, 4.5))
LAG = ((0.9, 135.0), (0.65, 115.0), (1.1, 150.0))
HALF = (1, 2)
HS = 64
ONV = ((0, 0),)
RELU = ()


def ap(n, a, b, s=1, p=(0, 128, 1)):
    if n in PART:
        n, a, b = PART[n][0], a + PART[n][1], b + PART[n][1]
    return {"n": n, "a": a, "b": b, "s": s, "p": p}


def ind(win, off):
    return {"win": win, "off": off}


def ps(bank, a, b, p=(0, 128, 1)):
    return ap("ps", 512 * bank + a, 512 * bank + b, 1, p)


def width(x):
    if "win" in x:
        return 16 * (x["off"]["b"] - x["off"]["a"])
    return (x["b"] - x["a"] + x["s"] - 1) // x["s"]


def size(x):
    x = x.get("win", x)
    return 2 if SCRATCH[x["n"]][2] in (BF, U16) else 4


def build(T, send, est=EST[0]):
    ops = []
    CYC, GAT, SCA = est
    PEC = CYC / 2

    def real(x):
        if not isinstance(x, dict):
            return x
        if "win" in x:
            return real(x["win"]).indirect(real(x["off"]))
        p = x["p"]
        return T[x["n"]][p[0]:p[1]:p[2], x["a"]:x["b"]:x["s"]]

    def add(eng, fn, outs, ins, cost, lat=0.0, sem=None, inc=1):
        w, r = [], []
        for x in ins:
            if isinstance(x, dict):
                r += [x["win"], x["off"]] if "win" in x else [x]
        for o in outs:
            if "win" in o:
                w.append(o["win"]); r.append(o["off"])
            else:
                w.append(o)
        ops.append({"e": eng, "fn": fn, "w": w, "r": r, "c": cost, "lat": lat, "sem": sem, "inc": inc})

    def vcost(out, ins, two=False):
        k = 0.5 if all(size(x) == 2 for x in [out] + ins) else 1.0
        if "win" in out:
            k = SCA
        elif "win" in ins[0]:
            k = GAT
        elif two and all(x["n"] != "ps" for x in ins):
            k *= 2
        return (60 + width(ins[0]) * k) * CYC

    def TS(out, x, s1, o1, s2=None, o2=None):
        if o2 is None:
            fn = lambda g: g.vector.tensor_scalar(real(out), real(x), real(s1), None, o1)
        else:
            fn = lambda g: g.vector.tensor_scalar(real(out), real(x), real(s1), real(s2), o1, o2)
        add("V", fn, [out], [x, s1, s2], vcost(out, [x]))

    def TT(out, x, y, o):
        add("V", lambda g: g.vector.tensor_tensor(real(out), real(x), real(y), o), [out], [x, y], vcost(out, [x, y], True))

    def CP(out, x):
        add("V", lambda g: g.vector.tensor_copy(real(out), real(x)), [out], [x], vcost(out, [x]))

    def MS(out, c):
        add("V", lambda g: g.vector.memset(real(out), c), [out], [], vcost(out, [out]))

    def ACT(out, x, f=AF.Identity, scale=1.0, bias=0.0, acc=None):
        def fn(g):
            if acc is None:
                return g.scalar.activation(real(out), real(x), f, bias=real(bias), scale=scale)
            return g.scalar.activation(real(out), real(x), f, bias=bias, scale=scale, accum_out=real(acc))
        add("A", fn, [out] + ([acc] if acc else []), [x, bias], (80 + width(x) * (GAT if "win" in x else 1.0)) * CYC + (100 if acc else 0))

    def MMS(groups, fresh=True, done=True):
        def fn(g):
            for out, terms in groups:
                for i, (l, r) in enumerate(terms):
                    last = g.tensor.matmul(real(out), real(l), real(r), fresh and i == 0, done and i == len(terms) - 1)
            return last
        add("P", fn, [o for o, _ in groups], [x for _, ts in groups for t in ts for x in t],
            60 + sum(max(64, width(r)) * (size(r) - 1 + size(r) // 4) for _, ts in groups for _, r in ts) * PEC)

    def MM(out, terms):
        MMS([(out, terms)])

    def TR(o, x, i):
        add("P", lambda g: g.tensor.transpose(real(o), real(x), real(i)), [o], [x, i], 300)

    def full(n):
        return ap(n, 0, SHAPES[n][1][1])

    def wrap(z, n, a, k):
        return [(ap("zz", ZZ[z] + 15 - r, ZZ[z] + 143 - r), ap(n, a + r, a + 16 * k, 16)) for r in range(16)]

    def pairs(z, n, a):
        return [(ap("zz", ZZ[z] + 15 - r, ZZ[z] + 143 - r), ap(n, a + r // 2, a + 192, 8)) for r in range(16)]

    def DMA(eng, sem, copies, outs, ins, lat=1900.0):
        def fn(g):
            for o, i in copies:
                if eng == "G":
                    g.dma_start(o(), i(), accum_op=OP.add).then_inc(T.sem[sem], 16)
                else:
                    (g.scalar if eng == "A" else g.sync).dma_start(o(), i()).then_inc(T.sem[sem], 16)
            return None
        add(eng, fn, outs, ins, (1000.0 if eng == "G" else 60.0) * len(copies), lat, sem, 16 * len(copies))

    def IOTA(out, pat, base, cm, t=None):
        if SCRATCH[out["n"]][2] != I32:
            fn = lambda g: g.iota(real(out), pat, base, cm, allow_small_or_imprecise_dtypes=True)
        else:
            fn = lambda g: g.iota(real(out), pat, base, cm)
        add("G", fn, [out], [] if t is None else [ap("sent", t, t + 1)], 130 + 2 * width(out) * CYC)

    def SEL(out, x, pat, o, base, cm):
        add("G", lambda g: g.affine_select(real(out), real(x), pat, o, 0.0, base, cm), [out], [x], 170 + 2 * width(out) * CYC)

    EYE = [([[-1, 128]], OP.is_equal, 0, 1)]
    BLK = [([[-16, 8], [0, 16]], OP.is_ge, 0, 1), ([[16, 8], [0, 16]], OP.is_ge, 15, -1)]

    def scaled(n, rules, c, t=0):
        IOTA(full(n), [[0, 128]], c, 0, t)
        for pat, o, base, cm in rules:
            SEL(full(n), full(n), pat, o, base, cm)

    col = lambda i: ap("col", i, i + 1)
    sm = lambda a, n: ap("sm", a, a + n)
    (R16, C256, R2, THR, LP, NB, SLC, C12, C13, BASE, WI, WC, K12, PAR, TMP, VNB, ALC, LT8, WS, DB, TM2, ACC) = [col(i) for i in range(22)]
    OWB = [col(24 + t) for t in range(2)]
    oh = lambda r: ap("oh", r, r + 1)
    Q = ap("coli", 2, 3)
    blk, idn, nidn, idf, i4k, n4k = [full(n) for n in ("blk", "idn", "nidn", "idf", "i4k", "n4k")]
    ones = lambda n: ap("one2", 0, n)
    ecol = lambda r: 128 * (r % 2) + 16 * (r // 2)
    ee = lambda h, a, b: ap("ee", 112 * h + a, 112 * h + b)
    w16 = lambda n, a, b, o=0: ap(n, o + 16 * a, o + 16 * b)

    DMA("S", "dy", [(lambda: T.y0r[:], lambda: T.y0[:])], [full("y0r")], [], 2800.0)
    DMA("S", "dx", [(lambda: T.xx[:, 0:V0], lambda: T.x0[:])], [ap("xx", 0, V0)], [], 2400.0)
    DMA("S", "dent", [(lambda r=r: T.ent[0:85, ecol(r):ecol(r) + 16], lambda r=r: T.en0[r, :]) for r in range(16)], [full("ent")], [], 3000.0)
    DMA("S", "dsnd", [(lambda: T.sndi[:], lambda: T.snd[:])], [full("sndi")], [])
    MS(full("enb"), 0)
    DMA("A", "denb", [(lambda h=h: T.enb[h:128:16, :], lambda h=h: T.en0[h:16:2, :]) for h in (0, 1)], [full("enb")], [], 2400.0)

    MS(ones(512), 1.0)
    IOTA(ap("coli", 0, 1), [[0, 1]], 0, 1)
    SEL(full("gm"), ones(8), [[-16, 8]], OP.is_ge, 0, 1)
    SEL(full("gm"), full("gm"), [[16, 8]], OP.is_ge, 15, -1)
    SEL(blk, ones(128), *BLK[0])
    SEL(blk, blk, *BLK[1])
    SEL(idn, ones(128), *EYE[0])
    IOTA(ap("iof", 0, 208), [[1, 208]], 0, 0)
    SEL(full("e01"), ones(128), [[-16, 8], [200, 16]], OP.is_equal, -200, 1)
    IOTA(ap("iof", 208, 592), [[1, 384]], 208, 0)
    TS(ap("coli", 1, 2), ap("coli", 0, 1), 15, OP.bitwise_and)
    CP(R16, ap("coli", 1, 2))
    TS(full("oh"), ap("iof", 0, 16), R16, OP.is_equal)
    TS(C256, R16, -256.0, OP.mult)
    TS(R2, R16, 2.0, OP.is_lt)
    TS(LT8, R16, 8.0, OP.is_lt)
    ACT(TMP, oh(0), scale=-240.0)
    ACT(BASE, oh(3), scale=255.0, bias=TMP)
    ACT(WI, oh(1), scale=1.0 / 4096, bias=oh(0))
    ACT(WC, oh(3), scale=4.0, bias=oh(0))
    ACT(WS, LT8, scale=1.0 / 1024, bias=-1.0 / 2048)
    TS(ap("coli", 3, 4), ap("coli", 0, 1), 1, OP.bitwise_and)
    TS(PAR, ap("coli", 3, 4), float(HD), OP.mult)
    MS(full("zz"), 0.0)
    for z, c in (("z4k", 4096.0), ("z01", R2), ("zs", WS), ("z1", 1.0), ("z8k", 8192.0), ("zc", WC), ("zn8", -8192.0), ("z16k", 16384.0)):
        TS(ap("zz", ZZ[z] + 15, ZZ[z] + 143, 16), full("gm"), c, OP.mult)
    TS(ap("zz", ZZ["zi"] + 15, ZZ["zi"] + 143, 16), full("gm"), WI, OP.mult, 1.0 / HD, OP.mult)
    MS(ap("e0a", 0, 256), 0.0)
    for n, r, c in (("e0a", 0, 16.0), ("e0a", 3, -255.0 / 16), ("e0b", 0, -255.0 / 16), ("e0b", 3, 255.0 / 16)):
        TS(ap(n, r, 128, 16), full("gm"), c, OP.mult)
    for n, s, c in (("idf", idn, 1.0), ("blkh", blk, 0.5), ("ne01", full("e01"), -1.0), ("idl0", idn, DELTA[0]),
                    ("nidl0", idn, -DELTA[0]), ("nidn", idn, -1.0), ("i4k", idn, 4096.0),
                    ("id0", idn, 400.0), ("ie0", idn, 400.0 + HD)):
        ACT(full(n), s, scale=float(c))

    def digits(a, b):
        ACT(ap("iov", a, b), ap("iof", a, b), AF.Relu, bias=C256)
        TS(ap("iov", a, b), ap("iov", a, b), 256.0, OP.min)
    digits(16, 592)
    TS(full("jw"), ap("iof", 0, 112), 16.0, OP.mult, R16, OP.add)
    ACT(full("jt"), ap("jw", 0, 48), bias=float(U0))
    for a, b in ((0, 112), (224, 288)):
        IOTA(ap("pbc", a, b), [[0, b - a]], KON, 0)
    IOTA(full("best"), [[0, 112]], 0, 0)
    MS(full("zero"), 0.0)
    ACT(full("c192"), full("zero"), bias=192.0)
    MS(ap("cum", 0, 16), 0.0)
    fills = [("tb", PB, PB + U0), ("tb", PB + U0 + V0, PB + 976), ("tb", PB + HD, PB + HD + U0), ("inf", WB[0], PB + U0),
             ("dzt", 0, U0)]
    MS(ap("tb", WB[0], WB[0] + 16), 0.0)
    for t in range(RO):
        MS(ap("i1", B0 + P * t, B0 + P * t + 16), 0.0)
    later = [("inf", 0, WB[1]), ("inf", WB[1], WB[0]), ("tb", PB + HD + U0 + V0, YO[0]), ("yf", 0, 16)]
    later += [("tb", a, a + 16) for t in (1, 2) for a in (WB[t], YO[t] - 16)]

    def zeros(sem, fl, more=()):
        DMA("S", sem, [(lambda n=n, a=a, b=b: T[n][:, a:b], lambda a=a, b=b: T.zero[:, 0:b - a]) for n, a, b in fl],
            [ap(n, a, b) for n, a, b in fl], [full("zero")] + list(more), 2600.0)
    zeros("dz", fills)
    MS(ap("tb", PB + 976, PB + HD), 128.0)
    for n, a, c in (("sgl", 85, 1), ("sw", 85, 0), ("far", 85, 0), ("swf", 85, 0), ("fa", 85, 0), ("c1k", 0, 1024), ("unt", 85, 0)):
        IOTA(ap(n, a, 112), [[0, 112 - a]], c, 0)
    for h in (0, 1):
        IOTA(ee(h, 85, 112), [[0, 27]], 0, 0)
    MS(ap("cp", 0, 1), 0.0)

    def late_constants():
        landed = ap("tb", WB[0] + 16, WB[0] + 400)
        zeros("dz2", later, [landed])
        DMA("S", "dbl", [(lambda: T.bli[:], lambda: T.bl0[:])], [full("bli")], [landed])
        CP(ap("bl", U0, U0 + V0), full("bli"))
        for n, a, b, c in (("c128", 0, 272, 128), ("bl", 0, U0, -1), ("k3", 0, 16, -524288), ("mone", 0, 192, -1)):
            IOTA(ap(n, a, b), [[0, b - a]], c, 0, 0)
        DMA("S", "dy0", [(lambda a=a: T.tb[:, YO[0] + a:YO[0] + a + 272], lambda: T.c128[:]) for a in range(0, B0, 272)],
            [ap("tb", YO[0], YO[0] + B0)], [full("c128"), landed])
        DMA("G", "gy0", [(lambda: T.tb[:, YO[0]:YO[0] + B0], lambda: T.y0r[:])], [ap("tb", YO[0], YO[0] + B0)], [full("y0r")], 4000.0)
        DMA("G", "gwd", [(lambda: T.wd[:], lambda: T.y0r[:, 0:1024])], [full("wd")], [ap("y0r", 0, 1024), landed], 4000.0)
        IOTA(ap("iof", 592, 976), [[1, 384]], 592, 0, 0)
        IOTA(full("nba"), [[1, P]], B0 % 64, 0, 0)
        ACT(full("ri"), ap("iof", 2, P + 2), scale=1.0 / 256)
        IOTA(full("half"), [[0, 512]], 1, 0, 0)
        SEL(full("half"), full("half"), [[0, 32], [-1, 16]], OP.is_ge, 7, 0)
        for r in range(0, 16, 4):
            SEL(ap("bm", 128 * r, 128 * r + 512), full("half"), [[-1, 4], [-16, 8], [0, 16]], OP.is_equal, -r, 1)
        for n, c in (("n4k", -4096), ("n64", -64), ("id1", 800), ("ie1", 800 + HD)):
            scaled(n, EYE, c)
        for n, c in (("b64", 64.0), ("nb64", -64.0), ("nblk", -1.0)):
            ACT(full(n), blk, scale=c)
        scaled("nd8", BLK + [([[0, 8], [1, 16]], OP.is_ge, -8, 0)], -4096)
        SEL(full("tri"), blk, [[1, 128]], OP.is_gt, 0, -1)
        TT(full("tri"), full("tri"), idn, OP.subtract)
        for n, c in (("t4", 4096.0), ("nt4", -4096.0)):
            ACT(full(n), full("tri"), scale=c)
        for n, c in (("i1k", 1024.0), ("i2", 2.0), ("ihf", 0.5), ("i63", 63.75), ("e1", oh(1))):
            TS(full(n), idn, c, OP.mult)
        for t in (0, 1):
            ACT(OWB[t], PAR, bias=U0 + V0 + P * t - 2.0)
        ACT(K12, LT8, scale=-1138944.0)
        ACT(full("k12"), ones(112), scale=256.0, bias=K12)
        ACT(DB, LT8, scale=-4096 * 2223.5, bias=4096 * 2223.5)
        ACT(TMP, oh(0), scale=-float(U0))
        ACT(VNB, oh(1), scale=float(V0 + 2 * P - B0 % 64), bias=TMP)
        digits(592, 976)

    def lists(t, g, bank):
        w, o = GW[g], 256 * g
        a, b = 64 * g, 64 * g + w
        sg = (i4k, ap("sgl", a, b))
        MMS([(ps(bank, o, o + w), [(idf, ee(0, a, b)), (full("id%d" % t), ap("mine", a, b)), sg]),
             (ps(bank, o + w, o + 2 * w), [(idf, ee(0, a, b)), (full("ie%d" % t), ap("mine", a, b)), (idn, ap("far", a, b)), sg]),
             (ps(bank, o + 2 * w, o + 3 * w), [(idf, ee(1, a, b)), sg])])
        TS(ap("gu", o, o + 3 * w), ps(bank, o, o + 3 * w), -4096.0, OP.add)

    MM(ps(6, 0, V0), [(blk, ap("xx", 0, V0))])
    MM(ps(7, 0, 85), wrap("z4k", "y0r", 0, 85))
    ACT(ap("sgl", 0, 85), ps(7, 0, 85), AF.Sign, bias=-4096 * 175.5, acc=ACC)
    MM(ps(7, 96, 97), [(full("blkh"), ACC)])
    TS(Q, ps(7, 96, 97), 8.0 * 85 - 15.5, OP.add, 1.0 / 32, OP.mult)
    TS(LP, ps(7, 96, 97), 8.0 * 85 + THETA[0], OP.add)
    TS(THR, Q, -32.0, OP.mult, LP, OP.add)
    CP(ap("old", P, P + 12), full("sndi"))
    CP(full("su"), full("sndi"))
    TS(full("eo"), ind(full("enb"), full("su")), 384.0, OP.min, -192.0, OP.add)
    MM(ps(3, 0, 24), pairs("z01", "eo", 0))
    TS(full("ou"), ps(3, 0, 24), PAR, OP.add, float(U0), OP.add)
    TS(full("own"), ps(3, 0, 24), PAR, OP.add, float(U0), OP.add)
    p85 = (0, 85, 1)
    CP(ap("entf", 0, 256, 1, p85), ap("ent", 0, 256, 1, p85))
    turn = lambda h: (ap("entf", 128 * h, 128 * h + 128, 1, p85), ap("idf", 0, 85, 1, p85))
    more = (idn, ap("c208", 0, 85))
    MS(ap("c208", 0, 85), float(U0))
    for bank, terms in ((1, [turn(1), more]), (0, [turn(0), more]), (5, [turn(0), turn(1), more, more])):
        MM(ps(bank, 0, 85), terms)
    k0 = lambda n: ap(n, 0, 85)
    TS(k0("sw"), ps(1, 0, 85), float(FAR + U0), OP.is_ge)
    TT(k0("swf"), ps(1, 0, 85), k0("sw"), OP.mult)
    TT(k0("araw"), ps(0, 0, 85), k0("swf"), OP.max)
    ACT(k0("r0"), k0("araw"), AF.Abs, scale=2.0, bias=16.0 - 2 * (FAR + U0))
    TT(ee(1, 0, 85), ps(5, 0, 85), k0("araw"), OP.subtract)
    TS(k0("far"), k0("araw"), float(FAR + U0), OP.is_ge)
    TT(ee(0, 0, 85), k0("araw"), k0("r0"), OP.min)
    TT(k0("fa"), k0("araw"), k0("far"), OP.mult)
    ACT(full("mine"), full("far"), scale=-1.0, bias=1.0)
    MS(ap("kk", 0, 112), 1.0 / HD)
    TS(ap("kk", 112, 224), full("mine"), 1.0 / HD, OP.mult)
    for g in (0, 1):
        lists(0, g, (1, 7)[g])
    TT(k0("fa"), k0("fa"), k0("swf"), OP.subtract)
    TT(full("tj"), full("far"), full("sw"), OP.subtract)
    TT(full("th"), full("tj"), full("sw"), OP.subtract)
    ACT(full("tj"), full("th"), scale=2048.0, bias=3072.0)
    ACT(full("th"), full("th"), scale=2048.0, bias=2048.0)
    for a, b in ((0, 1024), (1024, B0)):
        ACT(ap("rr", a, b), ap("y0r", a, b), scale=2.0)
    ACT(full("fl"), ap("y0r", 0, 1024), scale=0.125, bias=128.5625)
    TS(full("wd"), full("fl"), -8.0, OP.mult, 1029.0, OP.add)

    deferred = []
    for t in range(RO):
        M, C, last = B0 + P * t, V0 + P * t, t == RO - 1
        K, KC, UC = M // 16, C // 16, U0 + C
        S = K + 1
        sb, F = "sb%d" % t, WB[t] + 16
        yn, yo = ("yf", 16) if last else ("tb", YO[t + 1])
        pt = lambda a, b: ap("tb", PB + a, PB + b)
        idl, nidl = (full("idl0"), full("nidl0")) if t == 0 else (full("idl"), full("nidl"))
        GK = [(0, 64), (64, K)]
        wl, wh, wn, wi = pt(0, UC), pt(HD, HD + UC), ap("tb", WB[t], PB + HD + UC), [ap("inf", WB[t], PB + UC), ap("inf", PB, PB + UC)]
        gu = lambda j, g, a, b: ap("gu", 256 * g + GW[g] * j + a - 64 * g, 256 * g + GW[g] * j + b - 64 * g)
        cut = lambda a, b: [(c, min(b, c + 32)) for c in range(a, b, 32)]
        cells = [(0, C // 2), (C // 2, C)] if t in HALF else [(0, C)]
        cps = lambda bank, a, b: ps(bank + (a > 0), 0, b - a)
        k = lambda n, a=0: ap(n, a, a + K)
        for bank in (2, 4):
            MMS([(cps(bank, a, b), [(idn, ap("xx", a, b))]) for a, b in cells], done=False)
        for a, b in cells:
            if t == 0:
                TS(ap("nc", a, b), ps(6, a, b), THR, OP.is_ge)
            else:
                TS(ap("nc", a, b), ps(6, a, b), NB, OP.add, THR, OP.is_ge)
        for a, b in cells:
            o, x, z, i = ap("cum", 16 + a, 16 + b), ap("nc", a, b), ap("c192", a, b), ap("cum", 15 + a, 16 + a)
            add("V", lambda g, o=o, x=x, z=z, i=i: g.vector.tensor_tensor_scan(real(o), real(x), real(z), real(i), OP.add, OP.min),
                [o], [x, z, i], vcost(o, [x, z]))
        now, was = (lambda a, b: ap("cum", 16 + a, 16 + b)), (lambda a, b: ap("cum", 15 + a, 15 + b))
        for a, b in cells:
            MMS([(cps(2, a, b), [(idl, now(a, b)), (nidl, was(a, b))])], fresh=False)
            MMS([(cps(4, a, b), [(nidl, now(a, b)), (idl, was(a, b))])], fresh=False)
        for a, b in cells:
            ACT(pt(U0 + a, U0 + b), cps(4, a, b), AF.Relu)
            TS(pt(HD + U0 + a, HD + U0 + b), cps(2, a, b), 63.0, OP.min)
        ACT(full(sb), ind(pt(0, HD + UC), full("ou")))
        add("G", lambda g, t=t: send(g, t), [ap("sent", t, t + 1)], [full(sb)], 300.0, 0.0, "none")
        add("X", None, [ap("tb", F, F + 384)], [ap("sent", t, t + 1)], 0.0, 4200.0 if t == 0 else 3000.0, "arr%d" % t, 0)
        if t == 0:
            late_constants()
        else:
            deferred.pop()()
        if t == 1:
            IOTA(full("m128"), [[0, 436]], -128, 0, 1)
            for n, c in (("id2", 1200), ("ie2", 1200 + HD)):
                scaled(n, EYE, c, 1)
        for g, (a, b) in enumerate(GK):
            TT(w16("nw", a, b), ind(wl, gu(2, g, a, b)), w16("rr", a, b), OP.subtract)
        TT(ap("dzt", U0, UC), pt(HD + U0, HD + UC), pt(U0, UC), OP.subtract)
        for g, (a, b) in enumerate(GK):
            (CP if (2, g) in ONV else ACT)(w16("zt", a, b), ind(ap("dzt", 0, UC), gu(2, g, a, b)))
        MMS([(ps(6, a, min(C, a + 512)), [(full("e0a"), now(a, min(C, a + 512))), (full("e0b"), was(a, min(C, a + 512)))]) for a in range(0, C, 512)])
        ACT(ap("inf", PB + U0, PB + UC), ps(6, 0, C), AF.Relu, bias=BASE)
        MM(ps(5, 256, 448), [(full("ne01"), ap("tb", F, F + 384, 2)), (full("e01"), ap("tb", F + 1, F + 384, 2))])
        ACT(ap("inf", F, F + 384, 2), ps(5, 256, 448))
        MM(ps(7, 256, 256 + KC), wrap("zc", "inf", PB + U0, KC))
        TT(sm(0, KC), ps(7, 256, 256 + KC), ap("jt", 0, KC), OP.min)
        TS(ap("tg", 0, KC), sm(0, KC), -16.0, OP.add)
        DMA("S", "dd%d" % t, [(lambda: T.dlb[:, 0:P], lambda: T.iov[:, 16:16 + P])] +
            ([(lambda: T.dlb[:, P:960], lambda: T.zero[:, 0:768])] if t == 0 else []), [full("dlb")],
            [ap("iov", 16, 16 + P), full("zero")] + ([ap("tb", F, F + 384)] if t == 0 else []))
        for a in range(0, KC, 12):
            CP(ind(ap("dlb", 0, P + C), ap("tg", a, a + 12)), ap("iov", U0 + 16 * a, U0 + 16 * a + 192))
        MM(ps(7, 320, 332), wrap("z1", "dlb", 0, 12))
        CP(full("dlu"), ps(7, 320, 332))
        if not last:
            ACT(sm(64, 12), ps(7, 320, 332))
            ACT(sm(80, 12), ap("jw", 0, 12), bias=float(UC))
        ACT(ap("old", 0, P), ind(ap("bl", 0, UC), full("dlu")))
        W = P if last else P + 12
        ACT(ap("hib", 0, W), ap("old", 0, W), scale=0.0625, bias=128.53125)
        scaled("sf", EYE, S, t)
        scaled("ms", EYE, -16 * S, t)
        MM(ps(6, 256, 256 + W), [(full("sf"), ap("old", 0, W)), (full("ms"), ap("hib", 0, W)), (idn, ap("hib", 0, W))])
        TS(ap("ox", 0, W), ps(6, 256, 256 + W), 1.0 + 129 * (16 * S - 1), OP.add)
        IOTA(full("nbb"), [[0, P]], M // 64 * 64 - 4096, 0, t)
        ACT(full("hg"), ind(wh, full("dlu")))
        ACT(full("lg"), ind(wl, full("dlu")))
        nex, gap = ap("nex", P * t, P * t + P), [(idn, full("hg")), (nidn, full("lg"))]
        MMS([(ps(7, 0, P), gap)] + ([] if last else [(ps(7, P, 2 * P), [(blk, full("hg")), (full("nblk"), full("lg"))])]))
        ACT(nex, ps(7, 0, P), AF.Relu, scale=-1.0, bias=1.0)
        if last:
            DMA("S", "dout", [(lambda: T.yx[:, 0:768], lambda: T.tb[:, PB + U0:PB + U0 + 768]), (lambda: T.yx[:, 768:960], lambda: T.hg[:])],
                [], [pt(U0, U0 + 768), full("hg")])
        else:
            scaled("idl", EYE, DELTA[t + 1], t)
            scaled("nidl", EYE, -DELTA[t + 1], t)
            ACT(full("lc"), ps(7, P, 2 * P), AF.Sign, bias=-175.5, acc=ALC)
            ACT(SLC, ALC, scale=0.5, bias=8.0 * K + 96 - 15.5)
            C2, sh = C + P, 331 * t
            marks = sorted(set([0, V0, 512, C, C2] + ([1024 - sh] if 1024 - sh < C2 else [])))
            for a, b in zip(marks[:-1], marks[1:]):
                src = pt(U0 + a, U0 + b) if a < C else ap("hg", a - C, b - C)
                y = (a + sh) & 1023
                MM(ps(6, a, b), [(idn, src), (idn, ap("wd", y, y + b - a))] + ([(full("n64"), ap("nex", a - V0, b - V0))] if a >= V0 else []))
            TS(ap("xx", 0, C2), ps(6, 0, C2), 0.0, OP.max, 63.0, OP.min)
            MMS([(ps(6, a, min(C2, a + 512)), [(blk, ap("xx", a, min(C2, a + 512)))]) for a in (0, 512)])
        nb = [0]
        for h in (1, 0):
            for g, (a, b) in enumerate(GK):
                (CP if (h, g) in ONV else ACT)(w16("i%d" % h, a, b), ind(wi[h], gu(2 * h, g, a, b)))

        def sums(g):
            a, b = GK[g]
            for h in (0, 1):
                TT(w16("d%d" % h, a, b), ind(wn, gu(h, g, a, b)), w16("nw", a, b), OP.add)
                if (h, g) in RELU:
                    TS(w16("ab%d" % h, a, b), w16("d%d" % h, a, b), 0.0, OP.max)
                else:
                    ACT(w16("ab%d" % h, a, b), w16("d%d" % h, a, b), AF.Abs)
            for h in (0, 1):
                for c, d in cut(a, b):
                    pp = ps(nb[0] % 2, 0, 16 * (d - c)); nb[0] += 1
                    MM(pp, [(idn, w16("zt", c, d)), (idn, w16("d%d" % h, c, d))])
                    ACT(w16("ab%d" % (2 + h), c, d), pp, AF.Abs)

        def before(parts):
            MM(ps(4, 0, S), wrap("zi", "i1", 0, S))
            MM(ps(4, S, S + K), wrap("zi", "i0", 0, K))
            ACT(ap("iv", 0, S + K), ps(4, 0, S + K))
            scaled("ic", EYE, C + P, t)
            MMS([(ps(4, 0, S), [(idn, ap("iv", 0, S)), (full("ic"), ap("kk", 0, S))]), (ps(4, S, S + K), [(idn, k("iv", S)), (full("ic"), k("kk", 112))])])
            MM(ps(5, 256, 256 + K), [(full("i1k"), k("iv")), (full("i1k"), k("iv", S))])
            ACT(k("unt"), ps(5, 256, 256 + K), AF.Relu, scale=-2.0 ** 23, bias=8192.0)
            for a, b, o in parts:
                w, z = b - a, (288 if a else 112)
                we = w + w % 2
                ACT(ap("pbc", z, z + w), ap("jw", a, b), bias=float(YO[t] - WB[t]))
                MMS([(ps(5, o, o + we), [(idf, ee(1, a, a + we)), (idn, ap("unt", a, a + we))]),
                     (ps(5, o + we, o + we + w), [(idf, ee(0, a, b)), (full("id%d" % t), ap("mine", a, b)), (idn, ap("unt", a, b))])])
                pb = ps(5, o, o + we + w)
                TT(pb, pb, ap("pbc", z - we, z + w), OP.min)

        def choice(g, o):
            a, b = GK[g]
            w = b - a
            we = w + w % 2
            two_far = (full("i2"), ap("far", a, b))
            some = lambda h: ((wrap("zn8", "d%d" % h, 16 * a, w) + wrap("z16k", "ab%d" % h, 16 * a, w)) if (h, g) in RELU
                              else wrap("z8k", "ab%d" % h, 16 * a, w))
            MM(ps(2, 0, w), some(0))
            MM(ps(3, 0, w), [(idn, ap("th", a, b)), two_far] + some(1))
            MM(ps(2, w, 2 * w), [(idn, ap("c1k", a, b))] + wrap("z8k", "ab2", 16 * a, w))
            MM(ps(3, w, 2 * w), [(idn, ap("tj", a, b)), two_far] + wrap("z8k", "ab3", 16 * a, w))
            two = lambda n: ap(n, o, o + we + w)
            ACT(ap("c1", 0, 2 * w), ps(2, 0, 2 * w))
            TT(ap("mm", 0, 2 * w), ps(3, 0, 2 * w), ap("c1", 0, 2 * w), OP.min)
            TT(ap("best", a, b), ap("mm", 0, w), ap("mm", w, 2 * w), OP.min)
            TS(ap("ab", o, o + we), ap("best", a, a + we), HD, OP.bitwise_and)
            TS(ap("ab", o + we, o + we + w), ap("best", a, b), 1, OP.logical_shift_right, HD + 1, OP.bitwise_and)
            TT(two("t45"), ps(5, o, o + we + w), two("ab"), OP.add)
            CP(two("ix"), two("t45"))
            TT(ap("t01", a, b), ps(4, a, b), ap("ab", o, o + w), OP.mult)
            TT(ap("t01", S + a, S + b), ps(4, S + a, S + b), ap("ab", o + we, o + we + w), OP.mult)

        def new_y(parts, g, o):
            a, b = GK[g]
            we = b - a + (b - a) % 2
            for c, d in parts:
                pre = ps(nb[0] % 2, 0, 16 * (d - c)); nb[0] += 1
                MM(pre, [(full("ihf"), w16("tb", c, d, YO[t])), (full("i63"), ones(16 * (d - c)))])
                ACT(w16("az", c, d), ind(ap("tb", WB[t], YO[t] + M), ap("ix", o + we + c - a, o + we + d - a)))
                TT(w16("dz", c, d), ind(pt(0, HD + UC), ap("ix", o + c - a, o + d - a)), w16("az", c, d), OP.subtract)
                ACT(w16("gz", c, d), w16("dz", c, d), AF.Abs, scale=0.5)
                TT(w16(yn, c, d, yo), pre, w16("gz", c, d), OP.add)

        sums(0); before([(0, 64, 0), (64, K, 128)]); sums(1); choice(0, 0); choice(1, 128)
        new_y([(0, 32), (32, 64)], 0, 0); new_y([(64, 88), (88, K)] if K > 96 else [(64, K)], 1, 128)
        MM(ps(5, 256, 256 + K), [(idf, k("t01")), (idf, k("t01", S))])
        TS(k("cp", 1), ps(5, 256, 256 + K), 2.0 - UC, OP.add, 1.0, OP.max)
        for h in (0, 1):
            TT(ee(h, 0, K), ee(h, 0, K), k("t01", S * (1 - h)), OP.max)
        if last:
            pk = (0, K, 1)
            MMS([(ps(6, 0, K), [(idf, ee(1, 0, K)), (i4k, k("sw")), (n4k, ones(K))]),
                 (ps(6, 128, 128 + K), [(idf, ee(0, 0, K)), (n4k, k("far"))])])
            TT(k("araw"), ps(6, 0, K), k("fa"), OP.max)
            TT(k("r0"), ps(6, 128, 128 + K), k("araw"), OP.max)
            TT(k("r1"), ee(1, 0, K), k("swf"), OP.max)
            for h in (0, 1):
                TR(ps(7, 128 * h, 128 * h + 128, pk), k("r%d" % h), idf)
            ACT(ap("et", 0, 256, 1, pk), ps(7, 0, 256, pk), AF.Relu, bias=-float(U0))
            DMA("S", "dout", [(lambda r=r: T.ye[r, 0:1744], lambda r=r: T.et[0:109, ecol(r):ecol(r) + 16]) for r in range(16)], [], [full("et")], 6000.0)
            DMA("S", "dyy", [(lambda a=a: T.yy[:, a:a + 436], lambda: T.m128[:]) for a in range(0, 1744, 436)], [ap("yy", 0, 1)], [full("m128")], 3000.0)
            DMA("G", "gyy", [(lambda: T.yy[:, 0:1744], lambda: T.yf[:, 16:1760])], [ap("yy", 0, 1)], [full("yf")], 4000.0)
        for j in range(4):
            MMS([(ps(j, (r % 4) * S, (r % 4 + 1) * S), [(ap("bm", 128 * r, 128 * r + 128), ap("cp", 0, S)),
                                                         (full("nd8"), ap(yn, yo - 16 + r, yo + M, 16))]) for r in range(4 * j, 4 * j + 4)])
            if j % 2:
                TS(ap("st", 4 * S * j, 4 * S * (j + 1)), ps(j, 0, 4 * S), DB, OP.add, 0.0, OP.max)
            else:
                ACT(ap("st", 4 * S * j, 4 * S * (j + 1)), ps(j, 0, 4 * S), AF.Relu, bias=DB)
        if not last:
            for a, b in GK:
                ACT(w16("rr", a, b), w16(yn, a, b, yo), scale=2.0, bias=-256.0)
            lv = ps(4, 384, 384 + K)
            MM(lv, [(blk, k("k12"))] + wrap("z4k", yn, yo, K))
            ACT(k("sgl"), lv, AF.Sign, acc=ACC)
            MM(ps(4, 500, 501), [(full("blkh"), ACC)])
            ACT(TM2, ps(4, 500, 501), bias=SLC)
        stw = ap("st", 0, 16 * S)
        hs = [0, HS, 2 * HS, (2 * HS + W) // 4 * 2, W]
        for j in range(4):
            (CP if j % 2 else ACT)(w16("sg", hs[j], hs[j + 1]), ind(stw, ap("ox", hs[j], hs[j + 1])))
        parts = [(0, 2 * HS), (2 * HS, P)]
        for a, b in parts:
            cd = ps(2 if a else 3, a, b)
            MM(cd, wrap("zs", "sg", 16 * a, b - a))
            TT(ap("ne", a, b), cd, ap("ri", a, b), OP.not_equal)
            TS(ap("kbs", a, b), cd, 0.0, OP.is_gt)
            TT(ap("mv", a, b), cd, ap("ne", a, b), OP.is_ge)

        def held(m, a=0, b=P):
            return [(m[1], ap("mv", a, b)), (m[0], ap("kbs", a, b))], [(m[0], ap("mv", a, b))]
        for a, b in parts:
            lc = [] if last else [(full("ihf"), ap("lc", a, b))]
            x = held([full(n) for n in ("b64", "nb64")], a, b)
            nmb = 1 if a else 0
            MMS([(ps(nmb, 2 * a, a + b), lc + [(full("i1k"), ap("nex", P * t + a, P * t + b))] + x[0]), (ps(nmb, a + b, 2 * b), lc + x[1])])
            if last:
                ACT(ap("nm", 2 * a, 2 * b), ps(nmb, 2 * a, 2 * b), AF.Relu, bias=-1023.0)
            else:
                ACT(ap("nm", 2 * a, 2 * b), ps(nmb, 2 * a, 2 * b), AF.Relu, bias=-991.5, acc=NB if a else LP)
                if not a:
                    ACT(C12, LP, scale=-1.0, bias=TM2)
                    ACT(C13, C12, bias=THETA[t + 1] + 15.5)
        if not last:
            TS(Q, NB, C12, OP.subtract, -1.0 / 32, OP.mult)
            TS(THR, Q, -32.0, OP.mult, C13, OP.add)
            lists(t + 1, 0, 0)
            MM(ps(1, 400, 424), pairs("zs", "sg", 16 * P))
            ACT(sm(0, 24), ps(1, 400, 424), AF.Relu, scale=4096.0 * 256, bias=-6144.0)
            ACT(sm(24, 24), ps(1, 400, 424), scale=256.0, bias=OWB[t])
            TT(sm(0, 24), sm(0, 24), sm(24, 24), OP.min)
            TT(full("own"), sm(0, 24), full("own"), OP.max)
            CP(full("ou"), full("own"))
        cols = lambda terms, a, b: [(l, ap(x["n"], x["a"] + a, x["a"] + b)) for l, x in terms]
        made = lambda a, b: [(n4k, ap("nm", 2 * a, a + b)), (n4k, ap("nm", a + b, 2 * b))]
        tvb, rkb = ((4, 6), 7) if last else ((2, 3), 3)
        tvs = [[(idn, full("nba")), (idn, full("nbb")), (full("t4"), full("mone"))] + x for x in held([full("t4"), full("nt4")])]

        def slots(last=last, UC=UC, tvb=tvb, rkb=rkb, tvs=tvs):
            for a, b in (parts if last else [(0, P)]):
                x = held([i4k, n4k], a, b)
                MMS([(ps(rkb, a, b), [(idn, ap("mone", a, b))] + x[0]), (ps(rkb, P + a, P + b), [(idn, ap("mone", a, b))] + x[1])])
                for h in (0, 1):
                    TT(ap("rk", P * h + a, P * h + b), ps(rkb, P * h + a, P * h + b), ap("old", a, b), OP.min)
            if not last:
                for h in (0, 1):
                    MMS([(ps(tvb[h], a, b), cols(tvs[h], a, b) + made(a, b)) for a, b in parts])
            for a, b in (parts if last else [(0, P)]):
                if last:
                    for h in (0, 1):
                        MMS([(ps(tvb[h], a, b), cols(tvs[h], a, b))], done=False)
                    for h in (0, 1):
                        MMS([(ps(tvb[h], a, b), made(a, b))], fresh=False)
                TT(ap("tv", a, b), ps(tvb[0], a, b), ap("rk", a, b), OP.max)
                CP(ind(ap("bl", 0, UC), ap("dlu", a // 16, b // 16)), ap("tv", a, b))
                TT(ap("bl", UC + a, UC + b), ps(tvb[1], a, b), ap("rk", P + a, P + b), OP.max)
        MMS([(ps(5 if last else 0, a, b), cols(gap, a, b) + made(a, b)) for a, b in parts])
        if last:
            slots()
            MMS([(ps(5, P + a, P + b), cols([(ap("zz", ZZ["z1"] + 15, ZZ["z1"] + 143), ap("dlb", 0, P)), (full("e1"), full("nba"))], a, b) + made(a, b))
                 for a, b in parts])
            ACT(full("my"), ps(5, 0, P), AF.Relu)
            ACT(full("vn"), ps(5, P, 2 * P), AF.Relu, bias=VNB)
            DMA("S", "dout", [(lambda: T.yy[:, 1744:1936], lambda: T.my[:])], [], [full("my")])
            DMA("S", "dout", [(lambda h=h: T.ye[h:16:2, 1744:1936], lambda h=h: T.vn[h:128:16, :]) for h in (0, 1)], [], [full("vn")])
            DMA("S", "dout", [(lambda: T.yl[:, 768:960], lambda: T.bl[:, U0 + 768:U0 + 960])], [], [ap("bl", U0 + 768, U0 + 960)], 2500.0)
            DMA("S", "dout", [(lambda: T.yl[:, 0:768], lambda: T.bl[:, U0:U0 + 768])], [], [ap("bl", U0, U0 + 768)], 3600.0)
        else:
            TS(ap(yn, yo + M, yo + M + P), ps(0, 0, P), 128.0, OP.add, 128.0, OP.max)
            ACT(ap("rr", M, M + P), ps(0, 0, P), AF.Relu, scale=2.0)
            ny = ps(0, 400, 412)
            MM(ny, [(blk, ap("k3", 0, 12))] + wrap("z4k", yn, yo + M, 12))
            for h in (0, 1):
                TT(ee(h, K, K + 12), ny, sm(64 + 16 * h, 12), OP.min)
            ACT(ap("sgl", K, K + 12), ny, AF.Sign, bias=-4096 * 175.5)
            lists(t + 1, 1, 1)
            deferred.append(slots)
    return ops


def span(x):
    if x["n"] == "ps":
        return x["a"] // 512 * 512, (x["b"] + 511) // 512 * 512
    return x["a"], x["b"]


def depend(ops):
    log = {}
    for i, o in enumerate(ops):
        dep = {}
        for kind, xs in (("r", o["r"]), ("w", o["w"])):
            for x in xs:
                a, b = span(x)
                for (j, kj, aj, bj) in log.get(x["n"], []):
                    if j == i or bj <= a or b <= aj:
                        continue
                    same = ops[j]["e"] == o["e"]
                    if kind == "r" and kj == "r" and (x["n"] != "ps" or same):
                        continue
                    wait = not (x["n"] == "ps" and same and o["e"] == "P")
                    dep[j] = dep.get(j, False) or wait
        for kind, xs in (("r", o["r"]), ("w", o["w"])):
            for x in xs:
                a, b = span(x)
                l = log.setdefault(x["n"], [])
                if kind == "w":
                    l[:] = [e for e in l if not (a <= e[2] and e[3] <= b)]
                l.append((i, kind, a, b))
        o["dep"] = dep


def place(eng, cost, succ, left0, prio):
    n = len(cost)
    left, at, start = list(left0), [0.0] * n, [0.0] * n
    ready = sorted((prio[i], i) for i in range(n) if left[i] == 0)
    busy = {e: [] for e in "VAPGSX"}
    while ready:
        i = ready.pop(0)[1]
        s, b, c = at[i], busy[eng[i]], cost[i]
        x = k = len(b)
        while x > 0 and b[x - 1][1] > s:
            x -= 1
        while x < k and b[x][0] < s + c:
            if b[x][1] > s:
                s = b[x][1]
            x += 1
        b.insert(x, (s, s + c))
        start[i] = s
        s += c
        for j, d in succ[i]:
            if s + d > at[j]:
                at[j] = s + d
            left[j] -= 1
            if left[j] == 0:
                m = (prio[j], j)
                lo, hi = 0, len(ready)
                while lo < hi:
                    y = (lo + hi) // 2
                    if ready[y] > m:
                        hi = y
                    else:
                        lo = y + 1
                ready.insert(lo, m)
    return start


ORDER = {}


def schedule(ops, tries=1200, seed=1, starts=6, heat=60.0, windows=2400, moves=200, slack=40.0):
    n = len(ops)
    if n in ORDER:
        return ORDER[n][0]
    eng, cost = [o["e"] for o in ops] + ["X"], [o["c"] + 1.0 for o in ops] + [1.0]
    arcs = [[(j, ops[j]["lat"] * LAG[0][0] + (LAG[0][1] if w else 0.0)) for j, w in o["dep"].items()] for o in ops]
    via, bwd = [dict() for _ in ops], []
    for i, a in enumerate(arcs):
        bwd.append([(j, d) for j, d in a if not any(x != j and via[x].get(j, -1e9) + cost[x] + e >= d for x, e in a)])
        for j, d in a:
            via[i][j] = max(via[i].get(j, 0.0), d)
            for y, e in arcs[j]:
                via[i][y] = max(via[i].get(y, 0.0), e + cost[j] + d)
    ends = set(range(n)) - {j for a in bwd for j, _ in a} | {i for i, o in enumerate(ops) if o["lat"]}
    bwd.append([(i, ops[i]["lat"] * LAG[0][0]) for i in sorted(ends)])
    bwds = [[[(j, ops[j]["lat"] * f + (w if i < n and ops[i]["dep"][j] else 0.0)) for j, _ in a] for i, a in enumerate(bwd)] for f, w in LAG]
    fwds = [[[] for _ in range(n + 1)] for _ in LAG]
    for bw, fw in zip(bwds, fwds):
        for i, a in enumerate(bw):
            for j, d in a:
                fw[j].append((i, d))
    fwd = fwds[0]
    left, right = [len(a) for a in bwd], [len(f) for f in fwd]

    def packed(a):
        back = place(eng, cost, bwd, right, [-(a[i] + cost[i]) for i in range(n + 1)])
        b = place(eng, cost, fwd, left, [-back[i] - cost[i] for i in range(n + 1)])
        return b if b[n] <= a[n] else a

    others = [[o["c"] + 1.0 for o in build(None, None, e)] + [1.0] for e in EST[1:]]

    def worth(a):
        order, total = sorted(range(n + 1), key=lambda i: a[i]), a[n]
        for e, c, bw in zip(EST[1:], others, bwds[1:]):
            fin, free = [0.0] * (n + 1), dict.fromkeys("VAPGSX", 0.0)
            for i in order:
                s = free[eng[i]]
                for j, d in bw[i]:
                    if fin[j] + d > s:
                        s = fin[j] + d
                fin[i] = free[eng[i]] = s + c[i]
            total += fin[n] * EST[0][0] / e[0]
        return total / len(EST)

    rank = [0.0] * (n + 1)
    for i in range(n - 1, -1, -1):
        rank[i] = cost[i] + max(rank[j] + d for j, d in fwd[i])
    rng = np.random.RandomState(seed)
    first = packed(place(eng, cost, fwd, left, [-r for r in rank]))
    found = []
    for it in list(range(tries)) * starts:
        if it == 0:
            cur = best = first
            tight, now = None, worth(cur)
            least = now
        if tight is None:
            stop = {(eng[i], round(cur[i] + cost[i], 3)): i for i in range(n)}
            tight, i = [], n
            while i is not None:
                nxt = None
                for j, d in bwd[i]:
                    if abs(cur[j] + cost[j] + d - cur[i]) < 1e-6:
                        nxt = j
                if nxt is None:
                    nxt = stop.get((eng[i], round(cur[i], 3)))
                    if nxt is not None:
                        tight.append((nxt, i))
                i = nxt
        step = (300.0, 1500.0, 5000.0)[rng.randint(3)]
        if rng.uniform() < 0.3:
            c = np.array(cur)
            pick = (np.abs(c - rng.uniform(0, cur[n])) < (2000.0, 6000.0)[rng.randint(2)]) & (rng.uniform(size=n + 1) < (0.1, 0.3)[rng.randint(2)])
            prio = (c + pick * rng.normal(0.0, step, n + 1)).tolist()
        else:
            u, v = tight[rng.randint(len(tight))]
            prio, step = list(cur), float(rng.exponential(step))
            if rng.randint(2):
                prio[u] = cur[v] + step + 1.0
            else:
                to, todo = cur[u] - step * rng.randint(2) - 0.5, [v]
                while todo:
                    x = todo.pop()
                    if prio[x] > to:
                        prio[x] = to - 1e-3 * (cur[n] - cur[x])
                        todo += [j for j, _ in bwd[x]]
        new = place(eng, cost, fwd, left, prio)
        if rng.uniform() < 0.1:
            new = packed(new)
        room = heat * (1.0 - it / tries) * float(rng.exponential(1.0))
        if new[n] <= cur[n] + room + 600.0:
            w = worth(new)
            if w <= now + room:
                cur, now, tight = new, w, None
                if now < least:
                    best, least = cur, now
        if it == tries - 1:
            found.append(best)
    costs, share = [cost] + others, [EST[0][0] / e[0] for e in EST]

    def run(c, seq, fin, free, bw=bwd):
        for i in seq:
            s = free[eng[i]]
            for j, d in bw[i]:
                if fin[j] + d > s:
                    s = fin[j] + d
            fin[i] = free[eng[i]] = s + c[i]

    def polish(order, windows):
        for it in range(windows):
            anew(order, slack * (1.0 - it / windows))
        fin = [0.0] * (n + 1)
        run(cost, order, fin, dict.fromkeys("VAPGSX", 0.0))
        return [fin[i] - cost[i] for i in range(n + 1)]

    def anew(order, heat):
        many = (40, 70, 110)[rng.randint(3)]
        lo = rng.randint(-many // 2, n - many // 2)
        lo, hi = max(0, lo), min(n, lo + many)
        win, state = order[lo:hi], []
        inside = {x: k for k, x in enumerate(win)}
        for c, bw, fw in zip(costs, bwds, fwds):
            fin, free = [0.0] * (n + 1), dict.fromkeys("VAPGSX", 0.0)
            run(c, order[:lo], fin, free, bw)
            tail, nxt = [0.0] * (n + 1), dict.fromkeys("VAPGSX", 0.0)
            for i in order[:hi - 1:-1]:
                s = nxt[eng[i]]
                for j, d in fw[i]:
                    if tail[j] + d > s:
                        s = tail[j] + d
                tail[i] = nxt[eng[i]] = s + c[i]
            base = max([fin[j] + d + tail[i] for i in order[hi:] for j, d in bw[i] if j not in inside] + [0.0])
            out = {x: max([d + tail[j] for j, d in fw[x] if j not in inside] + [0.0]) for x in win}
            state.append((c, fin, free, nxt, base, out, bw))

        def value(seq, m):
            total, head, rest = 0.0, seq[:m], seq[m:]
            for w, (c, fin, free, nxt, base, out, bw) in zip(share, state):
                f = dict(free)
                for x in head:
                    f[eng[x]] = fin[x]
                run(c, rest, fin, f, bw)
                total += w * max(base, max([fin[x] + out[x] for x in seq]), max([f[e] + nxt[e] for e in f]))
            return total
        pred = {x: [j for j, _ in bwd[x] if j in inside] for x in win}
        succ = {x: [j for j, _ in fwd[x] if j in inside] for x in win}
        seq, pos, clean = win, inside, len(win)
        now = value(seq, 0)
        draw = rng.uniform(size=(moves, 2)).tolist()
        room = (rng.exponential(size=moves) * heat).tolist()
        for (u, v), z in zip(draw, room):
            p = int(u * len(seq))
            k = seq[p]
            a, b = max([pos[j] + 1 for j in pred[k]] + [0]), min([pos[j] - 1 for j in succ[k]] + [len(seq) - 1])
            same = [q for q in range(a, b + 1) if q != p and eng[seq[q]] == eng[k]]
            if not same:
                continue
            q = same[int(v * len(same))]
            new = seq[:p] + seq[p + 1:]
            new.insert(q, k)
            w = value(new, min(p, q, clean))
            if w <= now + z:
                seq, now, clean = new, w, len(win)
                pos = {x: y for y, x in enumerate(seq)}
            else:
                clean = min(p, q)
        order[lo:hi] = seq
        fin = [0.0] * (n + 1)
        run(cost, order, fin, dict.fromkeys("VAPGSX", 0.0))
        order.sort(key=lambda i: fin[i] - cost[i])

    by_start = lambda a: sorted(range(n + 1), key=lambda i: (a[i], i))
    found = [polish(by_start(a), windows // 8) for a in found]
    marks = [0] + [i for i, o in enumerate(ops) if o["e"] == "X"] + [n]
    prio, base = [0.0] * (n + 1), 0.0
    for a, b in zip(marks, marks[1:]):
        x = min(found, key=lambda s: s[b] - (s[a] if a else 0.0))
        for i in range(a, b + 1):
            prio[i] = x[i] - (x[a] if a else 0.0) + base
        base = prio[b]
    found.append(polish(by_start(place(eng, cost, fwd, left, prio)), windows // 8))
    order = by_start(min(found, key=worth))
    best = polish(order, windows)
    ORDER[n] = (order[:n], best)
    return ORDER[n][0]


def emit(g, T, ops, order, arrivals, sent):
    queue = {"V": g.vector, "A": g.scalar, "P": g.tensor, "G": g, "S": g.sync}
    count, known = {}, {e: {} for e in queue}
    for i in order:
        o = ops[i]
        e = o["e"]
        if e == "X":
            o["mark"], o["knows"] = (o["sem"], arrivals), {o["sem"]: arrivals}
            count[o["sem"]] = arrivals
            continue
        kn = known[e]
        need = sorted((j for j, w in o["dep"].items() if w and ops[j]["mark"]), key=lambda j: -ops[j]["mark"][1])
        for j in need:
            sem, val = ops[j]["mark"]
            if kn.get(sem, 0) < val:
                queue[e].wait_ge(T.sem[sem], val)
                for s, v in ops[j]["knows"].items():
                    kn[s] = max(kn.get(s, 0), v)
        ins = o["fn"](g)
        sem = o["sem"] or QSEM[e]
        if sem == "none":
            o["mark"] = None
            continue
        count[sem] = count.get(sem, 0) + o["inc"]
        if o["sem"] is None:
            ins.then_inc(T.sem[sem], 1)
        o["mark"] = (sem, count[sem])
        o["knows"] = dict(kn)
        o["knows"][sem] = count[sem]
    g.wait_ge(T.sem.sent, sent)
    for sem, val in count.items():
        g.sync.wait_ge(T.sem[sem], val)


def masks(topo, src, dsts):
    used, res = set(), {}
    for d in sorted(dsts, key=lambda d: len(topo.engines(src, d))):
        pick = [e for e in topo.engines(src, d) if e not in used][:4]
        used.update(pick)
        res[d] = sum(1 << e for e in pick)
    return res


def make_ops(T, core, q, topo):
    n = len(T.cores)
    peers = [T.cores[(q + d) % n] for d in range(1, n)]
    mask = masks(topo, core, peers)

    def send(g, t):
        trs = []
        for d in range(1, n):
            rid, pid = topo.addr(peers[d - 1], core)
            trs.append(RemoteDMATransfer(dst_ids=[DstId(rid=rid, pnc=pid)], dma_engine_mask=mask[peers[d - 1]],
                                         remote_sem=T.sem["arr%d" % t], src=T["sb%d" % t][:, 128 * (d - 1):128 * d],
                                         dst=T.tb[:, WB[t] + 16 + 128 * (n - 1 - d):WB[t] + 16 + 128 * (n - d)]))
        return g.remote_dma_fused(trs, local_sem=T.sem.sent)

    return build(T, send)


def rank_program(g, core, T, topo):
    q = T.rank_of(core)
    if q is None:
        return
    n = len(T.cores)
    ops = make_ops(T, core, q, topo)
    depend(ops)
    emit(g, T, ops, schedule(ops), 4 * (n - 1), 4 * (n - 1) * RO)
